import numpy as np, ml_dtypes
CORES = [24,25,26,27,28,29,30,31]
N = 8
BF = ml_dtypes.bfloat16
D, T, L, RO, CM, SH = 4096, 768, 4, 3, 255, 12
def at(c, p):
    return c.reshape(-1)[np.arange(N * 8).reshape((N, 8) + (1,) * (p.ndim - 2)) * D + p]
def grow(rng, c, p):
    e = at(c, p); u = rng.random(p.shape)
    e = np.where(u < 0.06, e + rng.integers(1, RO, p.shape), e)
    return np.where(u > 0.97, rng.integers(0, CM + 1, p.shape), e)
def parts(rng):
    c = rng.integers(0, CM - RO + 1, (N, 8, D)); p = rng.integers(0, D, (N, 8, 16, D)); hot = rng.integers(0, D, (N, 8, 32))
    for n in range(N):
        for g in range(8): p[n, g] = np.where(rng.random((16, D)) < 0.03, hot[n, g][rng.integers(0, 32, (16, D))], p[n, g])
    return c, p, rng.integers(0, 16, (N, 8, 16, D)), rng.integers(0, 16, (N, 8, 16, T))
def pack(k, x, c, z):
    return {"nkey": np.ascontiguousarray(k.reshape(N, 128, D)).astype(np.float32), "xreg": np.ascontiguousarray(x.reshape(N, 128, D)).astype(np.float32).astype(BF),
            "cnt": np.ascontiguousarray(c).astype(np.int32), "zin": np.ascontiguousarray(z.reshape(N, 128, T)).astype(np.float32).astype(BF)}
def setup_inputs(rng):
    c, p, x, z = parts(rng)
    return pack(np.where(rng.random(p.shape) < 0.04, -1, p + D * grow(rng, c, p)), x, c, z)
def setup_inputs_calm(rng):
    c, p, x, z = parts(rng)
    base = (np.arange(N)[:, None, None] + np.arange(8)[None, :, None]) & 3
    c = np.where(rng.random(c.shape) < 0.8, base, rng.integers(0, 4, c.shape))
    e = at(c, p); e = np.maximum(np.where(rng.random(p.shape) < 0.75, e, e + rng.integers(-3, 4, p.shape)), 0)
    return pack(np.where(rng.random(p.shape) < 0.02, -1, p + D * e), x, c, z)
def setup_inputs_corners(rng):
    c, p, x, z = parts(rng); k = np.where(rng.random(p.shape) < 0.04, -1, p + D * grow(rng, c, p)); col = np.arange(D); r16 = np.arange(16)[:, None]
    who = rng.permutation(N)
    for n in range(N):
        kinds = rng.permutation(8)
        for g in range(8):
            m = int(kinds[g]); w = c[n, g]
            if n == who[0]:
                if m < 4: k[n, g] = -1
                else:
                    q = p[n, g]; k[n, g] = np.where(rng.random((16, D)) < 0.1, -1, q + D * ((w[q] + rng.integers(1, CM + 1, (16, D))) & CM))
            elif n == who[1]:
                q = (col + (D >> 2) * ((r16 & 3) if m > 2 else 0 * r16)) & (D - 1); k[n, g] = q + D * w[q]
            elif m == 0: k[n, g] = col + D * (w[col] + (r16 >= 12))
            elif m == 1:
                q = (5 * col + int(rng.integers(0, D))) & (D - 1); k[n, g] = (q + D * w[q])[None, :]
            elif m == 2:
                k[n, g] = -1; k[n, g, :, T - 1] = T - 1 + D * w[T - 1]
            elif m == 3:
                q = np.array([0, 1, T - 1, T, D - 1])[rng.integers(0, 5, (16, D))]; k[n, g] = q + D * (w[q] + rng.integers(0, 3, (16, D)))
            elif m == 4:
                w = (CM - RO) * rng.integers(0, 2, D); c[n, g] = w; q = p[n, g]
                k[n, g] = q + D * np.maximum(w[q] + np.where(rng.random((16, D)) < 0.75, 0, rng.integers(-1, 2, (16, D))), 0)
            elif m == 5: k[n, g] = np.where((rng.random(D) < 0.5)[None, :], -1, k[n, g])
            elif m == 6:
                q = col ^ 1; k[n, g] = q + D * (w[q] + (r16 >= 13))
            else: z[n, g] = rng.integers(0, 16, (1, T)) + np.zeros((16, 1), np.int64)
    return pack(k, x, c, z)
def setup_inputs_crowd(rng):
    c, p, x, z = parts(rng); k = np.where(rng.random(p.shape) < 0.04, -1, p + D * grow(rng, c, p)); r16 = np.arange(16)
    for n in range(N):
        kinds = rng.permutation(8)
        for g in range(8):
            m = int(kinds[g]); w = c[n, g]
            if m > 5: continue
            h = T + rng.permutation(D - T)[:L + 7]; dd = h[L - 1:L + 3]; odd = int(rng.choice(np.array([0, T - 1])))
            k[n, g, :, :T] = h[0] + D * w[h[0]]
            for j in range(L - 2): k[n, g, :, h[j]] = h[j + 1] + D * w[h[j + 1]]
            to = dd[r16 & 3] if m == 2 else np.full(16, h[0] if m == 5 else dd[0])
            k[n, g, :, h[L - 2]] = to + D * (w[to] + ((r16 & 3) if m == 3 else 0))
            if m == 1: k[n, g, :, odd] = -1
            if m == 4: k[n, g, :, odd] = odd + D * w[odd]
    return pack(k, x, c, z)
def setup_inputs_ends(rng):
    F = D >> 4; M = 4; top = D * (CM + 1) - 1; last = np.arange(16) * F + F - 1
    c = (CM - RO) * rng.integers(0, 2, (N, 8, D)); x = 15 * rng.integers(0, 2, (N, 8, 16, D)); z = 15 * rng.integers(0, 2, (N, 8, 16, T))
    m = rng.integers(0, 3, (N, 8, 16, F)); m[:, :, 6:, F - 1] = 1; m[:, :, 6::2, 0] = 0; m[:, :, 7::2, 0] = 1
    m = np.tile(m, (1, 1, 1, 16)); k = np.where((m == 1) | ((m == 2) & (rng.random(m.shape) < 0.5)), top, -1)
    ti = np.concatenate([np.array([T - 1, 0]), 1 + rng.permutation(T - 2)[:M * RO - 2]]).reshape(M, RO); z[:, :, :, ti.reshape(-1)] = 0
    for n in range(N):
        for g in range(8):
            quiet = (n == N - 1 and g == 7) or (n + g) % 3 == 0
            cand = T + rng.permutation(D - T); cand = cand[(cand & (F - 1)) != F - 1][:M * (RO * (L - 1) + 1)]
            dd = cand[:M].copy(); nodes = cand[M:].reshape(M, RO, L - 1)
            if not quiet: dd[0] = D - 1
            c[n, g, dd] = (CM - RO) * ((np.arange(M) + g) & 1); x[n, g, :, dd] = 0
            tb = np.ones(D, bool); tb[cand] = False; tb[dd] = False; tb[ti.reshape(-1)] = False; tb[D - 1] = False
            if quiet:
                tb[last] = False; x[n, g, :, last] = 15
            lv = np.flatnonzero(tb)
            for s in (0, 15):
                q = np.where(rng.random(D) < 0.05, lv[rng.integers(0, 4, D)], lv[rng.integers(0, len(lv), D)])
                live = q + D * (c[n, g][q] + (rng.random(D) < 0.1)); k[n, g, s] = np.where(rng.random(D) < 0.1, k[n, g, s], live)
            if quiet: k[n, g, 15, last] = top
            for j in range(M):
                for t in range(RO):
                    v = ti[j, t]
                    for a in nodes[j, t]:
                        k[n, g, 0, v] = a + D * c[n, g, a]; v = a
                    k[n, g, 0, v] = dd[j] + D * (c[n, g, dd[j]] + t)
    return pack(k, x, c, z)
def setup_inputs_spread(rng):
    pw = rng.choice(np.array([0.3, 1.0, 4.0]), (N, 8, 1)); c = np.minimum(((CM - RO + 1) * rng.random((N, 8, D)) ** pw).astype(np.int64), CM - RO)
    pw = rng.choice(np.array([0.6, 1.0, 1.7]), (N, 8, 1, 1)); p = np.minimum((D * rng.random((N, 8, 16, D)) ** pw).astype(np.int64), D - 1)
    x = np.minimum((16 * rng.random((N, 8, 16, D)) ** rng.choice(np.array([0.4, 1.0, 2.5]), (N, 8, 1, D))).astype(np.int64), 15)
    z = np.minimum((16 * rng.random((N, 8, 16, T)) ** rng.choice(np.array([0.4, 1.0, 2.5]), (N, 8, 1, T))).astype(np.int64), 15)
    return pack(np.where(rng.random(p.shape) < 0.03, -1, p + D * grow(rng, c, p)), x, c, z)
def check_inputs(d):
    bad = []
    for k, lo, hi in (("nkey", -1, D * (CM + 1) - 1), ("xreg", 0, 15), ("cnt", 0, CM - RO), ("zin", 0, 15)):
        a = np.asarray(d[k]).astype(np.float64)
        if not (np.min(a) >= lo and np.max(a) <= hi): bad.append("range of " + k)
        elif np.any(a != np.floor(a)): bad.append("whole numbers in " + k)
    return bad
def reference(nkey, xreg, cnt, zin):
    K = nkey.astype(np.int64).reshape(N, 8, 16, D); X = xreg.astype(np.float32).astype(np.int64).reshape(N, 8, 16, D)
    C = cnt.astype(np.int64); Z = zin.astype(np.float32).astype(np.int64).reshape(N, 8, 16, T)
    for t in range(RO):
        if t > 0: Z = np.roll(Z, (1, t), axis=(0, 1))
        for q in range(N):
            for h in range(8):
                k, x, c, z = K[q, h], X[q, h], C[q, h], Z[q, h]
                v = np.arange(T); ok = np.ones(T, bool); key = None
                for m in range(L):
                    s = z[L * t + m].copy(); back = key
                    key = k[s, v]; v = key & (D - 1)
                    ok = ok & (key >= 0) & ((key >> SH) == c[v])
                w = np.flatnonzero(ok); d = v[w]
                u, first = np.unique(d, return_index=True); win = w[first]
                left = z[:, win]
                z[:, w] = x[:, d]
                x[:, u] = left
                c[u] += 1
                k[s[win], u] = back[win]
                k[t, w] = d + D * c[d]
    return {"yz": Z.reshape(N, 128, T).astype(np.float32).astype(BF), "yk": np.add.reduce(K.reshape(N, 128, 16, D >> 4), axis=2).astype(np.float32),
            "yx": np.add.reduce(X.reshape(N, 128, 16, D >> 4), axis=2).astype(np.float32).astype(BF), "yc": C.astype(np.float32)}

@@ -1,0 +1,510 @@
+from concourse.mybir import AluOpType as A, ActivationFunctionType as F
+
+D, NT, NC, HT, HC = 4096, 768, 48, 384, 24
+EXT = D + 32
+f32, bf, fh, i32, u16 = "float32", "bfloat16", "float16", "int32", "uint16"
+
+
+def _sb(n, dt):
+    return ("sbuf", [128, n], dt)
+
+
+SCRATCH = {
+    "K": _sb(EXT, f32), "XC": _sb(EXT + 3 * NT, bf),
+    "L0": _sb(NT, bf), "L1": _sb(NT, bf), "L2": _sb(NT, bf),
+    "ZN0": _sb(NT, bf), "ZN1": _sb(NT, bf), "ZN2": _sb(NT, bf),
+    "C0": _sb(D, bf), "T1": _sb(NT, bf), "SO": _sb(NC, u16),
+    "GA": _sb(NT, f32), "GB": _sb(NT, f32), "KA": _sb(NT, f32), "KB": _sb(NT, f32),
+    "M1": _sb(NT, bf), "M2": _sb(NT, bf), "M3": _sb(NT, bf), "NM": _sb(NT, bf),
+    "AB0": _sb(NT, bf), "AB1": _sb(NT, bf), "AB2": _sb(NT, bf), "AB3": _sb(NT, bf),
+    "TC": _sb(3 * NT, bf), "EQ": _sb(1152, bf), "PK": _sb(8 * NC, f32),
+    "KI": _sb(192, i32), "PL": _sb(192, i32), "CI": _sb(192, i32), "OFF": _sb(192, u16), "ZO": _sb(NC, u16),
+    "ZA": _sb(96, fh), "ZB": _sb(96, fh), "H": _sb(144, fh),
+    "S": _sb(NC * 16, f32), "E3": _sb(144, f32), "ND": _sb(72, f32),
+    "ones": _sb(384, bf), "onesh": _sb(384, fh), "kr": _sb(16, i32), "kr2": _sb(16, i32), "RM": _sb(16, f32), "GE": _sb(16, f32),
+    "col": _sb(16, f32), "BO0": _sb(128, bf), "BOb": _sb(128, bf), "BOf": _sb(128, f32),
+    "W0": _sb(144, bf), "Wb": _sb(144, bf), "W8": _sb(136, f32), "SEL": _sb(NC, f32),
+    "Ib": _sb(144, bf), "If": _sb(128, f32), "Ih": _sb(128, fh), "nIh": _sb(128, fh),
+    "Sb": _sb(12 * 128, bf), "Eh": _sb(16 * 128, fh), "Uh": _sb(16 * 144, fh),
+    "R": _sb(3 * 128, bf), "I15": _sb(128, bf), "I14": _sb(128, bf), "Bm": _sb(128, bf), "Bz": _sb(128, bf),
+    "I16": _sb(128, bf), "tm": _sb(128, bf), "tn": _sb(128, bf),
+    "Pn": _sb(72, f32), "Tp": _sb(1152, fh), "c16": _sb(NC, f32), "zi": _sb(3 * NC, f32), "dum": _sb(NC, f32),
+    "x14": _sb(256, bf), "x15": _sb(256, bf), "cn": _sb(256, i32), "pk": _sb(256, bf), "cb": _sb(256, bf),
+    "r14": _sb(256, bf), "h14": _sb(256, bf), "hz": _sb(NT, bf), "YZ": _sb(NT, bf), "YX": _sb(256, bf),
+    "YT": _sb(256, f32), "YU": _sb(256, f32), "YK": _sb(256, f32),
+    "P": ("psum", [128, 4096], f32),
+}
+NDMA = 24
+SEMAPHORES = ["sv", "sa", "sp", "sg", "arr1", "arr2", "snt1", "snt2"] + ["d%d" % k for k in range(NDMA)]
+
+
+def _meet(x, y):
+    if x[1] >= y[2] or y[1] >= x[2]:
+        return False
+    if x[3] > 1 and x[3] == y[3] and (x[1] - y[1]) % x[3]:
+        return False
+    return True
+
+
+def _emit(ops, queues, T):
+    hist, known, waits, need = {}, {}, [], set()
+    for q in queues:
+        known[q] = {}
+    for n, op in enumerate(ops):
+        q, dma = op["q"], op["dma"]
+        deps = set()
+        touch = [(x, False) for x in op["r"]] + [(x, True) for x in op["w"]]
+        for acc, wr in touch:
+            bank = (acc[0], acc[1] // 512 * 512, (acc[2] + 511) // 512 * 512, 1)
+            for m, x, w in hist.get(acc[0], []):
+                o = ops[m]
+                if o["q"] == q and not dma and not o["dma"]:
+                    if q != "p" and (w or wr) and _meet(acc, x):
+                        deps.add(m)
+                elif acc[0] == "P":
+                    if _meet(bank, (x[0], x[1], x[2], 1)):
+                        deps.add(m)
+                elif (w or wr) and _meet(acc, x):
+                    deps.add(m)
+        for acc, wr in touch:
+            hist.setdefault(acc[0], []).append((n, acc, wr))
+        mine = []
+        if q is not None:
+            kn = known[q]
+            for m in sorted(deps, reverse=True):
+                key = ops[m]["sem"]
+                if kn.get(key, -1) >= m:
+                    continue
+                mine.append(m)
+                need.add(m)
+                kn[key] = m
+                for k2, v2 in ops[m]["clock"].items():
+                    if kn.get(k2, -1) < v2:
+                        kn[k2] = v2
+            op["clock"] = dict(kn)
+        else:
+            op["clock"] = {}
+        waits.append(mine)
+    count, val = {}, {}
+    for n, op in enumerate(ops):
+        if op["dma"] or n in need:
+            count[op["sem"]] = count.get(op["sem"], 0) + op["inc"]
+            val[n] = count[op["sem"]]
+    for n, op in enumerate(ops):
+        if op["q"] is None:
+            continue
+        eng = queues[op["q"]]
+        for m in waits[n]:
+            eng.wait_ge(T.sem[ops[m]["sem"]], val[m])
+        ins = op["f"]()
+        if n in val and not op["own"]:
+            ins.then_inc(T.sem[op["sem"]], op["inc"])
+    for s in sorted(count):
+        queues["g"].wait_ge(T.sem[s], count[s])
+
+
+def rank_program(g, core, T, topo):
+    rank = T.rank_of(core)
+    if rank is None:
+        return
+    n_ranks = len(T.cores)
+    nxt, prv = T.cores[(rank + 1) % n_ranks], T.cores[(rank - 1) % n_ranks]
+    queues = {"g": g, "v": g.vector, "a": g.scalar, "p": g.tensor, "s": g.sync}
+    semof = {"g": "sg", "v": "sv", "a": "sa", "p": "sp"}
+    ops, nd = [], [0]
+
+    def b(name, a=0, e=None, st=1):
+        if e is None:
+            e = SCRATCH[name][1][1]
+        ap = T[name][:, a:e] if st == 1 else T[name][:, a:e:st]
+        return (ap, [(name, a, e, st)])
+
+    def p(bank, a, e, st=1):
+        return b("P", 512 * bank + a, 512 * bank + e, st)
+
+    def hf(name, h):
+        return b(name, HT * h, HT * h + HT)
+
+    def ind(win, off):
+        return (win[0].indirect(off[0]), win[1], off[1])
+
+    def rec(q, f, outs, ins):
+        r, w = [], []
+        for x in ins:
+            if isinstance(x, tuple):
+                r += x[1]
+                if len(x) == 3:
+                    r += x[2]
+        for x in outs:
+            w += x[1]
+            if len(x) == 3:
+                r += x[2]
+        ops.append({"q": q, "f": f, "r": r, "w": w, "dma": False, "sem": semof[q], "inc": 1, "own": False})
+
+    def v_(x):
+        return x[0] if isinstance(x, tuple) else x
+
+    def dma(q, out, in_):
+        s = "d%d" % nd[0]
+        nd[0] += 1
+        ops.append({"q": q, "f": lambda: queues[q].dma_start(out[0], in_[0]), "r": in_[1], "w": out[1], "dma": True,
+                    "sem": s, "inc": 16, "own": False})
+
+    def ts(out, in0, s1, op0, s2=None, op1=None):
+        if op1 is None:
+            rec("v", lambda: g.vector.tensor_scalar(out[0], in0[0], v_(s1), None, op0), [out], [in0, s1])
+        else:
+            rec("v", lambda: g.vector.tensor_scalar(out[0], in0[0], v_(s1), v_(s2), op0, op1), [out], [in0, s1, s2])
+
+    def tt(out, in0, in1, op):
+        rec("v", lambda: g.vector.tensor_tensor(out[0], in0[0], in1[0], op), [out], [in0, in1])
+
+    def cp(out, in_):
+        rec("v", lambda: g.vector.tensor_copy(out[0], in_[0]), [out], [in_])
+
+    def ms(out, c):
+        rec("v", lambda: g.vector.memset(out[0], c), [out], [])
+
+    def act(out, in_, func, bias=None, scale=None):
+        kw = {}
+        if bias is not None:
+            kw["bias"] = v_(bias)
+        if scale is not None:
+            kw["scale"] = v_(scale)
+        rec("a", lambda: g.scalar.activation(out[0], in_[0], func, **kw), [out], [in_, bias, scale])
+
+    def mm(out, lhsT, rhs, start=True, stop=True):
+        rec("p", lambda: g.tensor.matmul(out[0], lhsT[0], rhs[0], start, stop), [out], [lhsT, rhs])
+
+    def sel(out, in_, pattern, cmp, base, cm):
+        rec("g", lambda: g.affine_select(out[0], in_[0], pattern, cmp, 0.0, base, cm), [out], [in_])
+
+    def wrap(out, src, n):
+        for r in range(16):
+            mm(out, b("Wb", 15 - r, 143 - r), b(src, r, n, 16), r == 0, r == 15)
+
+    def wide(bank, mat, src):
+        mm(p(bank, 0, 512), mat, b(src, 0, 512))
+        mm(p(bank, 512, NT), mat, b(src, 512, NT))
+
+    def sm(k):
+        return b("S", NC * k, NC * k + NC)
+
+    def smp(k, par):
+        return b("S", NC * k + par, NC * k + NC, 2)
+
+    def rm(r):
+        return b("RM", r, r + 1)
+
+    def co(k):
+        return b("col", k, k + 1)
+
+    SC, NSC, N15, C16, L14, BX, BZ, DE, DO, CT = range(10)
+    OK, OK3, OK012, M01, Q1, ZT, ZT2, CN1, H1, H2, Q0, Q, TE, TO, Q1A = range(15)
+
+    dma("a", b("L0"), (T.zin[:], []))
+    dma("s", b("K", 0, NT), (T.nkey[:, 0:NT], []))
+    dma("s", b("cn"), (T.cnt[:], []))
+    dma("s", b("K", NT, D), (T.nkey[:, NT:D], []))
+    dma("s", b("x14"), (T.xreg[14:128:16, :], []))
+    dma("s", b("x15"), (T.xreg[15:128:16, :], []))
+
+    ms(b("ones"), 1.0)
+    rec("g", lambda: g.iota(T.kr[:], [[-1, 16]], 16, 1), [b("kr")], [])
+    sel(b("BO0"), b("ones", 0, 128), [[-16, 8], [0, 16]], A.is_ge, 0, 1)
+    sel(b("BOb"), b("BO0"), [[16, 8], [0, 16]], A.is_ge, 15, -1)
+    sel(b("W0"), b("ones", 0, 144), [[-16, 9], [256, 16]], A.is_ge, -3840, 1)
+    sel(b("Wb"), b("W0"), [[16, 9], [0, 16]], A.is_ge, 15, -1)
+    sel(b("Ib"), b("ones", 0, 144), [[-1, 144]], A.is_equal, 0, 1)
+    rec("g", lambda: g.iota(T.c16[:], [[16, NC]], 0, 0, allow_small_or_imprecise_dtypes=True), [b("c16")], [])
+    rec("g", lambda: g.iota(T.C0[:], [[0, D]], 0, 0, allow_small_or_imprecise_dtypes=True), [b("C0")], [])
+    ts(b("kr2"), b("kr"), 15, A.bitwise_and)
+    ts(b("RM"), b("kr2"), 0.0, A.is_equal)
+    cp(co(SC), b("kr2", 0, 1))
+    ts(co(NSC), b("kr2", 0, 1), -1.0, A.mult)
+
+    def turned(out, o0, src, t, scal):
+        ts(b(out, o0 + 16 * t, o0 + 128), b(src, 0, 128 - 16 * t), scal, A.mult)
+        if t:
+            ts(b(out, o0, o0 + 16 * t), b(src, 128 - 16 * t, 128), scal, A.mult)
+
+    for j in range(4):
+        turned("Sb", 128 * j, "BOb", 0, rm(j))
+    ts(b("SEL", 0, NC, 2), b("ones", 0, HC), co(SC), A.mult, 8.0, A.is_lt)
+    ts(b("SEL", 1, NC, 2), b("ones", 0, HC), co(SC), A.mult, 8.0, A.is_ge)
+    ts(co(N15), rm(15), -1.0, A.mult, 1.0, A.add)
+    ts(co(C16), rm(15), 16.0, A.mult)
+    tt(b("W8"), b("Wb", 8, 144), b("Wb", 0, 136), A.add)
+    ts(b("I15"), b("Ib", 0, 128), co(N15), A.mult)
+    ts(b("tm"), b("Ib", 1, 129), co(C16), A.mult)
+    cp(b("Ih"), b("Ib", 0, 128))
+    tt(b("R", 0, 128), b("I15"), b("tm"), A.add)
+
+    def consts0():
+        ms(b("Pn", 0, 24), 1024.0)
+        ms(b("Pn", 24, 48), 0.0)
+        ms(b("Pn", 48, 72), 1024.0)
+        ts(b("GE"), b("c16", 0, 16), 0.0625, A.mult, co(SC), A.is_le)
+        ts(co(DE), co(SC), float(D), A.add)
+        ts(co(DO), co(SC), float(D + 16), A.add)
+        ms(b("XC", D, EXT), 0.0)
+        cp(b("BOf"), b("BOb"))
+        ts(b("I16"), b("Ib", 0, 128), 16.0, A.mult)
+        for r in range(16):
+            ts(b("Tp", 72 * r, 72 * r + 72), b("Pn"), b("GE", r, r + 1), A.mult)
+
+    def consts1():
+        for r in range(16):
+            ts(b("Eh", 128 * r, 128 * r + 128), b("BOb"), rm(r), A.mult)
+        ts(b("nIh"), b("Ib", 0, 128), -1.0, A.mult)
+        for t in range(3):
+            ts(b("zi", NC * t, NC * t + NC), b("c16"), co(SC), A.add, float(EXT + NT * t), A.add)
+        ts(b("dum", 0, NC, 2), b("c16", 0, HC), 0.0, A.mult, co(DE), A.add)
+        ts(b("dum", 1, NC, 2), b("c16", 0, HC), 0.0, A.mult, co(DO), A.add)
+        for r in range(16):
+            ts(b("Uh", 144 * r, 144 * r + 144), b("Wb"), rm(r), A.mult, 64.0, A.mult)
+        cp(b("onesh"), b("ones"))
+        for t in (1, 2):
+            for j in range(4 * t, 4 * t + 4):
+                turned("Sb", 128 * j, "BOb", t, rm(j))
+            turned("R", 128 * t, "Ib", t, co(N15))
+        ts(co(L14), co(SC), 14.0, A.is_lt)
+        ts(co(CT), rm(15), -192.0, A.mult)
+        ts(b("tn"), b("Wb", 0, 128), 0.0625, A.mult)
+        cp(b("If"), b("Ib", 0, 128))
+        ts(co(BZ), rm(14), 3072.0, A.mult, co(CT), A.add)
+        ts(b("I14"), b("Ib", 0, 128), co(L14), A.mult)
+        tt(b("Bm"), b("tn"), b("Wb", 1, 129), A.subtract)
+        ts(co(BX), co(BZ), 16.0, A.mult)
+        ts(b("Bz"), b("Bm"), rm(14), A.mult)
+
+    def pack():
+        mm(p(6, 0, 256), b("Ib", 0, 128), b("x14"), True, False)
+        mm(p(6, 0, 256), b("I16"), b("x15"), False, True)
+        act(b("pk"), p(6, 0, 256), F.Copy)
+        dma("s", (T.XC[14:128:16, 0:D], [("XCa", 0, D, 1)]), b("pk"))
+
+    def write5(h):
+        tt(hf("K", h), hf("K", h), p(6 + h, 0, HT), A.mult)
+        tt(hf("K", h), hf("K", h), p(4 + h, 0, HT), A.add)
+
+    banks = [range(0, 6), range(6, 11), range(11, 16)]
+
+    def dreg(r):
+        k = 0 if r < 6 else (1 if r < 11 else 2)
+        return p(4 + k, 72 * (r - banks[k][0]), 72 * (r - banks[k][0]) + 72)
+
+    def part(name, m, h=None):
+        if h is None:
+            return b(name, NC * m, NC * m + NC)
+        return b(name, NC * m + HC * h, NC * m + HC * h + HC)
+
+    def wrap8(m, h):
+        for q in range(8):
+            mm(p(2 + h, 0, NC), b("W8", 7 - q, 135 - q), b("GB" if m & 1 else "GA", HT * h + q, HT * h + HT, 8), q == 0, q == 7)
+
+    def small(m, h):
+        c0 = NC * (2 * m + h)
+        tt(b("PK", c0, c0 + NC), p(2 + h, 0, NC), b("SEL"), A.mult)
+        tt(part("KI", m, h), b("PK", c0, c0 + NC, 2), b("PK", c0 + 1, c0 + NC, 2), A.add)
+        ts(part("PL", m, h), part("KI", m, h), D - 1, A.bitwise_and)
+        cp(part("OFF", m, h), part("PL", m, h))
+
+    def gather(m, h):
+        tt(hf("GB" if m & 1 else "GA", h), ind(b("K", 0, D), part("OFF", m - 1, h)), hf("M%d" % m, h), A.mult)
+
+    consts0()
+    for t in range(3):
+        L, ext, ZN = "L%d" % t, EXT + NT * t, "ZN%d" % t
+
+        def S_(m, t=t):
+            return b("Sb", 128 * (4 * t + m), 128 * (4 * t + m) + 128)
+
+        def mask(m, bank):
+            act(b("AB%d" % m), p(bank, 0, NT), F.Abs, co(NSC))
+            act(b("M%d" % m), b("AB%d" % m), F.Relu, 1.0, -1.0)
+
+        cw = b("XC", 0, D) if t else b("C0")
+
+        def counts(m, cw=cw):
+            act(b("TC", NT * m, NT * m + NT), ind(cw, part("OFF", m)), F.Identity, None, rm(15))
+
+        if t:
+            ops.append({"q": None, "f": None, "r": [], "w": b(L)[1], "dma": True, "sem": "arr%d" % t,
+                        "inc": len(topo.engines(prv, core)), "own": True})
+        for h in (0, 1):
+            mm(p(h, 0, HT), S_(0), hf(L, h))
+        wide(2, S_(1), L)
+        for h in (0, 1):
+            act(hf("AB0", h), p(h, 0, HT), F.Abs, co(NSC))
+        for h in (0, 1):
+            act(p(h, 0, HT), hf("AB0", h), F.Relu, 1.0, -1.0)
+        act(b("AB1"), p(2, 0, NT), F.Abs, co(NSC))
+        wide(2, S_(2), L)
+        act(b("AB2"), p(2, 0, NT), F.Abs, co(NSC))
+        act(b("M1"), b("AB1"), F.Relu, 1.0, -1.0)
+        act(b("M2"), b("AB2"), F.Relu, 1.0, -1.0)
+        for h in (0, 1):
+            if t:
+                write5(h)
+            tt(hf("GA", h), hf("K", h), p(h, 0, HT), A.mult)
+            wrap8(0, h)
+        wide(4, S_(3), L)
+        mask(3, 4)
+        if not t:
+            cp(b("cb"), b("cn"))
+            act(b("NM"), b("AB3"), F.Sign)
+            dma("s", (T.C0[15:128:16, :], b("C0")[1]), b("cb"))
+            dma("s", (T.XC[15:128:16, 0:D], [("XCb", 0, D, 1)]), b("cb"))
+            for k in range(8):
+                dma("s", (T.XC[16 * k:16 * k + 14, 0:D], [("XC%d" % k, 0, D, 1)]), (T.xreg[16 * k:16 * k + 14, :], []))
+            consts1()
+        small(0, 0)
+        if t:
+            gather(1, 0)
+        small(0, 1)
+        if not t:
+            gather(1, 0)
+        wrap8(1, 0)
+        gather(1, 1)
+        wrap8(1, 1)
+        if not t:
+            pack()
+        wide(0, b("R", 128 * t, 128 * t + 128), L)
+        counts(0)
+        small(1, 0)
+        gather(2, 0)
+        wrap8(2, 0)
+        small(1, 1)
+        counts(1)
+        if t:
+            act(b("NM"), b("AB3"), F.Sign)
+        gather(2, 1)
+        wrap8(2, 1)
+        small(2, 0)
+        gather(3, 0)
+        wrap8(3, 0)
+        small(2, 1)
+        counts(2)
+        gather(3, 1)
+        mm(p(7, 0, HT), b("BOf"), hf("GA", 1))
+        wrap8(3, 1)
+        small(3, 0)
+        act(hf("T1", 0), ind(cw, part("OFF", 3, 0)), F.Identity, rm(15), rm(15))
+        tt(hf("KB", 1), p(7, 0, HT), hf("M3", 1), A.mult)
+        tt(hf("KA", 0), ind(b("K", 0, D), part("OFF", 3, 0)), hf("NM", 0), A.mult)
+        ts(b("CI", 0, 144), b("KI", 0, 144), 12, A.arith_shift_right)
+        wrap(p(2, 0, 144), "TC", 3 * NT)
+        small(3, 1)
+        act(hf("T1", 1), ind(cw, part("OFF", 3, 1)), F.Identity, rm(15), rm(15))
+        act(b("XC", ext, ext + NT), p(0, 0, NT), F.Copy)
+        pl, ci = part("PL", 3), part("CI", 3)
+        for k, par in enumerate((1, 1, 0, 0)):
+            ts(b("ZA", HC * k, HC * k + HC), b("PL", 144 + par, 192, 2), -2048.0, A.add, 1.0 / D, A.mult)
+        ts(ci, part("KI", 3), 12, A.arith_shift_right)
+        tt(sm(Q1A), pl, part("zi", t), A.subtract)
+        for r in range(16):
+            mm(dreg(r), b("Eh", 128 * r, 128 * r + 128), b("ZA", 0, 72), r in (0, 6, 11), False)
+            mm(dreg(r), b("nIh"), b("ZA", 24, 96), False, False)
+        ts(sm(CN1), ci, 1.0, A.add)
+        tt(b("E3"), p(2, 0, 144), b("CI", 0, 144), A.is_equal)
+        tt(sm(Q0), pl, b("dum"), A.subtract)
+        tt(sm(M01), b("E3", 0, 48), b("E3", 48, 96), A.mult)
+        ts(sm(H1), pl, 1.0 / 64, A.mult, -32.0, A.add)
+        tt(sm(OK012), sm(M01), b("E3", 96, 144), A.mult)
+        ts(sm(H2), ci, 1.5, A.add, 64.0, A.mult)
+        for k, par in enumerate((1, 1, 0, 0)):
+            tt(b("ZB", HC * k, HC * k + HC), smp(CN1, par), smp(OK012, par), A.mult)
+        tt(sm(Q1), sm(Q1A), sm(OK012), A.mult)
+        tt(hf("KA", 1), ind(b("K", 0, D), part("OFF", 3, 1)), hf("NM", 1), A.mult)
+        wrap(p(3, 0, NC), "T1", NT)
+        for k in range(3):
+            for r in banks[k]:
+                mm(dreg(r), b("Eh", 128 * r, 128 * r + 128), b("ZB", 0, 72), False, False)
+                mm(dreg(r), b("nIh"), b("ZB", 24, 96), False, r == banks[k][-1])
+        tt(sm(OK3), p(3, 0, NC), sm(CN1), A.is_equal)
+        tt(sm(ZT), sm(OK3), sm(Q1), A.mult)
+        tt(sm(OK), sm(OK3), sm(OK012), A.mult)
+        tt(sm(ZT2), sm(ZT), part("zi", t), A.add)
+        tt(sm(Q), sm(Q0), sm(OK), A.mult)
+        cp(b("ZO"), sm(ZT2))
+        xc = b("XC", 0, ext + NT)
+        xc = (xc[0], xc[1] + [("XC" + k, 0, D, 1) for k in "ab01234567"])
+        act(b(ZN), ind(xc, b("ZO")), F.Copy)
+        if t < 2:
+            rid, pid, _se = topo.addr(nxt)
+            ops.append({"q": "g", "r": b(ZN)[1], "w": [], "dma": True, "sem": "snt%d" % (t + 1), "own": True,
+                        "inc": len(topo.engines(core, nxt)),
+                        "f": lambda t=t, rid=rid, pid=pid: g.remote_dma(
+                            T["L%d" % (t + 1)][:], T["ZN%d" % t][:], T.sem["arr%d" % (t + 1)], T.sem["snt%d" % (t + 1)],
+                            pid, rid, topo.mask(core, nxt))})
+        for k in range(3):
+            r0, r1 = banks[k][0], banks[k][-1] + 1
+            tt(b("EQ", 72 * r0, 72 * r1), p(4 + k, 0, 72 * (r1 - r0)), b("Tp", 72 * r0, 72 * r1), A.is_equal)
+        for r in range(16):
+            mm(p(7, 0, 72), b("Wb", 15 - r, 143 - r), b("EQ", 72 * r, 72 * r + 72), r == 0, r == 15)
+        mm(p(2, 0, HT), b("BOf"), hf("GA", 0))
+        ts(b("H", 96, 144), sm(OK), -1.0 / 64, A.mult)
+        tt(b("H", 0, 48), sm(H1), sm(OK), A.mult)
+        tt(b("H", 48, 96), sm(H2), sm(OK), A.mult)
+        ts(b("ND"), p(7, 0, 72), 0.0, A.is_equal)
+        te, to, to2 = b("S", NC * TE, NC * TE + HC), b("S", NC * TO, NC * TO + HC), b("S", NC * TO + HC, NC * TO + NC)
+        tt(to, b("ND", 0, 24), smp(Q, 1), A.mult)
+        tt(te, b("ND", 48, 72), smp(Q, 0), A.mult)
+        tt(to2, to, b("ND", 24, 48), A.mult)
+        ts(b("SO", 0, NC, 2), te, co(DE), A.add)
+        ts(b("SO", 1, NC, 2), to2, co(DO), A.add)
+        if t == 2:
+            act(b("hz"), b(ZN), F.Identity, 3064.5)
+        for h in (0, 1):
+            mm(p(6 + h, 0, HT), b("Ih"), b("onesh"), True, False)
+            for r in range(16):
+                u = b("Uh", 144 * r + 15 - t, 144 * r + 143 - t)
+                mm(p(4 + h, r, HT, 16), u, b("H", HC * h, HC * h + HC), True, False)
+                mm(p(4 + h, r, HT, 16), u, b("H", 48 + HC * h, 72 + HC * h), False, True)
+                mm(p(6 + h, r, HT, 16), u, b("H", 96 + HC * h, 120 + HC * h), False, r == 15)
+        if t == 2:
+            for a0, a1 in ((0, 512), (512, NT)):
+                mm(p(0, a0, a1), b("I15"), b(ZN, a0, a1), True, False)
+                mm(p(0, a0, a1), b("Bz"), b("hz", a0, a1), False, True)
+            act(b("YZ"), p(0, 0, NT), F.Identity, co(BZ))
+            dma("s", (T.yz[:], []), b("YZ"))
+        for k in range(23, -1, -1):
+            so = b("SO", 2 * k, 2 * k + 2)
+            kk = (ind(b("K", 0, EXT), so), b("KA", 32 * k, 32 * k + 32), b("KB", 32 * k, 32 * k + 32), A.add)
+            xx = (ind(b("XC", 0, EXT), so), b("XC", ext + 32 * k, ext + 32 * k + 32), b("T1", 32 * k, 32 * k + 32), A.add)
+            if k == 18:
+                tt(hf("KB", 0), p(2, 0, HT), hf("M3", 0), A.mult)
+            tt(*kk)
+            tt(*xx)
+
+    dma("s", b("r14"), (T.XC[14:128:16, 0:D], [("XC", 0, D, 1)]))
+    dma("g", (T.yc[:], []), (T.XC[15:128:16, 0:D], [("XC", 0, D, 1)]))
+    for k in range(16):
+        mm(p(2, 0, 256), b("I14"), b("XC", 256 * k, 256 * k + 256), k == 0, False)
+    act(p(0, 0, 512), b("K", 1024, 1536), F.Copy)
+    act(p(1, 0, 256), b("K", 2560, 2816), F.Copy)
+    act(b("h14"), b("r14"), F.Identity, 3064.5)
+    for k in range(11, 16):
+        mm(p(3, 0, 256), b("If"), b("K", 256 * k, 256 * k + 256), k == 11, k == 15)
+        if k == 12:
+            mm(p(2, 0, 256), b("Wb", 1, 129), b("r14"), False, False)
+            mm(p(2, 0, 256), b("Bm"), b("h14"), False, True)
+    act(b("YX"), p(2, 0, 256), F.Identity, co(BX))
+    dma("a", (T.yx[:], []), b("YX"))
+    for h in (0, 1):
+        tt(hf("K", h), hf("K", h), p(6 + h, 0, HT), A.mult)
+    for h in (0, 1):
+        tt(hf("K", h), hf("K", h), p(4 + h, 0, HT), A.add)
+    acc = p(0, 0, 512)
+    tt(acc, acc, b("K", 1536, 2048), A.add)
+    tt(b("YT"), p(1, 0, 256), b("K", 0, 256), A.add)
+    tt(acc, acc, b("K", 2048, 2560), A.add)
+    tt(acc, acc, b("K", 512, 1024), A.add)
+    tt(b("YU"), p(0, 0, 256), b("K", 256, 512), A.add)
+    tt(b("YT"), p(0, 256, 512), b("YT"), A.add)
+    tt(b("YU"), b("YU"), b("YT"), A.add)
+    tt(b("YK"), p(3, 0, 256), b("YU"), A.add)
+    dma("s", (T.yk[:], []), b("YK"))
+
+    _emit(ops, queues, T)

@@ -2,6 +2,7 @@ from concourse.mybir import AluOpType as A, ActivationFunctionType as F
 
 D, NT, NC, HT, HC = 4096, 768, 48, 384, 24
 EXT = D + 32
+QT, QC, WB = 192, 12, (2, 3, 6, 7)
 f32, bf, fh, i32, u16 = "float32", "bfloat16", "float16", "int32", "uint16"
 
 
@@ -17,12 +18,12 @@ SCRATCH = {
     "GA": _sb(NT, f32), "GB": _sb(NT, f32), "KA": _sb(NT, f32), "KB": _sb(NT, f32),
     "M1": _sb(NT, bf), "M2": _sb(NT, bf), "M3": _sb(NT, bf), "NM": _sb(NT, bf),
     "AB0": _sb(NT, bf), "AB1": _sb(NT, bf), "AB2": _sb(NT, bf), "AB3": _sb(NT, bf),
-    "TC": _sb(3 * NT, bf), "EQ": _sb(1152, bf), "PK": _sb(8 * NC, f32),
+    "TC": _sb(3 * NT, bf), "EQ": _sb(1152, bf), "PK": _sb(16 * NC, f32),
     "KI": _sb(192, i32), "PL": _sb(192, i32), "CI": _sb(192, i32), "OFF": _sb(192, u16), "ZO": _sb(NC, u16),
     "ZA": _sb(96, fh), "ZB": _sb(96, fh), "H": _sb(144, fh),
-    "S": _sb(NC * 16, f32), "E3": _sb(144, f32), "ND": _sb(72, f32),
+    "S": _sb(NC * 16, f32), "E3": _sb(144, f32), "Wk": _sb(144, bf),
     "ones": _sb(384, bf), "onesh": _sb(384, fh), "kr": _sb(16, i32), "kr2": _sb(16, i32), "RM": _sb(16, f32), "GE": _sb(16, f32),
-    "col": _sb(16, f32), "BO0": _sb(128, bf), "BOb": _sb(128, bf), "BOf": _sb(128, f32),
+    "W4": _sb(132, f32), "col": _sb(24, f32), "BO0": _sb(128, bf), "BOb": _sb(128, bf), "BOf": _sb(128, f32),
     "W0": _sb(144, bf), "Wb": _sb(144, bf), "W8": _sb(136, f32), "SEL": _sb(NC, f32),
     "Ib": _sb(144, bf), "If": _sb(128, f32), "Ih": _sb(128, fh), "nIh": _sb(128, fh),
     "Sb": _sb(12 * 128, bf), "Eh": _sb(16 * 128, fh), "Uh": _sb(16 * 144, fh),
@@ -44,6 +45,75 @@ def _meet(x, y):
     if x[3] > 1 and x[3] == y[3] and (x[1] - y[1]) % x[3]:
         return False
     return True
+
+
+WAKE, SLACK, CYC, PCYC, GAT, SCA = 0.17, 0.03, 0.9e-3, 0.45e-3, 1.56, 3.8
+ORDER = []
+
+
+def _plan(ops):
+    n_ops = len(ops)
+    hist, pred, last, sent = {}, [], {}, {}
+    for n, op in enumerate(ops):
+        q, deps = op["q"], {}
+        touch = [(x, False) for x in op["r"]] + [(x, True) for x in op["w"]]
+        for acc, wr in touch:
+            bank = (acc[0], acc[1] // 512 * 512, (acc[2] + 511) // 512 * 512, 1)
+            for m, x, w in hist.get(acc[0], []):
+                same = ops[m]["q"] == q
+                if acc[0] == "P" and (not same or q == "p"):
+                    if _meet(bank, (x[0], x[1], x[2], 1)):
+                        deps[m] = 0.0 if same else WAKE
+                elif (w or wr) and _meet(acc, x):
+                    deps[m] = WAKE
+        for acc, wr in touch:
+            hist.setdefault(acc[0], []).append((n, acc, wr))
+        if q in ("s", "g") and q in last:
+            deps.setdefault(last[q], None)
+        last[q] = n
+        if op["sem"][:3] == "snt":
+            sent[op["sem"][3:]] = n
+        if q is None:
+            deps[sent[op["sem"][3:]]] = 0.0
+        pred.append(deps)
+    succ = [[] for _ in ops]
+    for n in range(n_ops):
+        for m in pred[n]:
+            succ[m].append(n)
+    rank = [0.0] * n_ops
+    for n in range(n_ops - 1, -1, -1):
+        rank[n] = ops[n]["c"] + ops[n]["lat"] + max([rank[k] + (pred[k][n] or 0.0) for k in succ[n]] + [0.0])
+    left = [len(d) for d in pred]
+    ready = {}
+    at, done, issued, free, bus, order = [0.0] * n_ops, [0.0] * n_ops, [0.0] * n_ops, {}, [0.0], []
+    for n in range(n_ops):
+        if not left[n]:
+            ready.setdefault(ops[n]["q"], []).append(n)
+    while len(order) < n_ops:
+        best = None
+        for q, lst in ready.items():
+            if lst:
+                t0 = max(free.get(q, 0.0), min(at[k] for k in lst))
+                if best is None or t0 < best[0]:
+                    best = (t0, q)
+        t0, q = best
+        n = max([k for k in ready[q] if at[k] <= t0 + SLACK], key=lambda k: (int(rank[k] / (1.5 if q == "p" else 0.3)), -k))
+        ready[q].remove(n)
+        issued[n] = max(t0, at[n]) + ops[n]["c"]
+        free[q] = issued[n]
+        if ops[n]["dma"] and q is not None:
+            bus[0] = max(bus[0], issued[n]) + ops[n]["lat"] - 2.0
+            done[n] = bus[0] + 2.0
+        else:
+            done[n] = issued[n]
+        order.append(n)
+        for k in succ[n]:
+            lat = pred[k][n]
+            at[k] = max(at[k], issued[n] if lat is None else done[n] + lat)
+            left[k] -= 1
+            if not left[k]:
+                ready.setdefault(ops[k]["q"], []).append(k)
+    return order
 
 
 def _emit(ops, queues, T):
@@ -128,7 +198,10 @@ def rank_program(g, core, T, topo):
     def ind(win, off):
         return (win[0].indirect(off[0]), win[1], off[1])
 
-    def rec(q, f, outs, ins):
+    def cols(x):
+        return (x[1][0][2] - x[1][0][1] + x[1][0][3] - 1) // x[1][0][3]
+
+    def rec(q, f, outs, ins, both=False):
         r, w = [], []
         for x in ins:
             if isinstance(x, tuple):
@@ -139,7 +212,21 @@ def rank_program(g, core, T, topo):
             w += x[1]
             if len(x) == 3:
                 r += x[2]
-        ops.append({"q": q, "f": f, "r": r, "w": w, "dma": False, "sem": semof[q], "inc": 1, "own": False})
+        o, tens = outs[0], [x for x in ins if isinstance(x, tuple)]
+        two = [SCRATCH[x[1][0][0]][2] in (bf, fh, u16) for x in [o] + tens[:1]]
+        if q == "p":
+            c = max(64, cols(tens[1])) * PCYC * (1 if SCRATCH[tens[1][1][0][0]][2] != f32 else 4)
+        elif q == "g":
+            c = 0.17 + 2 * cols(o) * CYC
+        elif len(o) == 3:
+            c = 0.05 + cols(tens[0]) * SCA * CYC
+        elif tens and len(tens[0]) == 3:
+            c = 0.06 + cols(o) * GAT * CYC
+        elif both:
+            c = max(64, cols(o) * (1 if "P" in (tens[0][1][0][0], tens[1][1][0][0]) else 2)) * CYC
+        else:
+            c = max(64, cols(o) * (0.5 if q == "v" and all(two) else 1)) * CYC
+        ops.append({"q": q, "f": f, "r": r, "w": w, "dma": False, "sem": semof[q], "inc": 1, "own": False, "c": c, "lat": 0.0})
 
     def v_(x):
         return x[0] if isinstance(x, tuple) else x
@@ -148,7 +235,8 @@ def rank_program(g, core, T, topo):
         s = "d%d" % nd[0]
         nd[0] += 1
         ops.append({"q": q, "f": lambda: queues[q].dma_start(out[0], in_[0]), "r": in_[1], "w": out[1], "dma": True,
-                    "sem": s, "inc": 16, "own": False})
+                    "sem": s, "inc": 16, "own": False, "c": 1.5 if q == "g" else 0.1,
+                    "lat": 2.0 + (cols(out) * 512 if out[1] and out[1][0][0] == "K" else 120000) / 200e3})
 
     def ts(out, in0, s1, op0, s2=None, op1=None):
         if op1 is None:
@@ -157,7 +245,7 @@ def rank_program(g, core, T, topo):
             rec("v", lambda: g.vector.tensor_scalar(out[0], in0[0], v_(s1), v_(s2), op0, op1), [out], [in0, s1, s2])
 
     def tt(out, in0, in1, op):
-        rec("v", lambda: g.vector.tensor_tensor(out[0], in0[0], in1[0], op), [out], [in0, in1])
+        rec("v", lambda: g.vector.tensor_tensor(out[0], in0[0], in1[0], op), [out], [in0, in1], True)
 
     def cp(out, in_):
         rec("v", lambda: g.vector.tensor_copy(out[0], in_[0]), [out], [in_])
@@ -199,7 +287,7 @@ def rank_program(g, core, T, topo):
     def co(k):
         return b("col", k, k + 1)
 
-    SC, NSC, N15, C16, L14, BX, BZ, DE, DO, CT = range(10)
+    SC, NSC, N15, C16, L14, BX, BZ, DE, DO, CT, UP = range(11)
     OK, OK3, OK012, M01, Q1, ZT, ZT2, CN1, H1, H2, Q0, Q, TE, TO, Q1A = range(15)
 
     dma("a", b("L0"), (T.zin[:], []))
@@ -230,11 +318,17 @@ def rank_program(g, core, T, topo):
 
     for j in range(4):
         turned("Sb", 128 * j, "BOb", 0, rm(j))
-    ts(b("SEL", 0, NC, 2), b("ones", 0, HC), co(SC), A.mult, 8.0, A.is_lt)
-    ts(b("SEL", 1, NC, 2), b("ones", 0, HC), co(SC), A.mult, 8.0, A.is_ge)
+    ts(b("GE"), b("c16", 0, 16), 0.0625, A.mult, co(SC), A.is_le)
+    ms(b("SEL", 0, NC, 4), -8388608.0)
+    for u in (1, 2, 3):
+        ts(co(UP + u), b("GE", 4 * u, 4 * u + 1), -10485760.0, A.mult)
+        ts(co(UP + 3 + u), b("GE", 4 * u - 4, 4 * u - 3), 2097152.0, A.mult, co(UP + u), A.add)
+        ts(b("SEL", u, NC, 4), b("ones", 0, QC), co(UP + 3 + u), A.mult)
+    ts(co(UP), co(SC), 12.0, A.is_lt, 2097152.0, A.mult)
+    tt(b("W8"), b("Wb", 8, 144), b("Wb", 0, 136), A.add)
+    tt(b("W4"), b("W8", 4, 136), b("W8", 0, 132), A.add)
     ts(co(N15), rm(15), -1.0, A.mult, 1.0, A.add)
     ts(co(C16), rm(15), 16.0, A.mult)
-    tt(b("W8"), b("Wb", 8, 144), b("Wb", 0, 136), A.add)
     ts(b("I15"), b("Ib", 0, 128), co(N15), A.mult)
     ts(b("tm"), b("Ib", 1, 129), co(C16), A.mult)
     cp(b("Ih"), b("Ib", 0, 128))
@@ -244,7 +338,6 @@ def rank_program(g, core, T, topo):
         ms(b("Pn", 0, 24), 1024.0)
         ms(b("Pn", 24, 48), 0.0)
         ms(b("Pn", 48, 72), 1024.0)
-        ts(b("GE"), b("c16", 0, 16), 0.0625, A.mult, co(SC), A.is_le)
         ts(co(DE), co(SC), float(D), A.add)
         ts(co(DO), co(SC), float(D + 16), A.add)
         ms(b("XC", D, EXT), 0.0)
@@ -264,6 +357,7 @@ def rank_program(g, core, T, topo):
         for r in range(16):
             ts(b("Uh", 144 * r, 144 * r + 144), b("Wb"), rm(r), A.mult, 64.0, A.mult)
         cp(b("onesh"), b("ones"))
+        ts(b("Wk"), b("Wb"), 8192.0, A.mult)
         for t in (1, 2):
             for j in range(4 * t, 4 * t + 4):
                 turned("Sb", 128 * j, "BOb", t, rm(j))
@@ -279,14 +373,10 @@ def rank_program(g, core, T, topo):
         ts(b("Bz"), b("Bm"), rm(14), A.mult)
 
     def pack():
-        mm(p(6, 0, 256), b("Ib", 0, 128), b("x14"), True, False)
-        mm(p(6, 0, 256), b("I16"), b("x15"), False, True)
-        act(b("pk"), p(6, 0, 256), F.Copy)
+        mm(p(5, 256, 512), b("Ib", 0, 128), b("x14"), True, False)
+        mm(p(5, 256, 512), b("I16"), b("x15"), False, True)
+        act(b("pk"), p(5, 256, 512), F.Copy)
         dma("s", (T.XC[14:128:16, 0:D], [("XCa", 0, D, 1)]), b("pk"))
-
-    def write5(h):
-        tt(hf("K", h), hf("K", h), p(6 + h, 0, HT), A.mult)
-        tt(hf("K", h), hf("K", h), p(4 + h, 0, HT), A.add)
 
     banks = [range(0, 6), range(6, 11), range(11, 16)]
 
@@ -299,19 +389,27 @@ def rank_program(g, core, T, topo):
             return b(name, NC * m, NC * m + NC)
         return b(name, NC * m + HC * h, NC * m + HC * h + HC)
 
+    def qt(name, m, u):
+        return b(name, NC * m + QC * u, NC * m + QC * u + QC)
+
     def wrap8(m, h):
-        for q in range(8):
-            mm(p(2 + h, 0, NC), b("W8", 7 - q, 135 - q), b("GB" if m & 1 else "GA", HT * h + q, HT * h + HT, 8), q == 0, q == 7)
+        for u in (2 * h, 2 * h + 1):
+            for q in range(4):
+                mm(p(WB[u], 0, NC), b("W4", 3 - q, 131 - q), b("GB" if m & 1 else "GA", QT * u + q, QT * u + QT, 4), q == 0, q == 3)
 
     def small(m, h):
-        c0 = NC * (2 * m + h)
-        tt(b("PK", c0, c0 + NC), p(2 + h, 0, NC), b("SEL"), A.mult)
-        tt(part("KI", m, h), b("PK", c0, c0 + NC, 2), b("PK", c0 + 1, c0 + NC, 2), A.add)
-        ts(part("PL", m, h), part("KI", m, h), D - 1, A.bitwise_and)
-        cp(part("OFF", m, h), part("PL", m, h))
+        for u in (2 * h, 2 * h + 1):
+            c0 = NC * (4 * m + u)
+            o, d0, d1 = b("PK", c0, c0 + NC), b("SEL"), p(WB[u], 0, NC)
+            rec("v", lambda o=o, d0=d0, d1=d1: g.vector.tensor_tensor_scan(o[0], d0[0], d1[0], 0.0, A.add, A.max), [o], [d0, d1])
+            ts(qt("KI", m, u), b("PK", c0 + 3, c0 + NC, 4), co(UP), A.subtract)
+            ts(qt("PL", m, u), qt("KI", m, u), D - 1, A.bitwise_and)
+            cp(qt("OFF", m, u), qt("PL", m, u))
 
     def gather(m, h):
-        tt(hf("GB" if m & 1 else "GA", h), ind(b("K", 0, D), part("OFF", m - 1, h)), hf("M%d" % m, h), A.mult)
+        for u in (2 * h, 2 * h + 1):
+            tt(b("GB" if m & 1 else "GA", QT * u, QT * u + QT), ind(b("K", 0, D), qt("OFF", m - 1, u)),
+               b("M%d" % m, QT * u, QT * u + QT), A.mult)
 
     consts0()
     for t in range(3):
@@ -327,11 +425,17 @@ def rank_program(g, core, T, topo):
         cw = b("XC", 0, D) if t else b("C0")
 
         def counts(m, cw=cw):
-            act(b("TC", NT * m, NT * m + NT), ind(cw, part("OFF", m)), F.Identity, None, rm(15))
+            for h in (0, 1):
+                act(b("TC", NT * m + HT * h, NT * m + HT * h + HT), ind(cw, part("OFF", m, h)), F.Identity, None, rm(15))
+
+        def last(h, cw=cw):
+            for u in (2 * h, 2 * h + 1):
+                act(b("T1", QT * u, QT * u + QT), ind(cw, qt("OFF", 3, u)), F.Identity, rm(15), rm(15))
+                tt(b("KA", QT * u, QT * u + QT), ind(b("K", 0, D), qt("OFF", 3, u)), b("NM", QT * u, QT * u + QT), A.mult)
 
         if t:
             ops.append({"q": None, "f": None, "r": [], "w": b(L)[1], "dma": True, "sem": "arr%d" % t,
-                        "inc": len(topo.engines(prv, core)), "own": True})
+                        "inc": len(topo.engines(prv, core)), "own": True, "c": 0.0, "lat": 0.0})
         for h in (0, 1):
             mm(p(h, 0, HT), S_(0), hf(L, h))
         wide(2, S_(1), L)
@@ -345,9 +449,12 @@ def rank_program(g, core, T, topo):
         act(b("M1"), b("AB1"), F.Relu, 1.0, -1.0)
         act(b("M2"), b("AB2"), F.Relu, 1.0, -1.0)
         for h in (0, 1):
-            if t:
-                write5(h)
-            tt(hf("GA", h), hf("K", h), p(h, 0, HT), A.mult)
+            for j in (0, 1):
+                kq = b("K", HT * h + QT * j, HT * h + QT * j + QT)
+                if t:
+                    tt(kq, kq, p(6 + h, QT * j, QT * j + QT), A.mult)
+                    tt(kq, kq, p(4 + h, QT * j, QT * j + QT), A.add)
+                tt(b("GA", HT * h + QT * j, HT * h + QT * j + QT), kq, p(h, QT * j, QT * j + QT), A.mult)
             wrap8(0, h)
         wide(4, S_(3), L)
         mask(3, 4)
@@ -387,16 +494,15 @@ def rank_program(g, core, T, topo):
         small(2, 1)
         counts(2)
         gather(3, 1)
-        mm(p(7, 0, HT), b("BOf"), hf("GA", 1))
+        mm(p(4, 0, HT), b("BOf"), hf("GA", 1))
         wrap8(3, 1)
         small(3, 0)
-        act(hf("T1", 0), ind(cw, part("OFF", 3, 0)), F.Identity, rm(15), rm(15))
-        tt(hf("KB", 1), p(7, 0, HT), hf("M3", 1), A.mult)
-        tt(hf("KA", 0), ind(b("K", 0, D), part("OFF", 3, 0)), hf("NM", 0), A.mult)
+        last(0)
+        tt(hf("KB", 1), p(4, 0, HT), hf("M3", 1), A.mult)
         ts(b("CI", 0, 144), b("KI", 0, 144), 12, A.arith_shift_right)
         wrap(p(2, 0, 144), "TC", 3 * NT)
         small(3, 1)
-        act(hf("T1", 1), ind(cw, part("OFF", 3, 1)), F.Identity, rm(15), rm(15))
+        last(1)
         act(b("XC", ext, ext + NT), p(0, 0, NT), F.Copy)
         pl, ci = part("PL", 3), part("CI", 3)
         for k, par in enumerate((1, 1, 0, 0)):
@@ -416,12 +522,12 @@ def rank_program(g, core, T, topo):
         for k, par in enumerate((1, 1, 0, 0)):
             tt(b("ZB", HC * k, HC * k + HC), smp(CN1, par), smp(OK012, par), A.mult)
         tt(sm(Q1), sm(Q1A), sm(OK012), A.mult)
-        tt(hf("KA", 1), ind(b("K", 0, D), part("OFF", 3, 1)), hf("NM", 1), A.mult)
-        wrap(p(3, 0, NC), "T1", NT)
         for k in range(3):
             for r in banks[k]:
                 mm(dreg(r), b("Eh", 128 * r, 128 * r + 128), b("ZB", 0, 72), False, False)
                 mm(dreg(r), b("nIh"), b("ZB", 24, 96), False, r == banks[k][-1])
+            if k == 0:
+                wrap(p(3, 0, NC), "T1", NT)
         tt(sm(OK3), p(3, 0, NC), sm(CN1), A.is_equal)
         tt(sm(ZT), sm(OK3), sm(Q1), A.mult)
         tt(sm(OK), sm(OK3), sm(OK012), A.mult)
@@ -434,7 +540,7 @@ def rank_program(g, core, T, topo):
         if t < 2:
             rid, pid, _se = topo.addr(nxt)
             ops.append({"q": "g", "r": b(ZN)[1], "w": [], "dma": True, "sem": "snt%d" % (t + 1), "own": True,
-                        "inc": len(topo.engines(core, nxt)),
+                        "inc": len(topo.engines(core, nxt)), "c": 1.0, "lat": 3.5,
                         "f": lambda t=t, rid=rid, pid=pid: g.remote_dma(
                             T["L%d" % (t + 1)][:], T["ZN%d" % t][:], T.sem["arr%d" % (t + 1)], T.sem["snt%d" % (t + 1)],
                             pid, rid, topo.mask(core, nxt))})
@@ -442,18 +548,17 @@ def rank_program(g, core, T, topo):
             r0, r1 = banks[k][0], banks[k][-1] + 1
             tt(b("EQ", 72 * r0, 72 * r1), p(4 + k, 0, 72 * (r1 - r0)), b("Tp", 72 * r0, 72 * r1), A.is_equal)
         for r in range(16):
-            mm(p(7, 0, 72), b("Wb", 15 - r, 143 - r), b("EQ", 72 * r, 72 * r + 72), r == 0, r == 15)
+            mm(p(7, 0, 72), b("Wk", 15 - r, 143 - r), b("EQ", 72 * r, 72 * r + 72), r == 0, r == 15)
         mm(p(2, 0, HT), b("BOf"), hf("GA", 0))
         ts(b("H", 96, 144), sm(OK), -1.0 / 64, A.mult)
         tt(b("H", 0, 48), sm(H1), sm(OK), A.mult)
         tt(b("H", 48, 96), sm(H2), sm(OK), A.mult)
-        ts(b("ND"), p(7, 0, 72), 0.0, A.is_equal)
         te, to, to2 = b("S", NC * TE, NC * TE + HC), b("S", NC * TO, NC * TO + HC), b("S", NC * TO + HC, NC * TO + NC)
-        tt(to, b("ND", 0, 24), smp(Q, 1), A.mult)
-        tt(te, b("ND", 48, 72), smp(Q, 0), A.mult)
-        tt(to2, to, b("ND", 24, 48), A.mult)
-        ts(b("SO", 0, NC, 2), te, co(DE), A.add)
-        ts(b("SO", 1, NC, 2), to2, co(DO), A.add)
+        tt(to, p(7, 0, 24), smp(Q, 1), A.add)
+        tt(te, p(7, 48, 72), smp(Q, 0), A.add)
+        tt(to2, p(7, 24, 48), to, A.add)
+        ts(b("SO", 0, NC, 2), te, 0.0, A.min, co(DE), A.add)
+        ts(b("SO", 1, NC, 2), to2, 0.0, A.min, co(DO), A.add)
         if t == 2:
             act(b("hz"), b(ZN), F.Identity, 3064.5)
         for h in (0, 1):
@@ -487,7 +592,7 @@ def rank_program(g, core, T, topo):
     act(b("h14"), b("r14"), F.Identity, 3064.5)
     for k in range(11, 16):
         mm(p(3, 0, 256), b("If"), b("K", 256 * k, 256 * k + 256), k == 11, k == 15)
-        if k == 12:
+        if k == 15:
             mm(p(2, 0, 256), b("Wb", 1, 129), b("r14"), False, False)
             mm(p(2, 0, 256), b("Bm"), b("h14"), False, True)
     act(b("YX"), p(2, 0, 256), F.Identity, co(BX))
@@ -507,4 +612,6 @@ def rank_program(g, core, T, topo):
     tt(b("YK"), p(3, 0, 256), b("YU"), A.add)
     dma("s", (T.yk[:], []), b("YK"))
 
-    _emit(ops, queues, T)
+    if not ORDER:
+        ORDER.extend(_plan(ops))
+    _emit([ops[k] for k in ORDER], queues, T)

@@ -1,9 +1,12 @@
+import numpy as np
 from concourse.mybir import AluOpType as A, ActivationFunctionType as F
 
-D, NT, NC, HT, HC = 4096, 768, 48, 384, 24
-EXT = D + 32
-QT, QC, WB = 192, 12, (2, 3, 6, 7)
-f32, bf, fh, i32, u16 = "float32", "bfloat16", "float16", "int32", "uint16"
+D, NT, NC = 4096, 768, 48
+EXT = D + 64
+TT, TW, NB = 256, 16, 12
+BIG = 2097152.0
+WT = (2.0 ** 45, 2.0 ** 33, 2.0 ** 21)
+f32, bf, i32, u16 = "float32", "bfloat16", "int32", "uint16"
 
 
 def _sb(n, dt):
@@ -17,57 +20,82 @@ SCRATCH = {
     "C0": _sb(D, bf), "T1": _sb(NT, bf), "SO": _sb(NC, u16),
     "GA": _sb(NT, f32), "GB": _sb(NT, f32), "KA": _sb(NT, f32), "KB": _sb(NT, f32),
     "M1": _sb(NT, bf), "M2": _sb(NT, bf), "M3": _sb(NT, bf), "NM": _sb(NT, bf),
-    "AB0": _sb(NT, bf), "AB1": _sb(NT, bf), "AB2": _sb(NT, bf), "AB3": _sb(NT, bf),
-    "TC": _sb(3 * NT, bf), "EQ": _sb(1152, bf), "PK": _sb(16 * NC, f32),
-    "KI": _sb(192, i32), "PL": _sb(192, i32), "CI": _sb(192, i32), "OFF": _sb(192, u16), "ZO": _sb(NC, u16),
-    "ZA": _sb(96, fh), "ZB": _sb(96, fh), "H": _sb(144, fh),
-    "S": _sb(NC * 16, f32), "E3": _sb(144, f32), "Wk": _sb(144, bf),
-    "ones": _sb(384, bf), "onesh": _sb(384, fh), "kr": _sb(16, i32), "kr2": _sb(16, i32), "RM": _sb(16, f32), "GE": _sb(16, f32),
-    "W4": _sb(132, f32), "col": _sb(24, f32), "BO0": _sb(128, bf), "BOb": _sb(128, bf), "BOf": _sb(128, f32),
-    "W0": _sb(144, bf), "Wb": _sb(144, bf), "W8": _sb(136, f32), "SEL": _sb(NC, f32),
-    "Ib": _sb(144, bf), "If": _sb(128, f32), "Ih": _sb(128, fh), "nIh": _sb(128, fh),
-    "Sb": _sb(12 * 128, bf), "Eh": _sb(16 * 128, fh), "Uh": _sb(16 * 144, fh),
-    "R": _sb(3 * 128, bf), "I15": _sb(128, bf), "I14": _sb(128, bf), "Bm": _sb(128, bf), "Bz": _sb(128, bf),
-    "I16": _sb(128, bf), "tm": _sb(128, bf), "tn": _sb(128, bf),
-    "Pn": _sb(72, f32), "Tp": _sb(1152, fh), "c16": _sb(NC, f32), "zi": _sb(3 * NC, f32), "dum": _sb(NC, f32),
+    "LQ": _sb(NT, bf), "Sq": _sb(12 * 128, bf), "BO2": _sb(128, bf), "nBO": _sb(128, bf), "s2": _sb(128, bf),
+    "TC": _sb(3 * NT, bf), "PK": _sb(16 * NC, f32),
+    "KI": _sb(192, i32), "PL": _sb(192, i32), "OFF": _sb(192, u16), "ZO": _sb(NC, u16),
+    "OW": _sb(NC, f32), "OC": _sb(TW, u16), "CN": _sb(144, bf),
+    "OR": ("sbuf", [128, 3, TT], f32), "oc": _sb(TW, i32), "EQ": ("sbuf", [128, 4 * NB, 4, 16], bf), "OK": ("sbuf", [128, 2, NC], bf),
+    "S": _sb(NC * 8, f32), "Wk": _sb(144, bf), "Wt": _sb(16 * 128, bf), "Wf": _sb(144, f32), "Wd": _sb(144, bf),
+    "ones": _sb(256, bf), "kr": _sb(16, i32), "kr2": _sb(16, i32), "RM": _sb(16, f32), "GE": _sb(16, f32), "LT": _sb(16, f32),
+    "W4": _sb(132, f32), "col": _sb(32, f32), "BO0": _sb(128, bf), "BOb": _sb(128, bf), "BOf": _sb(128, f32),
+    "W0": _sb(144, bf), "Wb": _sb(144, bf), "W8": _sb(136, f32), "SEL": _sb(64, f32),
+    "Ib": _sb(144, bf), "If": _sb(128, f32), "BI": _sb(128, bf), "nBI": _sb(128, bf), "CB": _sb(128, bf),
+    "nW": _sb(3 * 128, bf), "nD": _sb(128, bf), "IU": _sb(128, bf), "Z0": _sb(128, bf),
+    "Sb": _sb(12 * 128, bf), "U": _sb(16 * 144, bf),
+    "R": _sb(128, bf), "I15": _sb(128, bf), "I14": _sb(128, bf), "Bm": _sb(128, bf), "Bz": _sb(128, bf),
+    "I16": _sb(128, bf), "tm": _sb(128, bf), "tn": _sb(128, bf), "to": _sb(128, bf),
+    "c16": _sb(NC, f32), "zi": _sb(3 * NC, f32), "dum": _sb(NC, f32),
     "x14": _sb(256, bf), "x15": _sb(256, bf), "cn": _sb(256, i32), "pk": _sb(256, bf), "cb": _sb(256, bf),
     "r14": _sb(256, bf), "h14": _sb(256, bf), "hz": _sb(NT, bf), "YZ": _sb(NT, bf), "YX": _sb(256, bf),
     "YT": _sb(256, f32), "YU": _sb(256, f32), "YK": _sb(256, f32),
-    "P": ("psum", [128, 4096], f32),
+    "P": ("psum", [128, 56, 64], f32), "PD": ("psum", [128, 8, 4, 16], f32),
 }
-NDMA = 24
+NDMA = 28
 SEMAPHORES = ["sv", "sa", "sp", "sg", "arr1", "arr2", "snt1", "snt2"] + ["d%d" % k for k in range(NDMA)]
+MASKS, PS = {}, ("P", "PD")
 
 
-def _meet(x, y):
-    if x[1] >= y[2] or y[1] >= x[2]:
-        return False
-    if x[3] > 1 and x[3] == y[3] and (x[1] - y[1]) % x[3]:
-        return False
-    return True
+def _mask(name, idx):
+    key = (name, repr(idx))
+    if key not in MASKS:
+        shape = SCRATCH[name][1][1:]
+        hit = np.zeros(shape, np.uint8)
+        hit[idx] = 1
+        flat = hit.reshape(-1)
+        if name in PS:
+            banks = np.repeat(flat.reshape(-1, 512).max(axis=1), 512)
+        else:
+            banks = flat
+        MASKS[key] = (int.from_bytes(np.packbits(flat).tobytes(), "big"), int.from_bytes(np.packbits(banks).tobytes(), "big"),
+                      int(flat.sum()))
+    return MASKS[key]
 
 
-WAKE, SLACK, CYC, PCYC, GAT, SCA = 0.17, 0.03, 0.9e-3, 0.45e-3, 1.56, 3.8
+WAKE, SLACK, HOLD, CYC, PCYC, GAT, SCA = 0.17, 0.03, 0.5, 0.83e-3, 0.42e-3, 1.56, 3.8
+PRI = {"mask": -5.0, "cnt": 0.5, "cwrap": 0.6, "own": 3.05, "last": 3.06, "pb": 3.35, "ok": 4.0, "eq": 4.2, "so": 4.3, "ka": 4.5,
+       "kb": 4.15, "five": 5.0, "sk": 6.0, "sx": 6.5, "const": 50.0}
 ORDER = []
 
 
-def _plan(ops):
-    n_ops = len(ops)
-    hist, pred, last, sent = {}, [], {}, {}
+def _deps(ops):
+    hist, pred = {}, []
     for n, op in enumerate(ops):
         q, deps = op["q"], {}
         touch = [(x, False) for x in op["r"]] + [(x, True) for x in op["w"]]
         for acc, wr in touch:
-            bank = (acc[0], acc[1] // 512 * 512, (acc[2] + 511) // 512 * 512, 1)
             for m, x, w in hist.get(acc[0], []):
                 same = ops[m]["q"] == q
-                if acc[0] == "P" and (not same or q == "p"):
-                    if _meet(bank, (x[0], x[1], x[2], 1)):
-                        deps[m] = 0.0 if same else WAKE
-                elif (w or wr) and _meet(acc, x):
-                    deps[m] = WAKE
+                if acc[0] in PS and (not same or q == "p"):
+                    if acc[2] & x[2]:
+                        deps[m] = not same
+                elif (w or wr) and acc[1] & x[1]:
+                    deps[m] = True
         for acc, wr in touch:
-            hist.setdefault(acc[0], []).append((n, acc, wr))
+            lst = hist.setdefault(acc[0], [])
+            if wr and acc[0] not in PS:
+                lst[:] = [h for h in lst if h[1][1] & ~acc[1]]
+            lst.append((n, acc, wr))
+        pred.append(deps)
+    return pred
+
+
+def _plan(ops):
+    n_ops = len(ops)
+    pred, last, sent = [], {}, {}
+    for n, deps in enumerate(_deps(ops)):
+        op = ops[n]
+        q = op["q"]
+        deps = {m: (WAKE if w else 0.0) for m, w in deps.items()}
         if q in ("s", "g") and q in last:
             deps.setdefault(last[q], None)
         last[q] = n
@@ -80,12 +108,12 @@ def _plan(ops):
     for n in range(n_ops):
         for m in pred[n]:
             succ[m].append(n)
-    rank = [0.0] * n_ops
+    pri = [op["pr"] for op in ops]
     for n in range(n_ops - 1, -1, -1):
-        rank[n] = ops[n]["c"] + ops[n]["lat"] + max([rank[k] + (pred[k][n] or 0.0) for k in succ[n]] + [0.0])
+        pri[n] = min([pri[n]] + [pri[k] for k in succ[n]])
     left = [len(d) for d in pred]
     ready = {}
-    at, done, issued, free, bus, order = [0.0] * n_ops, [0.0] * n_ops, [0.0] * n_ops, {}, [0.0], []
+    at, free, bus, order = [0.0] * n_ops, {}, 0.0, []
     for n in range(n_ops):
         if not left[n]:
             ready.setdefault(ops[n]["q"], []).append(n)
@@ -94,22 +122,31 @@ def _plan(ops):
         for q, lst in ready.items():
             if lst:
                 t0 = max(free.get(q, 0.0), min(at[k] for k in lst))
-                if best is None or t0 < best[0]:
-                    best = (t0, q)
-        t0, q = best
-        n = max([k for k in ready[q] if at[k] <= t0 + SLACK], key=lambda k: (int(rank[k] / (1.5 if q == "p" else 0.3)), -k))
+                limit, pick = 1e9, None
+                for k in sorted(lst, key=lambda k: (pri[k], k)):
+                    if max(t0, at[k]) + ops[k]["c"] <= limit + HOLD and at[k] <= t0 + SLACK:
+                        pick = k
+                        break
+                    limit = min(limit, at[k])
+                if pick is None:
+                    pick = min(lst, key=lambda k: (at[k] if at[k] > t0 + SLACK else 1e9, k))
+                    free[q] = at[pick]
+                    best = "again"
+                    break
+                if best is None or max(t0, at[pick]) < best[0]:
+                    best = (max(t0, at[pick]), q, pick)
+        if best == "again":
+            continue
+        t0, q, n = best
         ready[q].remove(n)
-        issued[n] = max(t0, at[n]) + ops[n]["c"]
-        free[q] = issued[n]
+        done = free[q] = t0 + ops[n]["c"]
         if ops[n]["dma"] and q is not None:
-            bus[0] = max(bus[0], issued[n]) + ops[n]["lat"] - 2.0
-            done[n] = bus[0] + 2.0
-        else:
-            done[n] = issued[n]
+            bus = max(bus, done) + ops[n]["lat"] - 2.0
+            done = bus + 2.0
         order.append(n)
         for k in succ[n]:
             lat = pred[k][n]
-            at[k] = max(at[k], issued[n] if lat is None else done[n] + lat)
+            at[k] = max(at[k], free[q] if lat is None else done + lat)
             left[k] -= 1
             if not left[k]:
                 ready.setdefault(ops[k]["q"], []).append(k)
@@ -117,31 +154,15 @@ def _plan(ops):
 
 
 def _emit(ops, queues, T):
-    hist, known, waits, need = {}, {}, [], set()
+    known, waits, need = {}, [], set()
     for q in queues:
         known[q] = {}
-    for n, op in enumerate(ops):
-        q, dma = op["q"], op["dma"]
-        deps = set()
-        touch = [(x, False) for x in op["r"]] + [(x, True) for x in op["w"]]
-        for acc, wr in touch:
-            bank = (acc[0], acc[1] // 512 * 512, (acc[2] + 511) // 512 * 512, 1)
-            for m, x, w in hist.get(acc[0], []):
-                o = ops[m]
-                if o["q"] == q and not dma and not o["dma"]:
-                    if q != "p" and (w or wr) and _meet(acc, x):
-                        deps.add(m)
-                elif acc[0] == "P":
-                    if _meet(bank, (x[0], x[1], x[2], 1)):
-                        deps.add(m)
-                elif (w or wr) and _meet(acc, x):
-                    deps.add(m)
-        for acc, wr in touch:
-            hist.setdefault(acc[0], []).append((n, acc, wr))
+    for n, deps in enumerate(_deps(ops)):
+        op = ops[n]
         mine = []
-        if q is not None:
-            kn = known[q]
-            for m in sorted(deps, reverse=True):
+        if op["q"] is not None:
+            kn = known[op["q"]]
+            for m in sorted([m for m, w in deps.items() if w], reverse=True):
                 key = ops[m]["sem"]
                 if kn.get(key, -1) >= m:
                     continue
@@ -181,25 +202,34 @@ def rank_program(g, core, T, topo):
     nxt, prv = T.cores[(rank + 1) % n_ranks], T.cores[(rank - 1) % n_ranks]
     queues = {"g": g, "v": g.vector, "a": g.scalar, "p": g.tensor, "s": g.sync}
     semof = {"g": "sg", "v": "sv", "a": "sa", "p": "sp"}
-    ops, nd = [], [0]
+    ops, nd, now = [], [0], [-10.0]
+    s_, al = slice, slice(None)
+
+    def nd_(name, *idx):
+        return (T[name][(al,) + idx], [(name,) + _mask(name, idx)])
 
     def b(name, a=0, e=None, st=1):
-        if e is None:
-            e = SCRATCH[name][1][1]
-        ap = T[name][:, a:e] if st == 1 else T[name][:, a:e:st]
-        return (ap, [(name, a, e, st)])
+        return nd_(name, s_(a, SCRATCH[name][1][1] if e is None else e, st if st > 1 else None))
 
-    def p(bank, a, e, st=1):
-        return b("P", 512 * bank + a, 512 * bank + e, st)
+    def p(bank, a, e):
+        if bank == 7:
+            return nd_("PD", s_(a // 64, e // 64), al, al)
+        return nd_("P", s_(8 * bank + a // 64, 8 * bank + e // 64), al)
 
-    def hf(name, h):
-        return b(name, HT * h, HT * h + HT)
+    def p48(bank, k=0, a=0, e=NC):
+        return nd_("P", 8 * bank + k, s_(a, e))
+
+    def th(name, u, o=0):
+        return b(name, o + TT * u, o + TT * u + TT)
+
+    def rows(name):
+        return [(name, 1, 1, D)]
 
     def ind(win, off):
         return (win[0].indirect(off[0]), win[1], off[1])
 
     def cols(x):
-        return (x[1][0][2] - x[1][0][1] + x[1][0][3] - 1) // x[1][0][3]
+        return x[1][0][3]
 
     def rec(q, f, outs, ins, both=False):
         r, w = [], []
@@ -213,7 +243,7 @@ def rank_program(g, core, T, topo):
             if len(x) == 3:
                 r += x[2]
         o, tens = outs[0], [x for x in ins if isinstance(x, tuple)]
-        two = [SCRATCH[x[1][0][0]][2] in (bf, fh, u16) for x in [o] + tens[:1]]
+        two = [SCRATCH[x[1][0][0]][2] in (bf, u16) for x in [o] + tens[:1]]
         if q == "p":
             c = max(64, cols(tens[1])) * PCYC * (1 if SCRATCH[tens[1][1][0][0]][2] != f32 else 4)
         elif q == "g":
@@ -223,10 +253,11 @@ def rank_program(g, core, T, topo):
         elif tens and len(tens[0]) == 3:
             c = 0.06 + cols(o) * GAT * CYC
         elif both:
-            c = max(64, cols(o) * (1 if "P" in (tens[0][1][0][0], tens[1][1][0][0]) else 2)) * CYC
+            c = max(64, cols(o) * (1 if tens[0][1][0][0] in PS or tens[1][1][0][0] in PS else 2)) * CYC
         else:
             c = max(64, cols(o) * (0.5 if q == "v" and all(two) else 1)) * CYC
-        ops.append({"q": q, "f": f, "r": r, "w": w, "dma": False, "sem": semof[q], "inc": 1, "own": False, "c": c, "lat": 0.0})
+        ops.append({"q": q, "f": f, "r": r, "w": w, "dma": False, "sem": semof[q], "inc": 1, "own": False, "c": c, "lat": 0.0,
+                    "pr": now[0]})
 
     def v_(x):
         return x[0] if isinstance(x, tuple) else x
@@ -235,7 +266,7 @@ def rank_program(g, core, T, topo):
         s = "d%d" % nd[0]
         nd[0] += 1
         ops.append({"q": q, "f": lambda: queues[q].dma_start(out[0], in_[0]), "r": in_[1], "w": out[1], "dma": True,
-                    "sem": s, "inc": 16, "own": False, "c": 1.5 if q == "g" else 0.1,
+                    "sem": s, "inc": 16, "own": False, "c": 1.5 if q == "g" else 0.1, "pr": now[0],
                     "lat": 2.0 + (cols(out) * 512 if out[1] and out[1][0][0] == "K" else 120000) / 200e3})
 
     def ts(out, in0, s1, op0, s2=None, op1=None):
@@ -267,19 +298,16 @@ def rank_program(g, core, T, topo):
     def sel(out, in_, pattern, cmp, base, cm):
         rec("g", lambda: g.affine_select(out[0], in_[0], pattern, cmp, 0.0, base, cm), [out], [in_])
 
-    def wrap(out, src, n):
+    def wrap(out, mat, src, a, start, stop):
         for r in range(16):
-            mm(out, b("Wb", 15 - r, 143 - r), b(src, r, n, 16), r == 0, r == 15)
+            mm(out, b(mat, 15 - r, 143 - r), b(src, a + r, a + NT, 16), start and r == 0, stop and r == 15)
 
-    def wide(bank, mat, src):
-        mm(p(bank, 0, 512), mat, b(src, 0, 512))
-        mm(p(bank, 512, NT), mat, b(src, 512, NT))
+    def wide(bank, mat, src, start=True, stop=True):
+        mm(p(bank, 0, 512), mat, b(src, 0, 512), start, stop)
+        mm(p(bank, 512, NT), mat, b(src, 512, NT), start, stop)
 
-    def sm(k):
-        return b("S", NC * k, NC * k + NC)
-
-    def smp(k, par):
-        return b("S", NC * k + par, NC * k + NC, 2)
+    def sm(k, a=0, st=1):
+        return b("S", NC * k + a, NC * k + NC, st)
 
     def rm(r):
         return b("RM", r, r + 1)
@@ -287,8 +315,9 @@ def rank_program(g, core, T, topo):
     def co(k):
         return b("col", k, k + 1)
 
-    SC, NSC, N15, C16, L14, BX, BZ, DE, DO, CT, UP = range(11)
-    OK, OK3, OK012, M01, Q1, ZT, ZT2, CN1, H1, H2, Q0, Q, TE, TO, Q1A = range(15)
+    SC, S2, N15, C16, L14, BX, BZ, CT, NU, DE, UP, B1, CW = 0, 1, 2, 3, 4, 5, 6, 7, 8, 9, 13, 20, 21
+    ZB, Q0, Q, TO, Q1, ZT, ZT2 = range(7)
+    MB = (3, 4, 6)
 
     dma("a", b("L0"), (T.zin[:], []))
     dma("s", b("K", 0, NT), (T.nkey[:, 0:NT], []))
@@ -297,319 +326,272 @@ def rank_program(g, core, T, topo):
     dma("s", b("x14"), (T.xreg[14:128:16, :], []))
     dma("s", b("x15"), (T.xreg[15:128:16, :], []))
 
+    now[0] = PRI["const"]
     ms(b("ones"), 1.0)
     rec("g", lambda: g.iota(T.kr[:], [[-1, 16]], 16, 1), [b("kr")], [])
     sel(b("BO0"), b("ones", 0, 128), [[-16, 8], [0, 16]], A.is_ge, 0, 1)
     sel(b("BOb"), b("BO0"), [[16, 8], [0, 16]], A.is_ge, 15, -1)
+    rec("g", lambda: g.iota(T.s2[:], [[0, 8], [2, 16]], 0, 0, allow_small_or_imprecise_dtypes=True), [b("s2")], [])
     sel(b("W0"), b("ones", 0, 144), [[-16, 9], [256, 16]], A.is_ge, -3840, 1)
     sel(b("Wb"), b("W0"), [[16, 9], [0, 16]], A.is_ge, 15, -1)
     sel(b("Ib"), b("ones", 0, 144), [[-1, 144]], A.is_equal, 0, 1)
     rec("g", lambda: g.iota(T.c16[:], [[16, NC]], 0, 0, allow_small_or_imprecise_dtypes=True), [b("c16")], [])
+    rec("g", lambda: g.iota(T.oc[:], [[1, 4], [4, 4]], 0, 0), [b("oc")], [])
     rec("g", lambda: g.iota(T.C0[:], [[0, D]], 0, 0, allow_small_or_imprecise_dtypes=True), [b("C0")], [])
     ts(b("kr2"), b("kr"), 15, A.bitwise_and)
     ts(b("RM"), b("kr2"), 0.0, A.is_equal)
     cp(co(SC), b("kr2", 0, 1))
-    ts(co(NSC), b("kr2", 0, 1), -1.0, A.mult)
 
     def turned(out, o0, src, t, scal):
         ts(b(out, o0 + 16 * t, o0 + 128), b(src, 0, 128 - 16 * t), scal, A.mult)
         if t:
             ts(b(out, o0, o0 + 16 * t), b(src, 128 - 16 * t, 128), scal, A.mult)
 
-    for j in range(4):
-        turned("Sb", 128 * j, "BOb", 0, rm(j))
+    tt(b("BO2"), b("BOb"), b("s2"), A.mult)
+    ts(b("nBO"), b("BOb"), -1.0, A.mult)
+    ts(co(S2), co(SC), co(SC), A.mult)
+    ts(co(B1), co(S2), -1.0, A.mult, 1.0, A.add)
+    for j in range(12):
+        turned("Sb", 128 * j, "BO2", j // 4, rm(j))
+        turned("Sq", 128 * j, "nBO", j // 4, rm(j))
     ts(b("GE"), b("c16", 0, 16), 0.0625, A.mult, co(SC), A.is_le)
-    ms(b("SEL", 0, NC, 4), -8388608.0)
+    ms(b("SEL", 0, 64, 4), -8388608.0)
     for u in (1, 2, 3):
         ts(co(UP + u), b("GE", 4 * u, 4 * u + 1), -10485760.0, A.mult)
-        ts(co(UP + 3 + u), b("GE", 4 * u - 4, 4 * u - 3), 2097152.0, A.mult, co(UP + u), A.add)
-        ts(b("SEL", u, NC, 4), b("ones", 0, QC), co(UP + 3 + u), A.mult)
-    ts(co(UP), co(SC), 12.0, A.is_lt, 2097152.0, A.mult)
+        ts(co(UP + 3 + u), b("GE", 4 * u - 4, 4 * u - 3), BIG, A.mult, co(UP + u), A.add)
+        ts(b("SEL", u, 64, 4), b("ones", 0, TW), co(UP + 3 + u), A.mult)
+    ts(co(UP), co(SC), 12.0, A.is_lt, BIG, A.mult)
     tt(b("W8"), b("Wb", 8, 144), b("Wb", 0, 136), A.add)
     tt(b("W4"), b("W8", 4, 136), b("W8", 0, 132), A.add)
     ts(co(N15), rm(15), -1.0, A.mult, 1.0, A.add)
     ts(co(C16), rm(15), 16.0, A.mult)
     ts(b("I15"), b("Ib", 0, 128), co(N15), A.mult)
     ts(b("tm"), b("Ib", 1, 129), co(C16), A.mult)
-    cp(b("Ih"), b("Ib", 0, 128))
     tt(b("R", 0, 128), b("I15"), b("tm"), A.add)
+    for a in range(4):
+        ts(co(DE + a), co(SC), float(D + 16 * a), A.add)
+        ts(b("dum", a, NC, 4), b("ones", 0, NB), co(DE + a), A.mult)
+    ms(b("XC", D, EXT), 0.0)
+    cp(b("BOf"), b("BOb"))
+    cp(b("Wf"), b("Wb"))
+    ts(b("I16"), b("Ib", 0, 128), 16.0, A.mult)
+    ts(b("BI"), b("Ib", 0, 128), BIG, A.mult)
+    ts(b("nBI"), b("Ib", 0, 128), -BIG, A.mult)
+    ts(b("to"), b("Ib", 1, 129), float(D), A.mult)
+    tt(b("CB"), b("to"), b("nBI"), A.add)
+    for m in range(3):
+        ts(co(CW + m), rm(15), WT[m], A.mult)
+        ts(b("nW", 128 * m, 128 * m + 128), b("Ib", 0, 128), -WT[m] / D, A.mult)
+    ts(b("nD"), b("Ib", 0, 128), -float(D), A.mult)
+    ts(b("IU"), b("Ib", 0, 128), co(UP), A.mult)
+    ts(b("Wd"), b("Wb"), float(D), A.mult)
+    ts(co(NU), co(UP), -1.0, A.mult)
+    cp(b("OC"), b("oc"))
+    ms(b("Z0"), 0.0)
+    ts(b("LT"), b("GE"), -8192.0, A.mult, 8192.0, A.add)
+    ts(b("Wk"), b("Wb"), 8192.0, A.mult)
+    for r in range(16):
+        ts(b("Wt", 128 * r, 128 * r + 128), b("Wb", 15 - r, 143 - r), b("LT", r, r + 1), A.mult)
+    for t in range(3):
+        ts(b("zi", NC * t, NC * t + NC), b("c16"), co(SC), A.add, float(EXT + NT * t), A.add)
+    for r in range(16):
+        ts(b("U", 144 * r, 144 * r + 144), b("Wb"), rm(r), A.mult, BIG, A.mult)
+    ts(co(L14), co(SC), 14.0, A.is_lt)
+    ts(co(CT), rm(15), -192.0, A.mult)
+    ts(b("tn"), b("Wb", 0, 128), 0.0625, A.mult)
+    cp(b("If"), b("Ib", 0, 128))
+    ts(co(BZ), rm(14), 3072.0, A.mult, co(CT), A.add)
+    ts(b("I14"), b("Ib", 0, 128), co(L14), A.mult)
+    tt(b("Bm"), b("tn"), b("Wb", 1, 129), A.subtract)
+    ts(co(BX), co(BZ), 16.0, A.mult)
+    ts(b("Bz"), b("Bm"), rm(14), A.mult)
 
-    def consts0():
-        ms(b("Pn", 0, 24), 1024.0)
-        ms(b("Pn", 24, 48), 0.0)
-        ms(b("Pn", 48, 72), 1024.0)
-        ts(co(DE), co(SC), float(D), A.add)
-        ts(co(DO), co(SC), float(D + 16), A.add)
-        ms(b("XC", D, EXT), 0.0)
-        cp(b("BOf"), b("BOb"))
-        ts(b("I16"), b("Ib", 0, 128), 16.0, A.mult)
-        for r in range(16):
-            ts(b("Tp", 72 * r, 72 * r + 72), b("Pn"), b("GE", r, r + 1), A.mult)
-
-    def consts1():
-        for r in range(16):
-            ts(b("Eh", 128 * r, 128 * r + 128), b("BOb"), rm(r), A.mult)
-        ts(b("nIh"), b("Ib", 0, 128), -1.0, A.mult)
-        for t in range(3):
-            ts(b("zi", NC * t, NC * t + NC), b("c16"), co(SC), A.add, float(EXT + NT * t), A.add)
-        ts(b("dum", 0, NC, 2), b("c16", 0, HC), 0.0, A.mult, co(DE), A.add)
-        ts(b("dum", 1, NC, 2), b("c16", 0, HC), 0.0, A.mult, co(DO), A.add)
-        for r in range(16):
-            ts(b("Uh", 144 * r, 144 * r + 144), b("Wb"), rm(r), A.mult, 64.0, A.mult)
-        cp(b("onesh"), b("ones"))
-        ts(b("Wk"), b("Wb"), 8192.0, A.mult)
-        for t in (1, 2):
-            for j in range(4 * t, 4 * t + 4):
-                turned("Sb", 128 * j, "BOb", t, rm(j))
-            turned("R", 128 * t, "Ib", t, co(N15))
-        ts(co(L14), co(SC), 14.0, A.is_lt)
-        ts(co(CT), rm(15), -192.0, A.mult)
-        ts(b("tn"), b("Wb", 0, 128), 0.0625, A.mult)
-        cp(b("If"), b("Ib", 0, 128))
-        ts(co(BZ), rm(14), 3072.0, A.mult, co(CT), A.add)
-        ts(b("I14"), b("Ib", 0, 128), co(L14), A.mult)
-        tt(b("Bm"), b("tn"), b("Wb", 1, 129), A.subtract)
-        ts(co(BX), co(BZ), 16.0, A.mult)
-        ts(b("Bz"), b("Bm"), rm(14), A.mult)
-
-    def pack():
-        mm(p(5, 256, 512), b("Ib", 0, 128), b("x14"), True, False)
-        mm(p(5, 256, 512), b("I16"), b("x15"), False, True)
-        act(b("pk"), p(5, 256, 512), F.Copy)
-        dma("s", (T.XC[14:128:16, 0:D], [("XCa", 0, D, 1)]), b("pk"))
-
-    banks = [range(0, 6), range(6, 11), range(11, 16)]
-
-    def dreg(r):
-        k = 0 if r < 6 else (1 if r < 11 else 2)
-        return p(4 + k, 72 * (r - banks[k][0]), 72 * (r - banks[k][0]) + 72)
-
-    def part(name, m, h=None):
-        if h is None:
+    def part(name, m, u=None):
+        if u is None:
             return b(name, NC * m, NC * m + NC)
-        return b(name, NC * m + HC * h, NC * m + HC * h + HC)
+        return b(name, NC * m + TW * u, NC * m + TW * u + TW)
 
-    def qt(name, m, u):
-        return b(name, NC * m + QC * u, NC * m + QC * u + QC)
+    def gbuf(m):
+        return "GB" if m & 1 else "GA"
 
-    def wrap8(m, h):
-        for u in (2 * h, 2 * h + 1):
-            for q in range(4):
-                mm(p(WB[u], 0, NC), b("W4", 3 - q, 131 - q), b("GB" if m & 1 else "GA", QT * u + q, QT * u + QT, 4), q == 0, q == 3)
+    def step(m, u):
+        for q in range(4):
+            mm(p(u, 0, 64), b("W4", 3 - q, 131 - q), b(gbuf(m), TT * u + q, TT * u + TT, 4), q == 0, q == 3)
+        c0 = 64 * (3 * m + u)
+        o, d0, d1 = b("PK", c0, c0 + 64), b("SEL"), p48(u, 0, 0, 64)
+        rec("v", lambda: g.vector.tensor_tensor_scan(o[0], d0[0], d1[0], 0.0, A.add, A.max), [o], [d0, d1])
+        ts(part("KI", m, u), b("PK", c0 + 3, c0 + 64, 4), co(UP), A.subtract)
+        ts(part("PL", m, u), part("KI", m, u), D - 1, A.bitwise_and)
+        cp(part("OFF", m, u), part("PL", m, u))
 
-    def small(m, h):
-        for u in (2 * h, 2 * h + 1):
-            c0 = NC * (4 * m + u)
-            o, d0, d1 = b("PK", c0, c0 + NC), b("SEL"), p(WB[u], 0, NC)
-            rec("v", lambda o=o, d0=d0, d1=d1: g.vector.tensor_tensor_scan(o[0], d0[0], d1[0], 0.0, A.add, A.max), [o], [d0, d1])
-            ts(qt("KI", m, u), b("PK", c0 + 3, c0 + NC, 4), co(UP), A.subtract)
-            ts(qt("PL", m, u), qt("KI", m, u), D - 1, A.bitwise_and)
-            cp(qt("OFF", m, u), qt("PL", m, u))
+    def write5(u):
+        tt(th("K", u), th("K", u), p(u, 0, TT), A.min)
+        tt(th("K", u), th("K", u), p(u, TT, 512), A.max)
 
-    def gather(m, h):
-        for u in (2 * h, 2 * h + 1):
-            tt(b("GB" if m & 1 else "GA", QT * u, QT * u + QT), ind(b("K", 0, D), qt("OFF", m - 1, u)),
-               b("M%d" % m, QT * u, QT * u + QT), A.mult)
-
-    consts0()
     for t in range(3):
         L, ext, ZN = "L%d" % t, EXT + NT * t, "ZN%d" % t
-
-        def S_(m, t=t):
-            return b("Sb", 128 * (4 * t + m), 128 * (4 * t + m) + 128)
-
-        def mask(m, bank):
-            act(b("AB%d" % m), p(bank, 0, NT), F.Abs, co(NSC))
-            act(b("M%d" % m), b("AB%d" % m), F.Relu, 1.0, -1.0)
-
         cw = b("XC", 0, D) if t else b("C0")
 
+        def at(name, d=0.0, t=t):
+            now[0] = 100.0 * t + (PRI[name] if name else 0.0) + d
+
         def counts(m, cw=cw):
-            for h in (0, 1):
-                act(b("TC", NT * m + HT * h, NT * m + HT * h + HT), ind(cw, part("OFF", m, h)), F.Identity, None, rm(15))
+            at("cnt", m)
+            for u in ((0, 1, 2) if m == 2 else (None,)):
+                o = b("TC", NT * m, NT * m + NT) if u is None else th("TC", u, NT * m)
+                act(o, ind(cw, part("OFF", m, u)), F.Identity, None, co(CW + m))
+            tt(part("CN", m), part("KI", m), part("PL", m), A.subtract)
+            at("cwrap", m)
+            mm(p48(6, 4), b("nW", 128 * m, 128 * m + 128), part("CN", m), m == 0, False)
+            wrap(p48(6, 4), "Wb", "TC", NT * m, False, m == 2)
 
-        def last(h, cw=cw):
-            for u in (2 * h, 2 * h + 1):
-                act(b("T1", QT * u, QT * u + QT), ind(cw, qt("OFF", 3, u)), F.Identity, rm(15), rm(15))
-                tt(b("KA", QT * u, QT * u + QT), ind(b("K", 0, D), qt("OFF", 3, u)), b("NM", QT * u, QT * u + QT), A.mult)
-
+        at("mask")
         if t:
-            ops.append({"q": None, "f": None, "r": [], "w": b(L)[1], "dma": True, "sem": "arr%d" % t,
+            ops.append({"q": None, "f": None, "r": [], "w": b(L)[1], "dma": True, "sem": "arr%d" % t, "pr": now[0],
                         "inc": len(topo.engines(prv, core)), "own": True, "c": 0.0, "lat": 0.0})
-        for h in (0, 1):
-            mm(p(h, 0, HT), S_(0), hf(L, h))
-        wide(2, S_(1), L)
-        for h in (0, 1):
-            act(hf("AB0", h), p(h, 0, HT), F.Abs, co(NSC))
-        for h in (0, 1):
-            act(p(h, 0, HT), hf("AB0", h), F.Relu, 1.0, -1.0)
-        act(b("AB1"), p(2, 0, NT), F.Abs, co(NSC))
-        wide(2, S_(2), L)
-        act(b("AB2"), p(2, 0, NT), F.Abs, co(NSC))
-        act(b("M1"), b("AB1"), F.Relu, 1.0, -1.0)
-        act(b("M2"), b("AB2"), F.Relu, 1.0, -1.0)
-        for h in (0, 1):
-            for j in (0, 1):
-                kq = b("K", HT * h + QT * j, HT * h + QT * j + QT)
-                if t:
-                    tt(kq, kq, p(6 + h, QT * j, QT * j + QT), A.mult)
-                    tt(kq, kq, p(4 + h, QT * j, QT * j + QT), A.add)
-                tt(b("GA", HT * h + QT * j, HT * h + QT * j + QT), kq, p(h, QT * j, QT * j + QT), A.mult)
-            wrap8(0, h)
-        wide(4, S_(3), L)
-        mask(3, 4)
+        for m in range(4):
+            for u in range(3):
+                at(None, m + 0.1 * u)
+                if not m:
+                    act(th("LQ", u), th(L, u), F.Square)
+                o = p(5 + 2 * ((m + u) % 2) if m else MB[u], 0, TT)
+                j = 128 * (4 * t + m)
+                mm(o, b("Sb", j, j + 128), th(L, u), True, False)
+                mm(o, b("Sq", j, j + 128), th("LQ", u), False, True)
+                act(th("M%d" % m, u) if m else o, o, F.Relu, co(B1))
+                if m == 3:
+                    act(th("NM", u), o, F.Sign, co(S2), -1.0)
+        at("ok")
+        if t:
+            dma("s", (T.XC[16 * t:128, ext:ext + NT], b("XC", ext, ext + NT)[1]), (T[L][0:128 - 16 * t, :], b(L)[1]))
+            dma("s", (T.XC[0:16 * t, ext:ext + NT], rows("XCc")), (T[L][128 - 16 * t:128, :], b(L)[1]))
+        for u in range(3):
+            at(None, 0.1 * u)
+            if t:
+                write5(u)
+            tt(th("GA", u), th("K", u), p(MB[u], 0, TT), A.mult)
+            step(0, u)
         if not t:
+            at(None, 1.0)
             cp(b("cb"), b("cn"))
-            act(b("NM"), b("AB3"), F.Sign)
             dma("s", (T.C0[15:128:16, :], b("C0")[1]), b("cb"))
-            dma("s", (T.XC[15:128:16, 0:D], [("XCb", 0, D, 1)]), b("cb"))
+            dma("s", (T.XC[15:128:16, 0:D], rows("XCb")), b("cb"))
             for k in range(8):
-                dma("s", (T.XC[16 * k:16 * k + 14, 0:D], [("XC%d" % k, 0, D, 1)]), (T.xreg[16 * k:16 * k + 14, :], []))
-            consts1()
-        small(0, 0)
-        if t:
-            gather(1, 0)
-        small(0, 1)
-        if not t:
-            gather(1, 0)
-        wrap8(1, 0)
-        gather(1, 1)
-        wrap8(1, 1)
-        if not t:
-            pack()
-        wide(0, b("R", 128 * t, 128 * t + 128), L)
+                dma("s", (T.XC[16 * k:16 * k + 14, 0:D], rows("XC%d" % k)), (T.xreg[16 * k:16 * k + 14, :], []))
+            mm(p(5, 256, 512), b("Ib", 0, 128), b("x14"), True, False)
+            mm(p(5, 256, 512), b("I16"), b("x15"), False, True)
+            act(b("pk"), p(5, 256, 512), F.Copy)
+            dma("s", (T.XC[14:128:16, 0:D], rows("XCa")), b("pk"))
+            wide(3, b("R"), L)
+            act(b("XC", ext, ext + NT), p(3, 0, NT), F.Copy)
         counts(0)
-        small(1, 0)
-        gather(2, 0)
-        wrap8(2, 0)
-        small(1, 1)
-        counts(1)
-        if t:
-            act(b("NM"), b("AB3"), F.Sign)
-        gather(2, 1)
-        wrap8(2, 1)
-        small(2, 0)
-        gather(3, 0)
-        wrap8(3, 0)
-        small(2, 1)
-        counts(2)
-        gather(3, 1)
-        mm(p(4, 0, HT), b("BOf"), hf("GA", 1))
-        wrap8(3, 1)
-        small(3, 0)
-        last(0)
-        tt(hf("KB", 1), p(4, 0, HT), hf("M3", 1), A.mult)
-        ts(b("CI", 0, 144), b("KI", 0, 144), 12, A.arith_shift_right)
-        wrap(p(2, 0, 144), "TC", 3 * NT)
-        small(3, 1)
-        last(1)
-        act(b("XC", ext, ext + NT), p(0, 0, NT), F.Copy)
-        pl, ci = part("PL", 3), part("CI", 3)
-        for k, par in enumerate((1, 1, 0, 0)):
-            ts(b("ZA", HC * k, HC * k + HC), b("PL", 144 + par, 192, 2), -2048.0, A.add, 1.0 / D, A.mult)
-        ts(ci, part("KI", 3), 12, A.arith_shift_right)
-        tt(sm(Q1A), pl, part("zi", t), A.subtract)
-        for r in range(16):
-            mm(dreg(r), b("Eh", 128 * r, 128 * r + 128), b("ZA", 0, 72), r in (0, 6, 11), False)
-            mm(dreg(r), b("nIh"), b("ZA", 24, 96), False, False)
-        ts(sm(CN1), ci, 1.0, A.add)
-        tt(b("E3"), p(2, 0, 144), b("CI", 0, 144), A.is_equal)
-        tt(sm(Q0), pl, b("dum"), A.subtract)
-        tt(sm(M01), b("E3", 0, 48), b("E3", 48, 96), A.mult)
-        ts(sm(H1), pl, 1.0 / 64, A.mult, -32.0, A.add)
-        tt(sm(OK012), sm(M01), b("E3", 96, 144), A.mult)
-        ts(sm(H2), ci, 1.5, A.add, 64.0, A.mult)
-        for k, par in enumerate((1, 1, 0, 0)):
-            tt(b("ZB", HC * k, HC * k + HC), smp(CN1, par), smp(OK012, par), A.mult)
-        tt(sm(Q1), sm(Q1A), sm(OK012), A.mult)
-        for k in range(3):
-            for r in banks[k]:
-                mm(dreg(r), b("Eh", 128 * r, 128 * r + 128), b("ZB", 0, 72), False, False)
-                mm(dreg(r), b("nIh"), b("ZB", 24, 96), False, r == banks[k][-1])
-            if k == 0:
-                wrap(p(3, 0, NC), "T1", NT)
-        tt(sm(OK3), p(3, 0, NC), sm(CN1), A.is_equal)
-        tt(sm(ZT), sm(OK3), sm(Q1), A.mult)
-        tt(sm(OK), sm(OK3), sm(OK012), A.mult)
+        for m in (1, 2, 3):
+            for u in range(3):
+                at(None, m + 0.1 * u)
+                tt(th(gbuf(m), u), ind(b("K", 0, D), part("OFF", m - 1, u)), th("M%d" % m, u), A.mult)
+                step(m, u)
+                if m == 3:
+                    at("pb", 0.1 * u)
+                    mm(p(3, TT * u, TT * u + TT), b("BOf"), th("GB", u))
+            if m < 3:
+                counts(m)
+        for u in range(3):
+            at("own", 0.1 * u)
+            tt(part("OW", 0, u), p48(6, 4, TW * u, TW * u + TW), b("PK", 64 * (9 + u) + 3, 64 * (10 + u), 4), A.add)
+            act(nd_("OR", u, al), ind(part("OW", 0, u), b("OC")), F.Identity, co(NU))
+            at("last", 0.1 * u)
+            act(th("T1", u), ind(cw, part("OFF", 3, u)), F.Identity, rm(15), rm(15))
+            at("ka", -0.1 * u)
+            tt(th("KA", u), ind(b("K", 0, D), part("OFF", 3, u)), th("NM", u), A.mult)
+        pl = part("PL", 3)
+        at("ok")
+        tt(sm(ZB), b("OW"), pl, A.subtract)
+        tt(sm(Q1), pl, part("zi", t), A.subtract)
+        mm(p48(5), b("nD"), b("ones", 0, NC), True, False)
+        mm(p48(5), b("IU"), b("ones", 0, NC), False, False)
+        wrap(p48(5), "Wd", "T1", 0, False, True)
+        ok = nd_("OK", 1, al)
+        tt(ok, p48(5), sm(ZB), A.is_equal)
+        tt(sm(ZT), sm(Q1), ok, A.mult)
         tt(sm(ZT2), sm(ZT), part("zi", t), A.add)
-        tt(sm(Q), sm(Q0), sm(OK), A.mult)
         cp(b("ZO"), sm(ZT2))
         xc = b("XC", 0, ext + NT)
-        xc = (xc[0], xc[1] + [("XC" + k, 0, D, 1) for k in "ab01234567"])
-        act(b(ZN), ind(xc, b("ZO")), F.Copy)
+        xc = (xc[0], xc[1] + [rows("XC" + k)[0] for k in "abc01234567"])
+        act(b(ZN), ind(xc, b("ZO")), F.Identity, None, co(N15))
         if t < 2:
             rid, pid, _se = topo.addr(nxt)
-            ops.append({"q": "g", "r": b(ZN)[1], "w": [], "dma": True, "sem": "snt%d" % (t + 1), "own": True,
-                        "inc": len(topo.engines(core, nxt)), "c": 1.0, "lat": 3.5,
+            ops.append({"q": "g", "r": b(ZN)[1], "w": [], "dma": True, "sem": "snt%d" % (t + 1), "own": True, "pr": now[0],
+                        "inc": len(topo.engines(core, nxt)), "c": 1.0, "lat": 3.0,
                         "f": lambda t=t, rid=rid, pid=pid: g.remote_dma(
                             T["L%d" % (t + 1)][:], T["ZN%d" % t][:], T.sem["arr%d" % (t + 1)], T.sem["snt%d" % (t + 1)],
                             pid, rid, topo.mask(core, nxt))})
-        for k in range(3):
-            r0, r1 = banks[k][0], banks[k][-1] + 1
-            tt(b("EQ", 72 * r0, 72 * r1), p(4 + k, 0, 72 * (r1 - r0)), b("Tp", 72 * r0, 72 * r1), A.is_equal)
-        for r in range(16):
-            mm(p(7, 0, 72), b("Wk", 15 - r, 143 - r), b("EQ", 72 * r, 72 * r + 72), r == 0, r == 15)
-        mm(p(2, 0, HT), b("BOf"), hf("GA", 0))
-        ts(b("H", 96, 144), sm(OK), -1.0 / 64, A.mult)
-        tt(b("H", 0, 48), sm(H1), sm(OK), A.mult)
-        tt(b("H", 48, 96), sm(H2), sm(OK), A.mult)
-        te, to, to2 = b("S", NC * TE, NC * TE + HC), b("S", NC * TO, NC * TO + HC), b("S", NC * TO + HC, NC * TO + NC)
-        tt(to, p(7, 0, 24), smp(Q, 1), A.add)
-        tt(te, p(7, 48, 72), smp(Q, 0), A.add)
-        tt(to2, p(7, 24, 48), to, A.add)
-        ts(b("SO", 0, NC, 2), te, 0.0, A.min, co(DE), A.add)
-        ts(b("SO", 1, NC, 2), to2, 0.0, A.min, co(DO), A.add)
+        at("eq")
+        mm(nd_("PD", s_(0, 3), al, s_(0, 4)), b("Z0"), b("ones", 0, NC), True, False)
+        for d in (3, 2, 1, 0):
+            for a in range(d, 4):
+                tt(nd_("EQ", s_(NB * d, NB * d + NB), a, al), nd_("P", s_(24, 24 + NB), s_(16 * a, 16 * a + 16)),
+                   nd_("OR", al, s_(64 * (a - d), 64 * (a - d) + 64)), A.is_equal)
+            for r in range(16):
+                mm(nd_("PD", s_(0, 3), al, s_(d, 4)), b("Wk", 15 - r, 143 - r) if d else b("Wt", 128 * r, 128 * r + 128),
+                   nd_("EQ", s_(NB * d, NB * d + NB), s_(d, 4), r), False, d == 0 and r == 15)
+        for u in (2, 1, 0):
+            at("kb" if u == 2 else "five", -0.1 * u)
+            o = p(5 if u == 1 else 6, 0, TT)
+            mm(o, b("nBI"), th("NM", u), True, False)
+            mm(o, b("BOf"), th("GA", u), False, True)
+            act(th("KB", u), o, F.Relu)
+        at("so")
+        tt(sm(Q0), pl, b("dum"), A.subtract)
+        tt(sm(Q), sm(Q0), ok, A.mult)
+        tt(sm(TO), nd_("PD", s_(0, 3), al, s_(0, 4)), sm(Q), A.add)
+        for a in range(4):
+            ts(b("SO", a, NC, 4), sm(TO, a, 4), 0.0, A.min, co(DE + a), A.add)
+        at("five")
+        ts(nd_("OK", 0, al), ok, -1.0, A.mult)
+        for u in range(3):
+            mm(p(u, 0, TT), b("BI"), b("ones"), True, False)
+            mm(p(u, TT, 512), b("CB"), b("ones"), False, False)
+            mm(p(u, TT, 512), b("Wf", 15 - t, 143 - t), th("GB", u), False, False)
+            for r in range(16):
+                mm(nd_("P", s_(8 * u, 8 * u + 8), s_(r, 64, 16)), b("U", 144 * r + 15 - t, 144 * r + 143 - t),
+                   nd_("OK", al, s_(TW * u, TW * u + TW)), False, r == 15)
         if t == 2:
             act(b("hz"), b(ZN), F.Identity, 3064.5)
-        for h in (0, 1):
-            mm(p(6 + h, 0, HT), b("Ih"), b("onesh"), True, False)
-            for r in range(16):
-                u = b("Uh", 144 * r + 15 - t, 144 * r + 143 - t)
-                mm(p(4 + h, r, HT, 16), u, b("H", HC * h, HC * h + HC), True, False)
-                mm(p(4 + h, r, HT, 16), u, b("H", 48 + HC * h, 72 + HC * h), False, True)
-                mm(p(6 + h, r, HT, 16), u, b("H", 96 + HC * h, 120 + HC * h), False, r == 15)
-        if t == 2:
-            for a0, a1 in ((0, 512), (512, NT)):
-                mm(p(0, a0, a1), b("I15"), b(ZN, a0, a1), True, False)
-                mm(p(0, a0, a1), b("Bz"), b("hz", a0, a1), False, True)
-            act(b("YZ"), p(0, 0, NT), F.Identity, co(BZ))
+            wide(3, b("I15"), ZN, True, False)
+            wide(3, b("Bz"), "hz", False, True)
+            act(b("YZ"), p(3, 0, NT), F.Identity, co(BZ))
             dma("s", (T.yz[:], []), b("YZ"))
-        for k in range(23, -1, -1):
-            so = b("SO", 2 * k, 2 * k + 2)
-            kk = (ind(b("K", 0, EXT), so), b("KA", 32 * k, 32 * k + 32), b("KB", 32 * k, 32 * k + 32), A.add)
-            xx = (ind(b("XC", 0, EXT), so), b("XC", ext + 32 * k, ext + 32 * k + 32), b("T1", 32 * k, 32 * k + 32), A.add)
-            if k == 18:
-                tt(hf("KB", 0), p(2, 0, HT), hf("M3", 0), A.mult)
-            tt(*kk)
-            tt(*xx)
+        for k in range(NB - 1, -1, -1):
+            so = b("SO", 4 * k, 4 * k + 4)
+            at("sk")
+            tt(ind(b("K", 0, EXT), so), b("KA", 64 * k, 64 * k + 64), b("KB", 64 * k, 64 * k + 64), A.add)
+            at("sx")
+            tt(ind(b("XC", 0, EXT), so), b("XC", ext + 64 * k, ext + 64 * k + 64), b("T1", 64 * k, 64 * k + 64), A.add)
 
-    dma("s", b("r14"), (T.XC[14:128:16, 0:D], [("XC", 0, D, 1)]))
-    dma("g", (T.yc[:], []), (T.XC[15:128:16, 0:D], [("XC", 0, D, 1)]))
+    now[0] = 300.0
+    dma("s", b("r14"), (T.XC[14:128:16, 0:D], b("XC", 0, D)[1]))
+    dma("g", (T.yc[:], []), (T.XC[15:128:16, 0:D], b("XC", 0, D)[1]))
     for k in range(16):
-        mm(p(2, 0, 256), b("I14"), b("XC", 256 * k, 256 * k + 256), k == 0, False)
-    act(p(0, 0, 512), b("K", 1024, 1536), F.Copy)
-    act(p(1, 0, 256), b("K", 2560, 2816), F.Copy)
+        mm(p(5, 0, 256), b("I14"), b("XC", 256 * k, 256 * k + 256), k == 0, False)
+    act(p(3, 0, 512), b("K", 768, 1280), F.Copy)
+    act(p(4, 0, 512), b("K", 1280, 1792), F.Copy)
     act(b("h14"), b("r14"), F.Identity, 3064.5)
     for k in range(11, 16):
-        mm(p(3, 0, 256), b("If"), b("K", 256 * k, 256 * k + 256), k == 11, k == 15)
-        if k == 15:
-            mm(p(2, 0, 256), b("Wb", 1, 129), b("r14"), False, False)
-            mm(p(2, 0, 256), b("Bm"), b("h14"), False, True)
-    act(b("YX"), p(2, 0, 256), F.Identity, co(BX))
+        mm(p(6, 0, 256), b("If"), b("K", 256 * k, 256 * k + 256), k == 11, k == 15)
+    mm(p(5, 0, 256), b("Wb", 1, 129), b("r14"), False, False)
+    mm(p(5, 0, 256), b("Bm"), b("h14"), False, True)
+    act(b("YX"), p(5, 0, 256), F.Identity, co(BX))
     dma("a", (T.yx[:], []), b("YX"))
-    for h in (0, 1):
-        tt(hf("K", h), hf("K", h), p(6 + h, 0, HT), A.mult)
-    for h in (0, 1):
-        tt(hf("K", h), hf("K", h), p(4 + h, 0, HT), A.add)
-    acc = p(0, 0, 512)
-    tt(acc, acc, b("K", 1536, 2048), A.add)
-    tt(b("YT"), p(1, 0, 256), b("K", 0, 256), A.add)
-    tt(acc, acc, b("K", 2048, 2560), A.add)
-    tt(acc, acc, b("K", 512, 1024), A.add)
-    tt(b("YU"), p(0, 0, 256), b("K", 256, 512), A.add)
-    tt(b("YT"), p(0, 256, 512), b("YT"), A.add)
-    tt(b("YU"), b("YU"), b("YT"), A.add)
-    tt(b("YK"), p(3, 0, 256), b("YU"), A.add)
+    for u in range(3):
+        write5(u)
+    tt(p(3, 0, 512), p(3, 0, 512), b("K", 1792, 2304), A.add)
+    tt(p(4, 0, 512), p(4, 0, 512), b("K", 2304, 2816), A.add)
+    tt(p(3, 0, 512), p(3, 0, 512), b("K", 0, 512), A.add)
+    tt(b("YT"), p(4, 0, 256), b("K", 512, 768), A.add)
+    tt(b("YT"), p(4, 256, 512), b("YT"), A.add)
+    tt(b("YU"), p(3, 0, 256), b("YT"), A.add)
+    tt(b("YU"), p(3, 256, 512), b("YU"), A.add)
+    tt(b("YK"), p(6, 0, 256), b("YU"), A.add)
     dma("s", (T.yk[:], []), b("YK"))
 
     if not ORDER:

@@ -3,7 +3,9 @@ from concourse.mybir import AluOpType as A, ActivationFunctionType as F
 
 D, NT, NC = 4096, 768, 48
 EXT = D + 64
-TT, TW, NB = 256, 16, 12
+TT, TW, HC, NB = 256, 16, 24, 12
+US = (2, 1, 0)
+CONV, KBS, CG, QS, QU = 10, 3, D - 2 * NT, "v", "a"
 BIG = 2097152.0
 WT = (2.0 ** 45, 2.0 ** 33, 2.0 ** 21)
 f32, bf, i32, u16 = "float32", "bfloat16", "int32", "uint16"
@@ -14,31 +16,31 @@ def _sb(n, dt):
 
 
 SCRATCH = {
-    "K": _sb(EXT, f32), "XC": _sb(EXT + 3 * NT, bf),
+    "K": _sb(EXT, f32), "XC": _sb(EXT + NT, bf), "XF": _sb(EXT + NT, f32), "f14": _sb(256, f32), "f15": _sb(256, f32),
     "L0": _sb(NT, bf), "L1": _sb(NT, bf), "L2": _sb(NT, bf),
     "ZN0": _sb(NT, bf), "ZN1": _sb(NT, bf), "ZN2": _sb(NT, bf),
     "C0": _sb(D, bf), "T1": _sb(NT, bf), "SO": _sb(NC, u16),
     "GA": _sb(NT, f32), "GB": _sb(NT, f32), "KA": _sb(NT, f32), "KB": _sb(NT, f32),
     "M1": _sb(NT, bf), "M2": _sb(NT, bf), "M3": _sb(NT, bf), "NM": _sb(NT, bf),
-    "LQ": _sb(NT, bf), "Sq": _sb(12 * 128, bf), "BO2": _sb(128, bf), "nBO": _sb(128, bf), "s2": _sb(128, bf),
-    "TC": _sb(3 * NT, bf), "PK": _sb(16 * NC, f32),
+    "LQ": _sb(NT, bf), "Sq": _sb(12 * 128, bf), "BO2": _sb(160, bf), "nBO": _sb(160, bf), "s2": _sb(128, bf),
+    "TC": _sb(3 * NT, bf), "PK": _sb(12 * NC, f32), "P3": _sb(NT, f32), "SL3": _sb(64, f32), "SLa": _sb(16, f32), "SLb": _sb(16, f32),
     "KI": _sb(192, i32), "PL": _sb(192, i32), "OFF": _sb(192, u16), "ZO": _sb(NC, u16),
-    "OW": _sb(NC, f32), "OC": _sb(TW, u16), "CN": _sb(144, bf),
-    "OR": ("sbuf", [128, 3, TT], f32), "oc": _sb(TW, i32), "EQ": ("sbuf", [128, 4 * NB, 4, 16], bf), "OK": ("sbuf", [128, 2, NC], bf),
-    "S": _sb(NC * 8, f32), "Wk": _sb(144, bf), "Wt": _sb(16 * 128, bf), "Wf": _sb(144, f32), "Wd": _sb(144, bf),
-    "ones": _sb(256, bf), "kr": _sb(16, i32), "kr2": _sb(16, i32), "RM": _sb(16, f32), "GE": _sb(16, f32), "LT": _sb(16, f32),
-    "W4": _sb(132, f32), "col": _sb(32, f32), "BO0": _sb(128, bf), "BOb": _sb(128, bf), "BOf": _sb(128, f32),
-    "W0": _sb(144, bf), "Wb": _sb(144, bf), "W8": _sb(136, f32), "SEL": _sb(64, f32),
+    "OW": _sb(NC, f32), "OC": _sb(HC, u16), "CN": _sb(144, bf), "DS": _sb(192, f32), "ZI": _sb(2 * NC, f32), "ZS": _sb(2 * NC, f32),
+    "OR": ("sbuf", [128, 2, 384], f32), "oc": _sb(HC, i32), "EQ": ("sbuf", [128, 4 * NB, 4, 16], bf), "OK": ("sbuf", [128, 2, 2 * NC], bf),
+    "S": _sb(NC * 8, f32), "Wk": _sb(132, bf), "Wt": _sb(4 * 128, bf), "Wf": _sb(144, f32), "Wd": _sb(144, bf),
+    "ones": _sb(256, bf), "kr": _sb(16, i32), "kr2": _sb(16, i32), "RM": _sb(16, f32), "GE": _sb(16, f32), "LT": _sb(128, bf),
+    "W4": _sb(132, f32), "col": _sb(40, f32), "BO0": _sb(128, bf), "BOb": _sb(128, bf), "BOf": _sb(128, f32),
+    "W0": _sb(144, bf), "Wb": _sb(144, bf), "W8": _sb(136, f32), "SEL": _sb(96, f32),
     "Ib": _sb(144, bf), "If": _sb(128, f32), "BI": _sb(128, bf), "nBI": _sb(128, bf), "CB": _sb(128, bf),
-    "nW": _sb(3 * 128, bf), "nD": _sb(128, bf), "IU": _sb(128, bf), "Z0": _sb(128, bf),
+    "nW": _sb(3 * 128, bf), "nD": _sb(128, bf), "IU": _sb(128, bf),
     "Sb": _sb(12 * 128, bf), "U": _sb(16 * 144, bf),
-    "R": _sb(128, bf), "I15": _sb(128, bf), "I14": _sb(128, bf), "Bm": _sb(128, bf), "Bz": _sb(128, bf),
-    "I16": _sb(128, bf), "tm": _sb(128, bf), "tn": _sb(128, bf), "to": _sb(128, bf),
-    "c16": _sb(NC, f32), "zi": _sb(3 * NC, f32), "dum": _sb(NC, f32),
+    "R": _sb(128, bf), "RB": _sb(16, f32), "I15": _sb(128, bf), "I14": _sb(128, bf), "Bm": _sb(128, bf), "Bz": _sb(128, bf),
+    "I16": _sb(160, bf), "tm": _sb(128, bf), "tn": _sb(128, bf), "to": _sb(128, bf), "tp": _sb(128, bf),
+    "c16": _sb(NC, f32), "dum": _sb(NC, f32),
     "x14": _sb(256, bf), "x15": _sb(256, bf), "cn": _sb(256, i32), "pk": _sb(256, bf), "cb": _sb(256, bf),
     "r14": _sb(256, bf), "h14": _sb(256, bf), "hz": _sb(NT, bf), "YZ": _sb(NT, bf), "YX": _sb(256, bf),
     "YT": _sb(256, f32), "YU": _sb(256, f32), "YK": _sb(256, f32),
-    "P": ("psum", [128, 56, 64], f32), "PD": ("psum", [128, 8, 4, 16], f32),
+    "P": ("psum", [128, 56, 64], f32), "PD": ("psum", [128, 512], f32),
 }
 NDMA = 28
 SEMAPHORES = ["sv", "sa", "sp", "sg", "arr1", "arr2", "snt1", "snt2"] + ["d%d" % k for k in range(NDMA)]
@@ -61,10 +63,11 @@ def _mask(name, idx):
     return MASKS[key]
 
 
-WAKE, SLACK, HOLD, CYC, PCYC, GAT, SCA = 0.17, 0.03, 0.5, 0.83e-3, 0.42e-3, 1.56, 3.8
-PRI = {"mask": -5.0, "cnt": 0.5, "cwrap": 0.6, "own": 3.05, "last": 3.06, "pb": 3.35, "ok": 4.0, "eq": 4.2, "so": 4.3, "ka": 4.5,
-       "kb": 4.15, "five": 5.0, "sk": 6.0, "sx": 6.5, "const": 50.0}
+WAKE, SLACK, HOLD, CYC, PCYC, GAT, SCA = 0.22, 0.03, 0.4, 0.83e-3, 0.42e-3, 1.56, 3.8
+DLAT, RATE, RLAT = 1.4, 350e3, 2.8
+LATER = {'regs.p': -3.0, 'src.p': 0.5, 'mask1.a': 1.0, 'count2.p': -0.5, 'kb0.p': 0.5, 'yz.v': 3.0, 'lower.v': 1.0, 'eq0.v': 5.0, 'const.v': 2.0, 'gather.v': -0.5, 'own0.v': 5.0, 'nm.a': -2.0, 'own1.a': -3.0, 'gather0.v': 1.0, 'step.p': 0.5, 'kb2.p': 5.0, 'kb1.a': -3.0, 'five.p': -0.5, 'five.v': -3.0, 'ka0.v': -1.0, 'src.a': 1.0, 'count2.a': -0.5, 'eq1.v': -0.5}
 ORDER = []
+HOOK = []
 
 
 def _deps(ops):
@@ -103,14 +106,23 @@ def _plan(ops):
             sent[op["sem"][3:]] = n
         if q is None:
             deps[sent[op["sem"][3:]]] = 0.0
+        if "after" in op:
+            deps.setdefault(op["after"], 0.0)
         pred.append(deps)
     succ = [[] for _ in ops]
     for n in range(n_ops):
         for m in pred[n]:
             succ[m].append(n)
-    pri = [op["pr"] for op in ops]
+    pri = [0.0] * n_ops
     for n in range(n_ops - 1, -1, -1):
-        pri[n] = min([pri[n]] + [pri[k] for k in succ[n]])
+        pri[n] = min([pri[k] - (pred[k][n] or 0.0) for k in succ[n]] + [0.0]) - ops[n]["c"] - ops[n]["lat"]
+    if HOOK:
+        return HOOK[0](ops, pred, succ, pri)
+    return _greedy(ops, pred, succ, [pri[n] + LATER.get(ops[n]["pr"], 0.0) for n in range(n_ops)])
+
+
+def _greedy(ops, pred, succ, pri):
+    n_ops = len(ops)
     left = [len(d) for d in pred]
     ready = {}
     at, free, bus, order = [0.0] * n_ops, {}, 0.0, []
@@ -141,8 +153,8 @@ def _plan(ops):
         ready[q].remove(n)
         done = free[q] = t0 + ops[n]["c"]
         if ops[n]["dma"] and q is not None:
-            bus = max(bus, done) + ops[n]["lat"] - 2.0
-            done = bus + 2.0
+            bus = max(bus, done) + ops[n]["lat"] - DLAT
+            done = bus + DLAT
         order.append(n)
         for k in succ[n]:
             lat = pred[k][n]
@@ -202,7 +214,11 @@ def rank_program(g, core, T, topo):
     nxt, prv = T.cores[(rank + 1) % n_ranks], T.cores[(rank - 1) % n_ranks]
     queues = {"g": g, "v": g.vector, "a": g.scalar, "p": g.tensor, "s": g.sync}
     semof = {"g": "sg", "v": "sv", "a": "sa", "p": "sp"}
-    ops, nd, now = [], [0], [-10.0]
+    ops, nd, now = [], [0], ["load"]
+
+    def at(name):
+        now[0] = name + "."
+
     s_, al = slice, slice(None)
 
     def nd_(name, *idx):
@@ -213,7 +229,7 @@ def rank_program(g, core, T, topo):
 
     def p(bank, a, e):
         if bank == 7:
-            return nd_("PD", s_(a // 64, e // 64), al, al)
+            return b("PD", a, e)
         return nd_("P", s_(8 * bank + a // 64, 8 * bank + e // 64), al)
 
     def p48(bank, k=0, a=0, e=NC):
@@ -244,20 +260,21 @@ def rank_program(g, core, T, topo):
                 r += x[2]
         o, tens = outs[0], [x for x in ins if isinstance(x, tuple)]
         two = [SCRATCH[x[1][0][0]][2] in (bf, u16) for x in [o] + tens[:1]]
+        k = 0
         if q == "p":
             c = max(64, cols(tens[1])) * PCYC * (1 if SCRATCH[tens[1][1][0][0]][2] != f32 else 4)
         elif q == "g":
             c = 0.17 + 2 * cols(o) * CYC
         elif len(o) == 3:
-            c = 0.05 + cols(tens[0]) * SCA * CYC
+            c, k = 0.06 + cols(tens[0]) * SCA * CYC, 1
         elif tens and len(tens[0]) == 3:
-            c = 0.06 + cols(o) * GAT * CYC
+            c, k = 0.06 + cols(o) * GAT * CYC, 2
         elif both:
             c = max(64, cols(o) * (1 if tens[0][1][0][0] in PS or tens[1][1][0][0] in PS else 2)) * CYC
         else:
             c = max(64, cols(o) * (0.5 if q == "v" and all(two) else 1)) * CYC
         ops.append({"q": q, "f": f, "r": r, "w": w, "dma": False, "sem": semof[q], "inc": 1, "own": False, "c": c, "lat": 0.0,
-                    "pr": now[0]})
+                    "pr": now[0] + q, "k": k})
 
     def v_(x):
         return x[0] if isinstance(x, tuple) else x
@@ -267,7 +284,7 @@ def rank_program(g, core, T, topo):
         nd[0] += 1
         ops.append({"q": q, "f": lambda: queues[q].dma_start(out[0], in_[0]), "r": in_[1], "w": out[1], "dma": True,
                     "sem": s, "inc": 16, "own": False, "c": 1.5 if q == "g" else 0.1, "pr": now[0],
-                    "lat": 2.0 + (cols(out) * 512 if out[1] and out[1][0][0] == "K" else 120000) / 200e3})
+                    "lat": DLAT + (cols(out) * 512 if out[1] and out[1][0][0] == "K" else 120000) / RATE})
 
     def ts(out, in0, s1, op0, s2=None, op1=None):
         if op1 is None:
@@ -277,6 +294,9 @@ def rank_program(g, core, T, topo):
 
     def tt(out, in0, in1, op):
         rec("v", lambda: g.vector.tensor_tensor(out[0], in0[0], in1[0], op), [out], [in0, in1], True)
+
+    def scan(out, d0, d1, op0, op1):
+        rec("v", lambda: g.vector.tensor_tensor_scan(out[0], d0[0], d1[0], 0.0, op0, op1), [out], [d0, d1])
 
     def cp(out, in_):
         rec("v", lambda: g.vector.tensor_copy(out[0], in_[0]), [out], [in_])
@@ -315,8 +335,9 @@ def rank_program(g, core, T, topo):
     def co(k):
         return b("col", k, k + 1)
 
-    SC, S2, N15, C16, L14, BX, BZ, CT, NU, DE, UP, B1, CW = 0, 1, 2, 3, 4, 5, 6, 7, 8, 9, 13, 20, 21
-    ZB, Q0, Q, TO, Q1, ZT, ZT2 = range(7)
+    SC, S2, N15, C16, L14, BX, BZ, CT, NU, U3, UP, B1, N16, CW, DE = 0, 1, 2, 3, 4, 5, 6, 7, 8, 9, 13, 20, 21, 22, 30
+    ZB, Q0, Q, TO = range(4)
+    came = [rows("XC" + k)[0] for k in "ab01234567"]
     MB = (3, 4, 6)
 
     dma("a", b("L0"), (T.zin[:], []))
@@ -326,7 +347,7 @@ def rank_program(g, core, T, topo):
     dma("s", b("x14"), (T.xreg[14:128:16, :], []))
     dma("s", b("x15"), (T.xreg[15:128:16, :], []))
 
-    now[0] = PRI["const"]
+    at("const")
     ms(b("ones"), 1.0)
     rec("g", lambda: g.iota(T.kr[:], [[-1, 16]], 16, 1), [b("kr")], [])
     sel(b("BO0"), b("ones", 0, 128), [[-16, 8], [0, 16]], A.is_ge, 0, 1)
@@ -336,66 +357,85 @@ def rank_program(g, core, T, topo):
     sel(b("Wb"), b("W0"), [[16, 9], [0, 16]], A.is_ge, 15, -1)
     sel(b("Ib"), b("ones", 0, 144), [[-1, 144]], A.is_equal, 0, 1)
     rec("g", lambda: g.iota(T.c16[:], [[16, NC]], 0, 0, allow_small_or_imprecise_dtypes=True), [b("c16")], [])
-    rec("g", lambda: g.iota(T.oc[:], [[1, 4], [4, 4]], 0, 0), [b("oc")], [])
-    rec("g", lambda: g.iota(T.C0[:], [[0, D]], 0, 0, allow_small_or_imprecise_dtypes=True), [b("C0")], [])
+    rec("g", lambda: g.iota(T.oc[:], [[1, 4], [4, 6]], 0, 0), [b("oc")], [])
+    rec("g", lambda: g.iota(T.C0[:, 0:CG], [[0, CG]], 0, 0, allow_small_or_imprecise_dtypes=True), [b("C0", 0, CG)], [])
+    for a in range(CG, D, NT):
+        act(b("C0", a, a + NT), b("L0"), F.Identity, None, 0.0)
+    for d in (1, 2, 3):
+        rec("g", lambda d=d: g.iota(T.EQ[:, NB * d:NB * d + NB, 0:d, :], [[0, NB], [0, 16 * d]], 0, 0,
+                                    allow_small_or_imprecise_dtypes=True), [nd_("EQ", s_(NB * d, NB * d + NB), s_(0, d), al)], [])
     ts(b("kr2"), b("kr"), 15, A.bitwise_and)
     ts(b("RM"), b("kr2"), 0.0, A.is_equal)
     cp(co(SC), b("kr2", 0, 1))
 
-    def turned(out, o0, src, t, scal):
-        ts(b(out, o0 + 16 * t, o0 + 128), b(src, 0, 128 - 16 * t), scal, A.mult)
-        if t:
-            ts(b(out, o0, o0 + 16 * t), b(src, 128 - 16 * t, 128), scal, A.mult)
+    def mul(q, out, in_, scal):
+        if q == "v":
+            ts(out, in_, scal, A.mult)
+        else:
+            act(out, in_, F.Identity, None, scal)
 
-    tt(b("BO2"), b("BOb"), b("s2"), A.mult)
-    ts(b("nBO"), b("BOb"), -1.0, A.mult)
+    tt(b("BO2", 32, 160), b("BOb"), b("s2"), A.mult)
+    ts(b("nBO", 32, 160), b("BOb"), -1.0, A.mult)
+    cp(b("BO2", 0, 32), b("BO2", 128, 160))
+    cp(b("nBO", 0, 32), b("nBO", 128, 160))
     ts(co(S2), co(SC), co(SC), A.mult)
     ts(co(B1), co(S2), -1.0, A.mult, 1.0, A.add)
     for j in range(12):
-        turned("Sb", 128 * j, "BO2", j // 4, rm(j))
-        turned("Sq", 128 * j, "nBO", j // 4, rm(j))
+        for name, src in (("Sb", "BO2"), ("Sq", "nBO")):
+            mul("v" if j < 4 else QS, b(name, 128 * j, 128 * j + 128), b(src, 32 - 16 * (j // 4), 160 - 16 * (j // 4)), rm(j))
     ts(b("GE"), b("c16", 0, 16), 0.0625, A.mult, co(SC), A.is_le)
-    ms(b("SEL", 0, 64, 4), -8388608.0)
+    ms(b("SEL", 0, 96, 4), -8388608.0)
     for u in (1, 2, 3):
         ts(co(UP + u), b("GE", 4 * u, 4 * u + 1), -10485760.0, A.mult)
         ts(co(UP + 3 + u), b("GE", 4 * u - 4, 4 * u - 3), BIG, A.mult, co(UP + u), A.add)
-        ts(b("SEL", u, 64, 4), b("ones", 0, TW), co(UP + 3 + u), A.mult)
+        ts(b("SEL", u, 96, 4), b("ones", 0, HC), co(UP + 3 + u), A.mult)
     ts(co(UP), co(SC), 12.0, A.is_lt, BIG, A.mult)
+    ts(co(U3), co(SC), 15.0, A.is_lt, BIG, A.mult)
+    ts(b("SLa"), b("GE"), -8388608.0, A.mult)
+    ts(b("SLb", 1, 16), b("RM", 0, 15), BIG, A.mult)
+    ms(b("SLb", 0, 1), 0.0)
+    for k in range(4):
+        tt(b("SL3", 16 * k, 16 * k + 16), b("SLa"), b("SLb"), A.add)
     tt(b("W8"), b("Wb", 8, 144), b("Wb", 0, 136), A.add)
     tt(b("W4"), b("W8", 4, 136), b("W8", 0, 132), A.add)
     ts(co(N15), rm(15), -1.0, A.mult, 1.0, A.add)
-    ts(co(C16), rm(15), 16.0, A.mult)
+    ts(co(N16), co(N15), 0.0625, A.mult)
+    ts(co(C16), rm(15), 256.0, A.mult)
     ts(b("I15"), b("Ib", 0, 128), co(N15), A.mult)
     ts(b("tm"), b("Ib", 1, 129), co(C16), A.mult)
-    tt(b("R", 0, 128), b("I15"), b("tm"), A.add)
+    ts(b("tp"), b("I15"), 16.0, A.mult)
+    tt(b("R"), b("tp"), b("tm"), A.add)
+    ts(b("I16", 32, 160), b("Ib", 0, 128), 16.0, A.mult)
+    cp(b("I16", 0, 32), b("I16", 128, 160))
     for a in range(4):
         ts(co(DE + a), co(SC), float(D + 16 * a), A.add)
+        ts(co(DE + 4 + a), co(DE + a), co(UP), A.subtract)
         ts(b("dum", a, NC, 4), b("ones", 0, NB), co(DE + a), A.mult)
     ms(b("XC", D, EXT), 0.0)
     cp(b("BOf"), b("BOb"))
     cp(b("Wf"), b("Wb"))
-    ts(b("I16"), b("Ib", 0, 128), 16.0, A.mult)
     ts(b("BI"), b("Ib", 0, 128), BIG, A.mult)
     ts(b("nBI"), b("Ib", 0, 128), -BIG, A.mult)
     ts(b("to"), b("Ib", 1, 129), float(D), A.mult)
     tt(b("CB"), b("to"), b("nBI"), A.add)
+    for m in range(8):
+        ts(co(CW + m), rm(15), (WT + (1.0,))[m % 4] * (0.0625 if m > 3 else 1.0), A.mult)
     for m in range(3):
-        ts(co(CW + m), rm(15), WT[m], A.mult)
         ts(b("nW", 128 * m, 128 * m + 128), b("Ib", 0, 128), -WT[m] / D, A.mult)
     ts(b("nD"), b("Ib", 0, 128), -float(D), A.mult)
-    ts(b("IU"), b("Ib", 0, 128), co(UP), A.mult)
+    ts(b("IU"), b("Ib", 0, 128), co(U3), A.mult)
     ts(b("Wd"), b("Wb"), float(D), A.mult)
-    ts(co(NU), co(UP), -1.0, A.mult)
+    ts(co(NU), co(U3), -1.0, A.mult)
     cp(b("OC"), b("oc"))
-    ms(b("Z0"), 0.0)
-    ts(b("LT"), b("GE"), -8192.0, A.mult, 8192.0, A.add)
-    ts(b("Wk"), b("Wb"), 8192.0, A.mult)
+    ms(nd_("OK", al, al), 0.0)
+    ts(b("LT"), b("s2"), 0.5, A.mult, co(SC), A.is_gt)
+    ts(b("Wk"), b("W4"), 8192.0, A.mult)
+    for q in range(4):
+        tt(b("Wt", 128 * q, 128 * q + 128), b("Wk", 3 - q, 131 - q), b("LT"), A.mult)
+    ts(b("ZI", 1, 2 * NC, 2), b("c16"), co(SC), A.add, float(EXT), A.add)
+    ts(b("RB"), b("RM"), BIG, A.mult)
     for r in range(16):
-        ts(b("Wt", 128 * r, 128 * r + 128), b("Wb", 15 - r, 143 - r), b("LT", r, r + 1), A.mult)
-    for t in range(3):
-        ts(b("zi", NC * t, NC * t + NC), b("c16"), co(SC), A.add, float(EXT + NT * t), A.add)
-    for r in range(16):
-        ts(b("U", 144 * r, 144 * r + 144), b("Wb"), rm(r), A.mult, BIG, A.mult)
+        mul(QU, b("U", 144 * r, 144 * r + 144), b("Wb"), b("RB", r, r + 1))
     ts(co(L14), co(SC), 14.0, A.is_lt)
     ts(co(CT), rm(15), -192.0, A.mult)
     ts(b("tn"), b("Wb", 0, 128), 0.0625, A.mult)
@@ -415,33 +455,38 @@ def rank_program(g, core, T, topo):
         return "GB" if m & 1 else "GA"
 
     def step(m, u):
-        for q in range(4):
-            mm(p(u, 0, 64), b("W4", 3 - q, 131 - q), b(gbuf(m), TT * u + q, TT * u + TT, 4), q == 0, q == 3)
-        c0 = 64 * (3 * m + u)
-        o, d0, d1 = b("PK", c0, c0 + 64), b("SEL"), p48(u, 0, 0, 64)
-        rec("v", lambda: g.vector.tensor_tensor_scan(o[0], d0[0], d1[0], 0.0, A.add, A.max), [o], [d0, d1])
-        ts(part("KI", m, u), b("PK", c0 + 3, c0 + 64, 4), co(UP), A.subtract)
+        at("step")
+        if m < 3:
+            for q in range(4):
+                mm(p(u, 0, 64), b("W4", 3 - q, 131 - q), b(gbuf(m), TT * u + q, TT * u + TT, 4), q == 0, q == 3)
+            c0 = 64 * (3 * m + u)
+            scan(b("PK", c0, c0 + 64), b("SEL", 0, 64), p48(u, 0, 0, 64), A.add, A.max)
+            ts(part("KI", m, u), b("PK", c0 + 3, c0 + 64, 4), co(UP), A.subtract)
+        else:
+            mm(p(3, TT * u, TT * u + TT), b("BOf"), th("GB", u))
+            for k in range(4 * u, 4 * u + 4):
+                scan(b("P3", 64 * k, 64 * k + 64), b("SL3"), p48(3, k, 0, 64), A.add, A.max)
+            ts(part("KI", m, u), b("P3", TT * u + 15, TT * u + TT, 16), co(U3), A.subtract)
         ts(part("PL", m, u), part("KI", m, u), D - 1, A.bitwise_and)
         cp(part("OFF", m, u), part("PL", m, u))
 
     def write5(u):
+        at("lower")
         tt(th("K", u), th("K", u), p(u, 0, TT), A.min)
+        at("lift")
         tt(th("K", u), th("K", u), p(u, TT, 512), A.max)
 
     for t in range(3):
-        L, ext, ZN = "L%d" % t, EXT + NT * t, "ZN%d" % t
-        cw = b("XC", 0, D) if t else b("C0")
+        L, ZN = "L%d" % t, "ZN%d" % t
+        cw = b("XF", 0, D) if t else b("C0")
+        sc = 4 if t else 0
 
-        def at(name, d=0.0, t=t):
-            now[0] = 100.0 * t + (PRI[name] if name else 0.0) + d
-
-        def counts(m, cw=cw):
-            at("cnt", m)
-            for u in ((0, 1, 2) if m == 2 else (None,)):
+        def counts(m, cw=cw, sc=sc):
+            at("count%d" % m)
+            for u in (US if m == 2 else (None,)):
                 o = b("TC", NT * m, NT * m + NT) if u is None else th("TC", u, NT * m)
-                act(o, ind(cw, part("OFF", m, u)), F.Identity, None, co(CW + m))
+                act(o, ind(cw, part("OFF", m, u)), F.Identity, None, co(CW + sc + m))
             tt(part("CN", m), part("KI", m), part("PL", m), A.subtract)
-            at("cwrap", m)
             mm(p48(6, 4), b("nW", 128 * m, 128 * m + 128), part("CN", m), m == 0, False)
             wrap(p48(6, 4), "Wb", "TC", NT * m, False, m == 2)
 
@@ -450,145 +495,180 @@ def rank_program(g, core, T, topo):
             ops.append({"q": None, "f": None, "r": [], "w": b(L)[1], "dma": True, "sem": "arr%d" % t, "pr": now[0],
                         "inc": len(topo.engines(prv, core)), "own": True, "c": 0.0, "lat": 0.0})
         for m in range(4):
-            for u in range(3):
-                at(None, m + 0.1 * u)
+            for n, u in enumerate(US):
+                at("mask%d" % m)
                 if not m:
                     act(th("LQ", u), th(L, u), F.Square)
-                o = p(5 + 2 * ((m + u) % 2) if m else MB[u], 0, TT)
+                o = p(5 + 2 * ((m + n) % 2) if m else MB[u], 0, TT)
                 j = 128 * (4 * t + m)
                 mm(o, b("Sb", j, j + 128), th(L, u), True, False)
                 mm(o, b("Sq", j, j + 128), th("LQ", u), False, True)
                 act(th("M%d" % m, u) if m else o, o, F.Relu, co(B1))
                 if m == 3:
+                    at("nm")
                     act(th("NM", u), o, F.Sign, co(S2), -1.0)
-        at("ok")
-        if t:
-            dma("s", (T.XC[16 * t:128, ext:ext + NT], b("XC", ext, ext + NT)[1]), (T[L][0:128 - 16 * t, :], b(L)[1]))
-            dma("s", (T.XC[0:16 * t, ext:ext + NT], rows("XCc")), (T[L][128 - 16 * t:128, :], b(L)[1]))
-        for u in range(3):
-            at(None, 0.1 * u)
+        for n, u in enumerate(US):
             if t:
                 write5(u)
+            at("gather0")
             tt(th("GA", u), th("K", u), p(MB[u], 0, TT), A.mult)
             step(0, u)
         if not t:
-            at(None, 1.0)
+            at("regs")
             cp(b("cb"), b("cn"))
             dma("s", (T.C0[15:128:16, :], b("C0")[1]), b("cb"))
             dma("s", (T.XC[15:128:16, 0:D], rows("XCb")), b("cb"))
             for k in range(8):
                 dma("s", (T.XC[16 * k:16 * k + 14, 0:D], rows("XC%d" % k)), (T.xreg[16 * k:16 * k + 14, :], []))
             mm(p(5, 256, 512), b("Ib", 0, 128), b("x14"), True, False)
-            mm(p(5, 256, 512), b("I16"), b("x15"), False, True)
+            mm(p(5, 256, 512), b("I16", 32, 160), b("x15"), False, True)
             act(b("pk"), p(5, 256, 512), F.Copy)
             dma("s", (T.XC[14:128:16, 0:D], rows("XCa")), b("pk"))
             wide(3, b("R"), L)
-            act(b("XC", ext, ext + NT), p(3, 0, NT), F.Copy)
+            act(b("XC", EXT, EXT + NT), p(3, 0, NT), F.Identity, None, 0.0625)
         counts(0)
         for m in (1, 2, 3):
-            for u in range(3):
-                at(None, m + 0.1 * u)
+            for n, u in enumerate(US):
+                at("gather")
                 tt(th(gbuf(m), u), ind(b("K", 0, D), part("OFF", m - 1, u)), th("M%d" % m, u), A.mult)
                 step(m, u)
-                if m == 3:
-                    at("pb", 0.1 * u)
-                    mm(p(3, TT * u, TT * u + TT), b("BOf"), th("GB", u))
             if m < 3:
                 counts(m)
-        for u in range(3):
-            at("own", 0.1 * u)
-            tt(part("OW", 0, u), p48(6, 4, TW * u, TW * u + TW), b("PK", 64 * (9 + u) + 3, 64 * (10 + u), 4), A.add)
-            act(nd_("OR", u, al), ind(part("OW", 0, u), b("OC")), F.Identity, co(NU))
-            at("last", 0.1 * u)
-            act(th("T1", u), ind(cw, part("OFF", 3, u)), F.Identity, rm(15), rm(15))
-            at("ka", -0.1 * u)
+        for n, u in enumerate(US):
+            at("kb%d" % n)
+            o = p(7 - 2 * (n % 2), TT, 512)
+            mm(o, b("nBI"), th("NM", u), True, False)
+            mm(o, b("BOf"), th("GA", u), False, True)
+            if n < KBS:
+                act(th("KB", u), o, F.Relu)
+            else:
+                ts(th("KB", u), o, 0.0, A.max)
+        for n, u in enumerate(US):
+            at("last%d" % n)
+            act(th("T1", u), ind(cw, part("OFF", 3, u)), F.Identity, rm(15), co(CW + sc + 3))
+            at("src")
+            mm(p(u, 0, TT), b("I16", 32 - 16 * t, 160 - 16 * t) if t else b("R"), th(L, u), True, False)
+            mm(p(u, 0, TT), b("I16", 32, 160), th("T1", u), False, True)
+            act(th("XF", u, EXT), p(u, 0, TT), F.Copy)
+            at("ka%d" % n)
             tt(th("KA", u), ind(b("K", 0, D), part("OFF", 3, u)), th("NM", u), A.mult)
-        pl = part("PL", 3)
+        for h in (1, 0):
+            c0, c1 = HC * h, HC * h + HC
+            at("own%d" % h)
+            tt(b("OW", c0, c1), p48(6, 4, c0, c1), b("P3", 16 * c0 + 15, 16 * c1, 16), A.add)
+            act(nd_("OR", h, al), ind(b("OW", c0, c1), b("OC")), F.Identity, co(NU))
+        pl, ok = part("PL", 3), nd_("OK", 1, s_(1, 2 * NC, 2))
         at("ok")
         tt(sm(ZB), b("OW"), pl, A.subtract)
-        tt(sm(Q1), pl, part("zi", t), A.subtract)
         mm(p48(5), b("nD"), b("ones", 0, NC), True, False)
         mm(p48(5), b("IU"), b("ones", 0, NC), False, False)
         wrap(p48(5), "Wd", "T1", 0, False, True)
-        ok = nd_("OK", 1, al)
         tt(ok, p48(5), sm(ZB), A.is_equal)
-        tt(sm(ZT), sm(Q1), ok, A.mult)
-        tt(sm(ZT2), sm(ZT), part("zi", t), A.add)
-        cp(b("ZO"), sm(ZT2))
-        xc = b("XC", 0, ext + NT)
-        xc = (xc[0], xc[1] + [rows("XC" + k)[0] for k in "abc01234567"])
-        act(b(ZN), ind(xc, b("ZO")), F.Identity, None, co(N15))
+        at("q")
+        tt(sm(Q0), pl, b("dum"), A.subtract)
+        tt(sm(Q), sm(Q0), ok, A.mult)
+        for h in (1, 0):
+            c0, c1 = HC * h, HC * h + HC
+
+            def hm(k, a=0, st=1, c0=c0, c1=c1):
+                return b("S", NC * k + c0 + a, NC * k + c1, st)
+
+            at("eq%d" % h)
+            o = b("PD", 128 * h, 128 * h + 96)
+            for d in (3, 2, 1, 0):
+                e0 = NB * d + 6 * h
+                for a in range(d, 4):
+                    tt(nd_("EQ", s_(e0, e0 + 6), a, al), nd_("P", s_(24 + 6 * h, 30 + 6 * h), s_(16 * a, 16 * a + 16)),
+                       nd_("OR", h, s_(96 * (a - d), 96 * (a - d) + 96)), A.is_equal)
+                for q in range(4):
+                    mm(o, b("Wk", 3 - q, 131 - q) if d else b("Wt", 128 * q, 128 * q + 128),
+                       nd_("EQ", s_(e0, e0 + 6), al, s_(q, 16, 4)), d == 3 and q == 0, d == 0 and q == 3)
+            dups = len(ops) - 1
+            at("so%d" % h)
+            scan(b("DS", 96 * h, 96 * h + 96), b("SEL"), o, A.add, A.max)
+            tt(hm(TO), b("DS", 96 * h + 3, 96 * h + 96, 4), hm(Q), A.add)
+            for a in range(4):
+                ts(b("SO", c0 + a, c1, 4), hm(TO, a, 4), co(UP), A.min, co(DE + 4 + a), A.add)
+        at("z")
+        tt(b("ZI", 0, 2 * NC, 2), part("PL", 3), b("ZI", 1, 2 * NC, 2), A.subtract)
+        scan(b("ZS"), nd_("OK", 1, al), b("ZI"), A.mult, A.add)
+        cp(b("ZO"), b("ZS", 1, 2 * NC, 2))
+        xc = b("XF") if t else (b("XC")[0], b("XC")[1] + came)
+        act(b(ZN), ind(xc, b("ZO")), F.Identity, None, co(N16 if t else N15))
+        if not t:
+            sent0 = len(ops) - 1
+            at("conv")
+            for k in range(16):
+                a, e = 256 * k, 256 * k + 256 if k < 15 else EXT
+                src = (b("XC", a, e)[0], b("XC", a, e)[1] + came)
+                if k < CONV:
+                    act(b("XF", a, e), src, F.Silu, None, 16.0)
+                    ops[-1]["c"] += 0.0 if k else 1.3
+                else:
+                    ts(b("XF", a, e), src, 16.0, A.mult)
+                ops[-1]["after"] = sent0
         if t < 2:
             rid, pid, _se = topo.addr(nxt)
             ops.append({"q": "g", "r": b(ZN)[1], "w": [], "dma": True, "sem": "snt%d" % (t + 1), "own": True, "pr": now[0],
-                        "inc": len(topo.engines(core, nxt)), "c": 1.0, "lat": 3.0,
+                        "inc": len(topo.engines(core, nxt)), "c": 1.0, "lat": RLAT,
                         "f": lambda t=t, rid=rid, pid=pid: g.remote_dma(
                             T["L%d" % (t + 1)][:], T["ZN%d" % t][:], T.sem["arr%d" % (t + 1)], T.sem["snt%d" % (t + 1)],
                             pid, rid, topo.mask(core, nxt))})
-        at("eq")
-        mm(nd_("PD", s_(0, 3), al, s_(0, 4)), b("Z0"), b("ones", 0, NC), True, False)
-        for d in (3, 2, 1, 0):
-            for a in range(d, 4):
-                tt(nd_("EQ", s_(NB * d, NB * d + NB), a, al), nd_("P", s_(24, 24 + NB), s_(16 * a, 16 * a + 16)),
-                   nd_("OR", al, s_(64 * (a - d), 64 * (a - d) + 64)), A.is_equal)
-            for r in range(16):
-                mm(nd_("PD", s_(0, 3), al, s_(d, 4)), b("Wk", 15 - r, 143 - r) if d else b("Wt", 128 * r, 128 * r + 128),
-                   nd_("EQ", s_(NB * d, NB * d + NB), s_(d, 4), r), False, d == 0 and r == 15)
-        for u in (2, 1, 0):
-            at("kb" if u == 2 else "five", -0.1 * u)
-            o = p(5 if u == 1 else 6, 0, TT)
-            mm(o, b("nBI"), th("NM", u), True, False)
-            mm(o, b("BOf"), th("GA", u), False, True)
-            act(th("KB", u), o, F.Relu)
-        at("so")
-        tt(sm(Q0), pl, b("dum"), A.subtract)
-        tt(sm(Q), sm(Q0), ok, A.mult)
-        tt(sm(TO), nd_("PD", s_(0, 3), al, s_(0, 4)), sm(Q), A.add)
-        for a in range(4):
-            ts(b("SO", a, NC, 4), sm(TO, a, 4), 0.0, A.min, co(DE + a), A.add)
         at("five")
-        ts(nd_("OK", 0, al), ok, -1.0, A.mult)
-        for u in range(3):
-            mm(p(u, 0, TT), b("BI"), b("ones"), True, False)
+        ts(nd_("OK", 0, al), nd_("OK", 1, al), -1.0 if t < 2 else -1.0 / BIG, A.mult)
+        for u in US:
+            mm(p(u, 0, TT), b("BI") if t < 2 else b("Ib", 0, 128), b("ones"), True, False)
+            ops[-1]["after"] = dups
             mm(p(u, TT, 512), b("CB"), b("ones"), False, False)
             mm(p(u, TT, 512), b("Wf", 15 - t, 143 - t), th("GB", u), False, False)
             for r in range(16):
                 mm(nd_("P", s_(8 * u, 8 * u + 8), s_(r, 64, 16)), b("U", 144 * r + 15 - t, 144 * r + 143 - t),
-                   nd_("OK", al, s_(TW * u, TW * u + TW)), False, r == 15)
+                   nd_("OK", al, s_(2 * TW * u + 1, 2 * TW * (u + 1), 2)), False, r == 15)
+            if t == 2:
+                ts(th("GA", u), p(u, TT, 512), 0.0, A.max)
+                mm(p(6, 0, 256), b("If"), th("GA", u), u == US[0], False)
         if t == 2:
-            act(b("hz"), b(ZN), F.Identity, 3064.5)
+            at("yz")
+            for u in range(3):
+                ts(th("hz", u), th(ZN, u), 3064.5, A.add)
             wide(3, b("I15"), ZN, True, False)
             wide(3, b("Bz"), "hz", False, True)
-            act(b("YZ"), p(3, 0, NT), F.Identity, co(BZ))
+            for k in range(4):
+                ts(b("YZ", 192 * k, 192 * k + 192), p(3, 192 * k, 192 * k + 192), co(BZ), A.add)
             dma("s", (T.yz[:], []), b("YZ"))
         for k in range(NB - 1, -1, -1):
             so = b("SO", 4 * k, 4 * k + 4)
             at("sk")
             tt(ind(b("K", 0, EXT), so), b("KA", 64 * k, 64 * k + 64), b("KB", 64 * k, 64 * k + 64), A.add)
             at("sx")
-            tt(ind(b("XC", 0, EXT), so), b("XC", ext + 64 * k, ext + 64 * k + 64), b("T1", 64 * k, 64 * k + 64), A.add)
+            act(ind(b("XF", 0, EXT), so), b("XF", EXT + 64 * k, EXT + 64 * k + 64), F.Silu)
 
-    now[0] = 300.0
-    dma("s", b("r14"), (T.XC[14:128:16, 0:D], b("XC", 0, D)[1]))
-    dma("g", (T.yc[:], []), (T.XC[15:128:16, 0:D], b("XC", 0, D)[1]))
-    for k in range(16):
-        mm(p(5, 0, 256), b("I14"), b("XC", 256 * k, 256 * k + 256), k == 0, False)
-    act(p(3, 0, 512), b("K", 768, 1280), F.Copy)
-    act(p(4, 0, 512), b("K", 1280, 1792), F.Copy)
-    act(b("h14"), b("r14"), F.Identity, 3064.5)
+    at("sumk")
+    dma("s", b("f14"), (T.XF[14:128:16, 0:D], b("XF", 0, D)[1]))
+    dma("s", b("f15"), (T.XF[15:128:16, 0:D], b("XF", 0, D)[1]))
     for k in range(11, 16):
-        mm(p(6, 0, 256), b("If"), b("K", 256 * k, 256 * k + 256), k == 11, k == 15)
+        mm(p(6, 0, 256), b("If"), b("K", 256 * k, 256 * k + 256), False, k == 15)
+    at("sumx")
+    for k in range(16):
+        if k % 2 == 0:
+            act(b("XC", 256 * k, 256 * k + 512), b("XF", 256 * k, 256 * k + 512), F.Identity, None, 0.0625)
+        mm(p(5, 0, 256), b("I14"), b("XC", 256 * k, 256 * k + 256), k == 0, False)
+    at("rows")
+    act(b("r14"), b("f14"), F.Identity, None, 0.0625)
+    act(b("h14"), b("f14"), F.Identity, 3064.5, 0.0625)
+    act(b("cb"), b("f15"), F.Identity, None, 0.0625)
     mm(p(5, 0, 256), b("Wb", 1, 129), b("r14"), False, False)
     mm(p(5, 0, 256), b("Bm"), b("h14"), False, True)
+    act(b("f15"), b("cb"), F.Copy)
+    dma("s", (T.yc[:], []), b("f15"))
     act(b("YX"), p(5, 0, 256), F.Identity, co(BX))
     dma("a", (T.yx[:], []), b("YX"))
     for u in range(3):
-        write5(u)
-    tt(p(3, 0, 512), p(3, 0, 512), b("K", 1792, 2304), A.add)
-    tt(p(4, 0, 512), p(4, 0, 512), b("K", 2304, 2816), A.add)
-    tt(p(3, 0, 512), p(3, 0, 512), b("K", 0, 512), A.add)
-    tt(b("YT"), p(4, 0, 256), b("K", 512, 768), A.add)
-    tt(b("YT"), p(4, 256, 512), b("YT"), A.add)
+        tt(p(3, TT * u, TT * u + TT), th("K", u), p(u, 0, TT), A.mult)
+    for k in range(3):
+        tt(p(3, 0, 512), p(3, 0, 512), b("K", 768 + 512 * k, 1280 + 512 * k), A.add)
+        if k:
+            tt(p(4, 0, 256) if k == 1 else b("YT"), p(4, 0, 256), b("K", 2048 + 256 * k, 2304 + 256 * k), A.add)
     tt(b("YU"), p(3, 0, 256), b("YT"), A.add)
     tt(b("YU"), p(3, 256, 512), b("YU"), A.add)
     tt(b("YK"), p(6, 0, 256), b("YU"), A.add)

import numpy as np
from concourse.mybir import AluOpType as A, ActivationFunctionType as F

D, NT, NC = 4096, 768, 48
EXT = D + 64
TT, TW, HC, NB = 256, 16, 24, 12
US = (2, 1, 0)
CONV, KBS, CG, QS, QU = 10, 3, D - 2 * NT, "v", "a"
BIG = 2097152.0
WT = (2.0 ** 45, 2.0 ** 33, 2.0 ** 21)
f32, bf, i32, u16 = "float32", "bfloat16", "int32", "uint16"


def _sb(n, dt):
    return ("sbuf", [128, n], dt)


SCRATCH = {
    "K": _sb(EXT, f32), "XC": _sb(EXT + NT, bf), "XF": _sb(EXT + NT, f32), "f14": _sb(256, f32), "f15": _sb(256, f32),
    "L0": _sb(NT, bf), "L1": _sb(NT, bf), "L2": _sb(NT, bf),
    "ZN0": _sb(NT, bf), "ZN1": _sb(NT, bf), "ZN2": _sb(NT, bf),
    "C0": _sb(D, bf), "T1": _sb(NT, bf), "SO": _sb(NC, u16),
    "GA": _sb(NT, f32), "GB": _sb(NT, f32), "KA": _sb(NT, f32), "KB": _sb(NT, f32),
    "M1": _sb(NT, bf), "M2": _sb(NT, bf), "M3": _sb(NT, bf), "NM": _sb(NT, bf),
    "LQ": _sb(NT, bf), "Sq": _sb(12 * 128, bf), "BO2": _sb(160, bf), "nBO": _sb(160, bf), "s2": _sb(128, bf),
    "TC": _sb(3 * NT, bf), "PK": _sb(12 * NC, f32), "P3": _sb(NT, f32), "SL3": _sb(64, f32), "SLa": _sb(16, f32), "SLb": _sb(16, f32),
    "KI": _sb(192, i32), "PL": _sb(192, i32), "OFF": _sb(192, u16), "ZO": _sb(NC, u16),
    "OW": _sb(NC, f32), "OC": _sb(HC, u16), "CN": _sb(144, bf), "DS": _sb(192, f32), "ZI": _sb(2 * NC, f32), "ZS": _sb(2 * NC, f32),
    "OR": ("sbuf", [128, 2, 384], f32), "oc": _sb(HC, i32), "EQ": ("sbuf", [128, 4 * NB, 4, 16], bf), "OK": ("sbuf", [128, 2, 2 * NC], bf),
    "S": _sb(NC * 8, f32), "Wk": _sb(132, bf), "Wt": _sb(4 * 128, bf), "Wf": _sb(144, f32), "Wd": _sb(144, bf),
    "ones": _sb(256, bf), "kr": _sb(16, i32), "kr2": _sb(16, i32), "RM": _sb(16, f32), "GE": _sb(16, f32), "LT": _sb(128, bf),
    "W4": _sb(132, f32), "col": _sb(40, f32), "BO0": _sb(128, bf), "BOb": _sb(128, bf), "BOf": _sb(128, f32),
    "W0": _sb(144, bf), "Wb": _sb(144, bf), "W8": _sb(136, f32), "SEL": _sb(96, f32),
    "Ib": _sb(144, bf), "If": _sb(128, f32), "BI": _sb(128, bf), "nBI": _sb(128, bf), "CB": _sb(128, bf),
    "nW": _sb(3 * 128, bf), "nD": _sb(128, bf), "IU": _sb(128, bf),
    "Sb": _sb(12 * 128, bf), "U": _sb(16 * 144, bf),
    "R": _sb(128, bf), "RB": _sb(16, f32), "I15": _sb(128, bf), "I14": _sb(128, bf), "Bm": _sb(128, bf), "Bz": _sb(128, bf),
    "I16": _sb(160, bf), "tm": _sb(128, bf), "tn": _sb(128, bf), "to": _sb(128, bf), "tp": _sb(128, bf),
    "c16": _sb(NC, f32), "dum": _sb(NC, f32),
    "x14": _sb(256, bf), "x15": _sb(256, bf), "cn": _sb(256, i32), "pk": _sb(256, bf), "cb": _sb(256, bf),
    "r14": _sb(256, bf), "h14": _sb(256, bf), "hz": _sb(NT, bf), "YZ": _sb(NT, bf), "YX": _sb(256, bf),
    "YT": _sb(256, f32), "YU": _sb(256, f32), "YK": _sb(256, f32),
    "P": ("psum", [128, 56, 64], f32), "PD": ("psum", [128, 512], f32),
}
NDMA = 28
SEMAPHORES = ["sv", "sa", "sp", "sg", "arr1", "arr2", "snt1", "snt2"] + ["d%d" % k for k in range(NDMA)]
MASKS, PS = {}, ("P", "PD")


def _mask(name, idx):
    key = (name, repr(idx))
    if key not in MASKS:
        shape = SCRATCH[name][1][1:]
        hit = np.zeros(shape, np.uint8)
        hit[idx] = 1
        flat = hit.reshape(-1)
        if name in PS:
            banks = np.repeat(flat.reshape(-1, 512).max(axis=1), 512)
        else:
            banks = flat
        MASKS[key] = (int.from_bytes(np.packbits(flat).tobytes(), "big"), int.from_bytes(np.packbits(banks).tobytes(), "big"),
                      int(flat.sum()))
    return MASKS[key]


WAKE, SLACK, HOLD, CYC, PCYC, GAT, SCA = 0.22, 0.03, 0.4, 0.83e-3, 0.42e-3, 1.56, 3.8
DLAT, RATE, RLAT = 1.4, 350e3, 2.8
LATER = {'regs.p': -3.0, 'src.p': 0.5, 'mask1.a': 1.0, 'count2.p': -0.5, 'kb0.p': 0.5, 'yz.v': 3.0, 'lower.v': 1.0, 'eq0.v': 5.0, 'const.v': 2.0, 'gather.v': -0.5, 'own0.v': 5.0, 'nm.a': -2.0, 'own1.a': -3.0, 'gather0.v': 1.0, 'step.p': 0.5, 'kb2.p': 5.0, 'kb1.a': -3.0, 'five.p': -0.5, 'five.v': -3.0, 'ka0.v': -1.0, 'src.a': 1.0, 'count2.a': -0.5, 'eq1.v': -0.5}
ORDER = []
HOOK = []


def _deps(ops):
    hist, pred = {}, []
    for n, op in enumerate(ops):
        q, deps = op["q"], {}
        touch = [(x, False) for x in op["r"]] + [(x, True) for x in op["w"]]
        for acc, wr in touch:
            for m, x, w in hist.get(acc[0], []):
                same = ops[m]["q"] == q
                if acc[0] in PS and (not same or q == "p"):
                    if acc[2] & x[2]:
                        deps[m] = not same
                elif (w or wr) and acc[1] & x[1]:
                    deps[m] = True
        for acc, wr in touch:
            lst = hist.setdefault(acc[0], [])
            if wr and acc[0] not in PS:
                lst[:] = [h for h in lst if h[1][1] & ~acc[1]]
            lst.append((n, acc, wr))
        pred.append(deps)
    return pred


def _plan(ops):
    n_ops = len(ops)
    pred, last, sent = [], {}, {}
    for n, deps in enumerate(_deps(ops)):
        op = ops[n]
        q = op["q"]
        deps = {m: (WAKE if w else 0.0) for m, w in deps.items()}
        if q in ("s", "g") and q in last:
            deps.setdefault(last[q], None)
        last[q] = n
        if op["sem"][:3] == "snt":
            sent[op["sem"][3:]] = n
        if q is None:
            deps[sent[op["sem"][3:]]] = 0.0
        if "after" in op:
            deps.setdefault(op["after"], 0.0)
        pred.append(deps)
    succ = [[] for _ in ops]
    for n in range(n_ops):
        for m in pred[n]:
            succ[m].append(n)
    pri = [0.0] * n_ops
    for n in range(n_ops - 1, -1, -1):
        pri[n] = min([pri[k] - (pred[k][n] or 0.0) for k in succ[n]] + [0.0]) - ops[n]["c"] - ops[n]["lat"]
    if HOOK:
        return HOOK[0](ops, pred, succ, pri)
    return _greedy(ops, pred, succ, [pri[n] + LATER.get(ops[n]["pr"], 0.0) for n in range(n_ops)])


def _greedy(ops, pred, succ, pri):
    n_ops = len(ops)
    left = [len(d) for d in pred]
    ready = {}
    at, free, bus, order = [0.0] * n_ops, {}, 0.0, []
    for n in range(n_ops):
        if not left[n]:
            ready.setdefault(ops[n]["q"], []).append(n)
    while len(order) < n_ops:
        best = None
        for q, lst in ready.items():
            if lst:
                t0 = max(free.get(q, 0.0), min(at[k] for k in lst))
                limit, pick = 1e9, None
                for k in sorted(lst, key=lambda k: (pri[k], k)):
                    if max(t0, at[k]) + ops[k]["c"] <= limit + HOLD and at[k] <= t0 + SLACK:
                        pick = k
                        break
                    limit = min(limit, at[k])
                if pick is None:
                    pick = min(lst, key=lambda k: (at[k] if at[k] > t0 + SLACK else 1e9, k))
                    free[q] = at[pick]
                    best = "again"
                    break
                if best is None or max(t0, at[pick]) < best[0]:
                    best = (max(t0, at[pick]), q, pick)
        if best == "again":
            continue
        t0, q, n = best
        ready[q].remove(n)
        done = free[q] = t0 + ops[n]["c"]
        if ops[n]["dma"] and q is not None:
            bus = max(bus, done) + ops[n]["lat"] - DLAT
            done = bus + DLAT
        order.append(n)
        for k in succ[n]:
            lat = pred[k][n]
            at[k] = max(at[k], free[q] if lat is None else done + lat)
            left[k] -= 1
            if not left[k]:
                ready.setdefault(ops[k]["q"], []).append(k)
    return order


def _emit(ops, queues, T):
    known, waits, need = {}, [], set()
    for q in queues:
        known[q] = {}
    for n, deps in enumerate(_deps(ops)):
        op = ops[n]
        mine = []
        if op["q"] is not None:
            kn = known[op["q"]]
            for m in sorted([m for m, w in deps.items() if w], reverse=True):
                key = ops[m]["sem"]
                if kn.get(key, -1) >= m:
                    continue
                mine.append(m)
                need.add(m)
                kn[key] = m
                for k2, v2 in ops[m]["clock"].items():
                    if kn.get(k2, -1) < v2:
                        kn[k2] = v2
            op["clock"] = dict(kn)
        else:
            op["clock"] = {}
        waits.append(mine)
    count, val = {}, {}
    for n, op in enumerate(ops):
        if op["dma"] or n in need:
            count[op["sem"]] = count.get(op["sem"], 0) + op["inc"]
            val[n] = count[op["sem"]]
    for n, op in enumerate(ops):
        if op["q"] is None:
            continue
        eng = queues[op["q"]]
        for m in waits[n]:
            eng.wait_ge(T.sem[ops[m]["sem"]], val[m])
        ins = op["f"]()
        if n in val and not op["own"]:
            ins.then_inc(T.sem[op["sem"]], op["inc"])
    for s in sorted(count):
        queues["g"].wait_ge(T.sem[s], count[s])


def rank_program(g, core, T, topo):
    rank = T.rank_of(core)
    if rank is None:
        return
    n_ranks = len(T.cores)
    nxt, prv = T.cores[(rank + 1) % n_ranks], T.cores[(rank - 1) % n_ranks]
    queues = {"g": g, "v": g.vector, "a": g.scalar, "p": g.tensor, "s": g.sync}
    semof = {"g": "sg", "v": "sv", "a": "sa", "p": "sp"}
    ops, nd, now = [], [0], ["load"]

    def at(name):
        now[0] = name + "."

    s_, al = slice, slice(None)

    def nd_(name, *idx):
        return (T[name][(al,) + idx], [(name,) + _mask(name, idx)])

    def b(name, a=0, e=None, st=1):
        return nd_(name, s_(a, SCRATCH[name][1][1] if e is None else e, st if st > 1 else None))

    def p(bank, a, e):
        if bank == 7:
            return b("PD", a, e)
        return nd_("P", s_(8 * bank + a // 64, 8 * bank + e // 64), al)

    def p48(bank, k=0, a=0, e=NC):
        return nd_("P", 8 * bank + k, s_(a, e))

    def th(name, u, o=0):
        return b(name, o + TT * u, o + TT * u + TT)

    def rows(name):
        return [(name, 1, 1, D)]

    def ind(win, off):
        return (win[0].indirect(off[0]), win[1], off[1])

    def cols(x):
        return x[1][0][3]

    def rec(q, f, outs, ins, both=False):
        r, w = [], []
        for x in ins:
            if isinstance(x, tuple):
                r += x[1]
                if len(x) == 3:
                    r += x[2]
        for x in outs:
            w += x[1]
            if len(x) == 3:
                r += x[2]
        o, tens = outs[0], [x for x in ins if isinstance(x, tuple)]
        two = [SCRATCH[x[1][0][0]][2] in (bf, u16) for x in [o] + tens[:1]]
        k = 0
        if q == "p":
            c = max(64, cols(tens[1])) * PCYC * (1 if SCRATCH[tens[1][1][0][0]][2] != f32 else 4)
        elif q == "g":
            c = 0.17 + 2 * cols(o) * CYC
        elif len(o) == 3:
            c, k = 0.06 + cols(tens[0]) * SCA * CYC, 1
        elif tens and len(tens[0]) == 3:
            c, k = 0.06 + cols(o) * GAT * CYC, 2
        elif both:
            c = max(64, cols(o) * (1 if tens[0][1][0][0] in PS or tens[1][1][0][0] in PS else 2)) * CYC
        else:
            c = max(64, cols(o) * (0.5 if q == "v" and all(two) else 1)) * CYC
        ops.append({"q": q, "f": f, "r": r, "w": w, "dma": False, "sem": semof[q], "inc": 1, "own": False, "c": c, "lat": 0.0,
                    "pr": now[0] + q, "k": k})

    def v_(x):
        return x[0] if isinstance(x, tuple) else x

    def dma(q, out, in_):
        s = "d%d" % nd[0]
        nd[0] += 1
        ops.append({"q": q, "f": lambda: queues[q].dma_start(out[0], in_[0]), "r": in_[1], "w": out[1], "dma": True,
                    "sem": s, "inc": 16, "own": False, "c": 1.5 if q == "g" else 0.1, "pr": now[0],
                    "lat": DLAT + (cols(out) * 512 if out[1] and out[1][0][0] == "K" else 120000) / RATE})

    def ts(out, in0, s1, op0, s2=None, op1=None):
        if op1 is None:
            rec("v", lambda: g.vector.tensor_scalar(out[0], in0[0], v_(s1), None, op0), [out], [in0, s1])
        else:
            rec("v", lambda: g.vector.tensor_scalar(out[0], in0[0], v_(s1), v_(s2), op0, op1), [out], [in0, s1, s2])

    def tt(out, in0, in1, op):
        rec("v", lambda: g.vector.tensor_tensor(out[0], in0[0], in1[0], op), [out], [in0, in1], True)

    def scan(out, d0, d1, op0, op1):
        rec("v", lambda: g.vector.tensor_tensor_scan(out[0], d0[0], d1[0], 0.0, op0, op1), [out], [d0, d1])

    def cp(out, in_):
        rec("v", lambda: g.vector.tensor_copy(out[0], in_[0]), [out], [in_])

    def ms(out, c):
        rec("v", lambda: g.vector.memset(out[0], c), [out], [])

    def act(out, in_, func, bias=None, scale=None):
        kw = {}
        if bias is not None:
            kw["bias"] = v_(bias)
        if scale is not None:
            kw["scale"] = v_(scale)
        rec("a", lambda: g.scalar.activation(out[0], in_[0], func, **kw), [out], [in_, bias, scale])

    def mm(out, lhsT, rhs, start=True, stop=True):
        rec("p", lambda: g.tensor.matmul(out[0], lhsT[0], rhs[0], start, stop), [out], [lhsT, rhs])

    def sel(out, in_, pattern, cmp, base, cm):
        rec("g", lambda: g.affine_select(out[0], in_[0], pattern, cmp, 0.0, base, cm), [out], [in_])

    def wrap(out, mat, src, a, start, stop):
        for r in range(16):
            mm(out, b(mat, 15 - r, 143 - r), b(src, a + r, a + NT, 16), start and r == 0, stop and r == 15)

    def wide(bank, mat, src, start=True, stop=True):
        mm(p(bank, 0, 512), mat, b(src, 0, 512), start, stop)
        mm(p(bank, 512, NT), mat, b(src, 512, NT), start, stop)

    def sm(k, a=0, st=1):
        return b("S", NC * k + a, NC * k + NC, st)

    def rm(r):
        return b("RM", r, r + 1)

    def co(k):
        return b("col", k, k + 1)

    SC, S2, N15, C16, L14, BX, BZ, CT, NU, U3, UP, B1, N16, CW, DE = 0, 1, 2, 3, 4, 5, 6, 7, 8, 9, 13, 20, 21, 22, 30
    ZB, Q0, Q, TO = range(4)
    came = [rows("XC" + k)[0] for k in "ab01234567"]
    MB = (3, 4, 6)

    dma("a", b("L0"), (T.zin[:], []))
    dma("s", b("K", 0, NT), (T.nkey[:, 0:NT], []))
    dma("s", b("cn"), (T.cnt[:], []))
    dma("s", b("K", NT, D), (T.nkey[:, NT:D], []))
    dma("s", b("x14"), (T.xreg[14:128:16, :], []))
    dma("s", b("x15"), (T.xreg[15:128:16, :], []))

    at("const")
    ms(b("ones"), 1.0)
    rec("g", lambda: g.iota(T.kr[:], [[-1, 16]], 16, 1), [b("kr")], [])
    sel(b("BO0"), b("ones", 0, 128), [[-16, 8], [0, 16]], A.is_ge, 0, 1)
    sel(b("BOb"), b("BO0"), [[16, 8], [0, 16]], A.is_ge, 15, -1)
    rec("g", lambda: g.iota(T.s2[:], [[0, 8], [2, 16]], 0, 0, allow_small_or_imprecise_dtypes=True), [b("s2")], [])
    sel(b("W0"), b("ones", 0, 144), [[-16, 9], [256, 16]], A.is_ge, -3840, 1)
    sel(b("Wb"), b("W0"), [[16, 9], [0, 16]], A.is_ge, 15, -1)
    sel(b("Ib"), b("ones", 0, 144), [[-1, 144]], A.is_equal, 0, 1)
    rec("g", lambda: g.iota(T.c16[:], [[16, NC]], 0, 0, allow_small_or_imprecise_dtypes=True), [b("c16")], [])
    rec("g", lambda: g.iota(T.oc[:], [[1, 4], [4, 6]], 0, 0), [b("oc")], [])
    rec("g", lambda: g.iota(T.C0[:, 0:CG], [[0, CG]], 0, 0, allow_small_or_imprecise_dtypes=True), [b("C0", 0, CG)], [])
    for a in range(CG, D, NT):
        act(b("C0", a, a + NT), b("L0"), F.Identity, None, 0.0)
    for d in (1, 2, 3):
        rec("g", lambda d=d: g.iota(T.EQ[:, NB * d:NB * d + NB, 0:d, :], [[0, NB], [0, 16 * d]], 0, 0,
                                    allow_small_or_imprecise_dtypes=True), [nd_("EQ", s_(NB * d, NB * d + NB), s_(0, d), al)], [])
    ts(b("kr2"), b("kr"), 15, A.bitwise_and)
    ts(b("RM"), b("kr2"), 0.0, A.is_equal)
    cp(co(SC), b("kr2", 0, 1))

    def mul(q, out, in_, scal):
        if q == "v":
            ts(out, in_, scal, A.mult)
        else:
            act(out, in_, F.Identity, None, scal)

    tt(b("BO2", 32, 160), b("BOb"), b("s2"), A.mult)
    ts(b("nBO", 32, 160), b("BOb"), -1.0, A.mult)
    cp(b("BO2", 0, 32), b("BO2", 128, 160))
    cp(b("nBO", 0, 32), b("nBO", 128, 160))
    ts(co(S2), co(SC), co(SC), A.mult)
    ts(co(B1), co(S2), -1.0, A.mult, 1.0, A.add)
    for j in range(12):
        for name, src in (("Sb", "BO2"), ("Sq", "nBO")):
            mul("v" if j < 4 else QS, b(name, 128 * j, 128 * j + 128), b(src, 32 - 16 * (j // 4), 160 - 16 * (j // 4)), rm(j))
    ts(b("GE"), b("c16", 0, 16), 0.0625, A.mult, co(SC), A.is_le)
    ms(b("SEL", 0, 96, 4), -8388608.0)
    for u in (1, 2, 3):
        ts(co(UP + u), b("GE", 4 * u, 4 * u + 1), -10485760.0, A.mult)
        ts(co(UP + 3 + u), b("GE", 4 * u - 4, 4 * u - 3), BIG, A.mult, co(UP + u), A.add)
        ts(b("SEL", u, 96, 4), b("ones", 0, HC), co(UP + 3 + u), A.mult)
    ts(co(UP), co(SC), 12.0, A.is_lt, BIG, A.mult)
    ts(co(U3), co(SC), 15.0, A.is_lt, BIG, A.mult)
    ts(b("SLa"), b("GE"), -8388608.0, A.mult)
    ts(b("SLb", 1, 16), b("RM", 0, 15), BIG, A.mult)
    ms(b("SLb", 0, 1), 0.0)
    for k in range(4):
        tt(b("SL3", 16 * k, 16 * k + 16), b("SLa"), b("SLb"), A.add)
    tt(b("W8"), b("Wb", 8, 144), b("Wb", 0, 136), A.add)
    tt(b("W4"), b("W8", 4, 136), b("W8", 0, 132), A.add)
    ts(co(N15), rm(15), -1.0, A.mult, 1.0, A.add)
    ts(co(N16), co(N15), 0.0625, A.mult)
    ts(co(C16), rm(15), 256.0, A.mult)
    ts(b("I15"), b("Ib", 0, 128), co(N15), A.mult)
    ts(b("tm"), b("Ib", 1, 129), co(C16), A.mult)
    ts(b("tp"), b("I15"), 16.0, A.mult)
    tt(b("R"), b("tp"), b("tm"), A.add)
    ts(b("I16", 32, 160), b("Ib", 0, 128), 16.0, A.mult)
    cp(b("I16", 0, 32), b("I16", 128, 160))
    for a in range(4):
        ts(co(DE + a), co(SC), float(D + 16 * a), A.add)
        ts(co(DE + 4 + a), co(DE + a), co(UP), A.subtract)
        ts(b("dum", a, NC, 4), b("ones", 0, NB), co(DE + a), A.mult)
    ms(b("XC", D, EXT), 0.0)
    cp(b("BOf"), b("BOb"))
    cp(b("Wf"), b("Wb"))
    ts(b("BI"), b("Ib", 0, 128), BIG, A.mult)
    ts(b("nBI"), b("Ib", 0, 128), -BIG, A.mult)
    ts(b("to"), b("Ib", 1, 129), float(D), A.mult)
    tt(b("CB"), b("to"), b("nBI"), A.add)
    for m in range(8):
        ts(co(CW + m), rm(15), (WT + (1.0,))[m % 4] * (0.0625 if m > 3 else 1.0), A.mult)
    for m in range(3):
        ts(b("nW", 128 * m, 128 * m + 128), b("Ib", 0, 128), -WT[m] / D, A.mult)
    ts(b("nD"), b("Ib", 0, 128), -float(D), A.mult)
    ts(b("IU"), b("Ib", 0, 128), co(U3), A.mult)
    ts(b("Wd"), b("Wb"), float(D), A.mult)
    ts(co(NU), co(U3), -1.0, A.mult)
    cp(b("OC"), b("oc"))
    ms(nd_("OK", al, al), 0.0)
    ts(b("LT"), b("s2"), 0.5, A.mult, co(SC), A.is_gt)
    ts(b("Wk"), b("W4"), 8192.0, A.mult)
    for q in range(4):
        tt(b("Wt", 128 * q, 128 * q + 128), b("Wk", 3 - q, 131 - q), b("LT"), A.mult)
    ts(b("ZI", 1, 2 * NC, 2), b("c16"), co(SC), A.add, float(EXT), A.add)
    ts(b("RB"), b("RM"), BIG, A.mult)
    for r in range(16):
        mul(QU, b("U", 144 * r, 144 * r + 144), b("Wb"), b("RB", r, r + 1))
    ts(co(L14), co(SC), 14.0, A.is_lt)
    ts(co(CT), rm(15), -192.0, A.mult)
    ts(b("tn"), b("Wb", 0, 128), 0.0625, A.mult)
    cp(b("If"), b("Ib", 0, 128))
    ts(co(BZ), rm(14), 3072.0, A.mult, co(CT), A.add)
    ts(b("I14"), b("Ib", 0, 128), co(L14), A.mult)
    tt(b("Bm"), b("tn"), b("Wb", 1, 129), A.subtract)
    ts(co(BX), co(BZ), 16.0, A.mult)
    ts(b("Bz"), b("Bm"), rm(14), A.mult)

    def part(name, m, u=None):
        if u is None:
            return b(name, NC * m, NC * m + NC)
        return b(name, NC * m + TW * u, NC * m + TW * u + TW)

    def gbuf(m):
        return "GB" if m & 1 else "GA"

    def step(m, u):
        at("step")
        if m < 3:
            for q in range(4):
                mm(p(u, 0, 64), b("W4", 3 - q, 131 - q), b(gbuf(m), TT * u + q, TT * u + TT, 4), q == 0, q == 3)
            c0 = 64 * (3 * m + u)
            scan(b("PK", c0, c0 + 64), b("SEL", 0, 64), p48(u, 0, 0, 64), A.add, A.max)
            ts(part("KI", m, u), b("PK", c0 + 3, c0 + 64, 4), co(UP), A.subtract)
        else:
            mm(p(3, TT * u, TT * u + TT), b("BOf"), th("GB", u))
            for k in range(4 * u, 4 * u + 4):
                scan(b("P3", 64 * k, 64 * k + 64), b("SL3"), p48(3, k, 0, 64), A.add, A.max)
            ts(part("KI", m, u), b("P3", TT * u + 15, TT * u + TT, 16), co(U3), A.subtract)
        ts(part("PL", m, u), part("KI", m, u), D - 1, A.bitwise_and)
        cp(part("OFF", m, u), part("PL", m, u))

    def write5(u):
        at("lower")
        tt(th("K", u), th("K", u), p(u, 0, TT), A.min)
        at("lift")
        tt(th("K", u), th("K", u), p(u, TT, 512), A.max)

    for t in range(3):
        L, ZN = "L%d" % t, "ZN%d" % t
        cw = b("XF", 0, D) if t else b("C0")
        sc = 4 if t else 0

        def counts(m, cw=cw, sc=sc):
            at("count%d" % m)
            for u in (US if m == 2 else (None,)):
                o = b("TC", NT * m, NT * m + NT) if u is None else th("TC", u, NT * m)
                act(o, ind(cw, part("OFF", m, u)), F.Identity, None, co(CW + sc + m))
            tt(part("CN", m), part("KI", m), part("PL", m), A.subtract)
            mm(p48(6, 4), b("nW", 128 * m, 128 * m + 128), part("CN", m), m == 0, False)
            wrap(p48(6, 4), "Wb", "TC", NT * m, False, m == 2)

        at("mask")
        if t:
            ops.append({"q": None, "f": None, "r": [], "w": b(L)[1], "dma": True, "sem": "arr%d" % t, "pr": now[0],
                        "inc": len(topo.engines(prv, core)), "own": True, "c": 0.0, "lat": 0.0})
        for m in range(4):
            for n, u in enumerate(US):
                at("mask%d" % m)
                if not m:
                    act(th("LQ", u), th(L, u), F.Square)
                o = p(5 + 2 * ((m + n) % 2) if m else MB[u], 0, TT)
                j = 128 * (4 * t + m)
                mm(o, b("Sb", j, j + 128), th(L, u), True, False)
                mm(o, b("Sq", j, j + 128), th("LQ", u), False, True)
                act(th("M%d" % m, u) if m else o, o, F.Relu, co(B1))
                if m == 3:
                    at("nm")
                    act(th("NM", u), o, F.Sign, co(S2), -1.0)
        for n, u in enumerate(US):
            if t:
                write5(u)
            at("gather0")
            tt(th("GA", u), th("K", u), p(MB[u], 0, TT), A.mult)
            step(0, u)
        if not t:
            at("regs")
            cp(b("cb"), b("cn"))
            dma("s", (T.C0[15:128:16, :], b("C0")[1]), b("cb"))
            dma("s", (T.XC[15:128:16, 0:D], rows("XCb")), b("cb"))
            for k in range(8):
                dma("s", (T.XC[16 * k:16 * k + 14, 0:D], rows("XC%d" % k)), (T.xreg[16 * k:16 * k + 14, :], []))
            mm(p(5, 256, 512), b("Ib", 0, 128), b("x14"), True, False)
            mm(p(5, 256, 512), b("I16", 32, 160), b("x15"), False, True)
            act(b("pk"), p(5, 256, 512), F.Copy)
            dma("s", (T.XC[14:128:16, 0:D], rows("XCa")), b("pk"))
            wide(3, b("R"), L)
            act(b("XC", EXT, EXT + NT), p(3, 0, NT), F.Identity, None, 0.0625)
        counts(0)
        for m in (1, 2, 3):
            for n, u in enumerate(US):
                at("gather")
                tt(th(gbuf(m), u), ind(b("K", 0, D), part("OFF", m - 1, u)), th("M%d" % m, u), A.mult)
                step(m, u)
            if m < 3:
                counts(m)
        for n, u in enumerate(US):
            at("kb%d" % n)
            o = p(7 - 2 * (n % 2), TT, 512)
            mm(o, b("nBI"), th("NM", u), True, False)
            mm(o, b("BOf"), th("GA", u), False, True)
            if n < KBS:
                act(th("KB", u), o, F.Relu)
            else:
                ts(th("KB", u), o, 0.0, A.max)
        for n, u in enumerate(US):
            at("last%d" % n)
            act(th("T1", u), ind(cw, part("OFF", 3, u)), F.Identity, rm(15), co(CW + sc + 3))
            at("src")
            mm(p(u, 0, TT), b("I16", 32 - 16 * t, 160 - 16 * t) if t else b("R"), th(L, u), True, False)
            mm(p(u, 0, TT), b("I16", 32, 160), th("T1", u), False, True)
            act(th("XF", u, EXT), p(u, 0, TT), F.Copy)
            at("ka%d" % n)
            tt(th("KA", u), ind(b("K", 0, D), part("OFF", 3, u)), th("NM", u), A.mult)
        for h in (1, 0):
            c0, c1 = HC * h, HC * h + HC
            at("own%d" % h)
            tt(b("OW", c0, c1), p48(6, 4, c0, c1), b("P3", 16 * c0 + 15, 16 * c1, 16), A.add)
            act(nd_("OR", h, al), ind(b("OW", c0, c1), b("OC")), F.Identity, co(NU))
        pl, ok = part("PL", 3), nd_("OK", 1, s_(1, 2 * NC, 2))
        at("ok")
        tt(sm(ZB), b("OW"), pl, A.subtract)
        mm(p48(5), b("nD"), b("ones", 0, NC), True, False)
        mm(p48(5), b("IU"), b("ones", 0, NC), False, False)
        wrap(p48(5), "Wd", "T1", 0, False, True)
        tt(ok, p48(5), sm(ZB), A.is_equal)
        at("q")
        tt(sm(Q0), pl, b("dum"), A.subtract)
        tt(sm(Q), sm(Q0), ok, A.mult)
        for h in (1, 0):
            c0, c1 = HC * h, HC * h + HC

            def hm(k, a=0, st=1, c0=c0, c1=c1):
                return b("S", NC * k + c0 + a, NC * k + c1, st)

            at("eq%d" % h)
            o = b("PD", 128 * h, 128 * h + 96)
            for d in (3, 2, 1, 0):
                e0 = NB * d + 6 * h
                for a in range(d, 4):
                    tt(nd_("EQ", s_(e0, e0 + 6), a, al), nd_("P", s_(24 + 6 * h, 30 + 6 * h), s_(16 * a, 16 * a + 16)),
                       nd_("OR", h, s_(96 * (a - d), 96 * (a - d) + 96)), A.is_equal)
                for q in range(4):
                    mm(o, b("Wk", 3 - q, 131 - q) if d else b("Wt", 128 * q, 128 * q + 128),
                       nd_("EQ", s_(e0, e0 + 6), al, s_(q, 16, 4)), d == 3 and q == 0, d == 0 and q == 3)
            dups = len(ops) - 1
            at("so%d" % h)
            scan(b("DS", 96 * h, 96 * h + 96), b("SEL"), o, A.add, A.max)
            tt(hm(TO), b("DS", 96 * h + 3, 96 * h + 96, 4), hm(Q), A.add)
            for a in range(4):
                ts(b("SO", c0 + a, c1, 4), hm(TO, a, 4), co(UP), A.min, co(DE + 4 + a), A.add)
        at("z")
        tt(b("ZI", 0, 2 * NC, 2), part("PL", 3), b("ZI", 1, 2 * NC, 2), A.subtract)
        scan(b("ZS"), nd_("OK", 1, al), b("ZI"), A.mult, A.add)
        cp(b("ZO"), b("ZS", 1, 2 * NC, 2))
        xc = b("XF") if t else (b("XC")[0], b("XC")[1] + came)
        act(b(ZN), ind(xc, b("ZO")), F.Identity, None, co(N16 if t else N15))
        if not t:
            sent0 = len(ops) - 1
            at("conv")
            for k in range(16):
                a, e = 256 * k, 256 * k + 256 if k < 15 else EXT
                src = (b("XC", a, e)[0], b("XC", a, e)[1] + came)
                if k < CONV:
                    act(b("XF", a, e), src, F.Silu, None, 16.0)
                    ops[-1]["c"] += 0.0 if k else 1.3
                else:
                    ts(b("XF", a, e), src, 16.0, A.mult)
                ops[-1]["after"] = sent0
        if t < 2:
            rid, pid, _se = topo.addr(nxt)
            ops.append({"q": "g", "r": b(ZN)[1], "w": [], "dma": True, "sem": "snt%d" % (t + 1), "own": True, "pr": now[0],
                        "inc": len(topo.engines(core, nxt)), "c": 1.0, "lat": RLAT,
                        "f": lambda t=t, rid=rid, pid=pid: g.remote_dma(
                            T["L%d" % (t + 1)][:], T["ZN%d" % t][:], T.sem["arr%d" % (t + 1)], T.sem["snt%d" % (t + 1)],
                            pid, rid, topo.mask(core, nxt))})
        at("five")
        ts(nd_("OK", 0, al), nd_("OK", 1, al), -1.0 if t < 2 else -1.0 / BIG, A.mult)
        for u in US:
            mm(p(u, 0, TT), b("BI") if t < 2 else b("Ib", 0, 128), b("ones"), True, False)
            ops[-1]["after"] = dups
            mm(p(u, TT, 512), b("CB"), b("ones"), False, False)
            mm(p(u, TT, 512), b("Wf", 15 - t, 143 - t), th("GB", u), False, False)
            for r in range(16):
                mm(nd_("P", s_(8 * u, 8 * u + 8), s_(r, 64, 16)), b("U", 144 * r + 15 - t, 144 * r + 143 - t),
                   nd_("OK", al, s_(2 * TW * u + 1, 2 * TW * (u + 1), 2)), False, r == 15)
            if t == 2:
                ts(th("GA", u), p(u, TT, 512), 0.0, A.max)
                mm(p(6, 0, 256), b("If"), th("GA", u), u == US[0], False)
        if t == 2:
            at("yz")
            for u in range(3):
                ts(th("hz", u), th(ZN, u), 3064.5, A.add)
            wide(3, b("I15"), ZN, True, False)
            wide(3, b("Bz"), "hz", False, True)
            for k in range(4):
                ts(b("YZ", 192 * k, 192 * k + 192), p(3, 192 * k, 192 * k + 192), co(BZ), A.add)
            dma("s", (T.yz[:], []), b("YZ"))
        for k in range(NB - 1, -1, -1):
            so = b("SO", 4 * k, 4 * k + 4)
            at("sk")
            tt(ind(b("K", 0, EXT), so), b("KA", 64 * k, 64 * k + 64), b("KB", 64 * k, 64 * k + 64), A.add)
            at("sx")
            act(ind(b("XF", 0, EXT), so), b("XF", EXT + 64 * k, EXT + 64 * k + 64), F.Silu)

    at("sumk")
    dma("s", b("f14"), (T.XF[14:128:16, 0:D], b("XF", 0, D)[1]))
    dma("s", b("f15"), (T.XF[15:128:16, 0:D], b("XF", 0, D)[1]))
    for k in range(11, 16):
        mm(p(6, 0, 256), b("If"), b("K", 256 * k, 256 * k + 256), False, k == 15)
    at("sumx")
    for k in range(16):
        if k % 2 == 0:
            act(b("XC", 256 * k, 256 * k + 512), b("XF", 256 * k, 256 * k + 512), F.Identity, None, 0.0625)
        mm(p(5, 0, 256), b("I14"), b("XC", 256 * k, 256 * k + 256), k == 0, False)
    at("rows")
    act(b("r14"), b("f14"), F.Identity, None, 0.0625)
    act(b("h14"), b("f14"), F.Identity, 3064.5, 0.0625)
    act(b("cb"), b("f15"), F.Identity, None, 0.0625)
    mm(p(5, 0, 256), b("Wb", 1, 129), b("r14"), False, False)
    mm(p(5, 0, 256), b("Bm"), b("h14"), False, True)
    act(b("f15"), b("cb"), F.Copy)
    dma("s", (T.yc[:], []), b("f15"))
    act(b("YX"), p(5, 0, 256), F.Identity, co(BX))
    dma("a", (T.yx[:], []), b("YX"))
    for u in range(3):
        tt(p(3, TT * u, TT * u + TT), th("K", u), p(u, 0, TT), A.mult)
    for k in range(3):
        tt(p(3, 0, 512), p(3, 0, 512), b("K", 768 + 512 * k, 1280 + 512 * k), A.add)
        if k:
            tt(p(4, 0, 256) if k == 1 else b("YT"), p(4, 0, 256), b("K", 2048 + 256 * k, 2304 + 256 * k), A.add)
    tt(b("YU"), p(3, 0, 256), b("YT"), A.add)
    tt(b("YU"), p(3, 256, 512), b("YU"), A.add)
    tt(b("YK"), p(6, 0, 256), b("YU"), A.add)
    dma("s", (T.yk[:], []), b("YK"))

    if not ORDER:
        ORDER.extend(_plan(ops))
    _emit([ops[k] for k in ORDER], queues, T)
